import numpy as np, ml_dtypes
CORES = [13,21,141,149]
N = 4
BF = ml_dtypes.bfloat16
V, HV, LV, K, T, S, EPS, LK = 2048, 1024, 11, 256, 4, 3, 84, 10
def pick(tab, ix):
    return np.take_along_axis(tab, ix[:, :, None, :], 3)
def parts(rng):
    px = np.clip(rng.integers(0, 256, (1, 8, 16, V)) + rng.integers(-48, 49, (N, 8, 16, V)), 0, 255)
    vi = rng.integers(0, V, (N, 8, 16, V))
    few = rng.integers(0, V, (N, 8, 16))
    v = np.where(rng.random((N, 8, K)) < 0.25, np.take_along_axis(few, rng.integers(0, 16, (N, 8, K)), 2), rng.integers(0, V, (N, 8, K)))
    near = np.clip(pick(px, v) + rng.integers(-120, 121, (N, 8, 16, K)), 0, 255)
    z = np.where(rng.random((N, 8, 1, K)) < 0.4, near, rng.integers(0, 256, (N, 8, 16, K)))
    f = rng.integers(0, V, (N, 8, 16, K)); d = rng.integers(0, 4, (N, 8, K))
    return px, vi, z, f, v, d, rng.integers(0, 256, (N, 8, 16)), rng.integers(0, 4096, (N, 8, 16))
def pack(px, vi, z, f, v, d, w, k):
    return {"px": np.ascontiguousarray(px.reshape(N, 128, V)).astype(np.float32).astype(BF), "vw": (vi[..., :HV] + V * vi[..., HV:]).reshape(N, 128, HV).astype(np.int32),
            "z0": z.reshape(N, 128, K).astype(np.float32).astype(BF), "f0": f.reshape(N, 128, K).astype(np.int32), "v0": v.astype(np.int32), "d0": d.astype(np.int32),
            "wt": w.reshape(N, 128, 1).astype(np.int32), "kap": k.reshape(N, 128, 1).astype(np.int32)}
def setup_inputs(rng):
    return pack(*parts(rng))
def setup_inputs_corners(rng):
    px, vi, z, f, v, d, w, k = parts(rng); own = np.arange(V)[None, :]; lane = np.arange(16); i = np.arange(K); one = 0 * i
    for r in range(N):
        for g in range(8):
            m = r + g
            d[r, g] = (one, one + 1, one + 3, 3 * (i & 1))[m & 3]
            v[r, g] = (one + (0, V - 1, HV)[m % 3], rng.permutation(V)[:K], (V - 1) * (i & 1), V - K + i)[(r + (g >> 1)) & 3]
            vi[r, g] = (own + 0 * lane[:, None], V - 1 - own + 0 * lane[:, None], (own + 1 + lane[:, None]) & (V - 1), (V - 1) * rng.integers(0, 2, (16, V)))[g & 3]
            f[r, g] = vi[r, g][:, v[r, g]] if m & 1 else (V - 1) * rng.integers(0, 2, (16, K))
            w[r, g] = (0 * lane, 0 * lane + 255, 255 * (lane == 15), w[r, g])[(m >> 1) & 3]
            k[r, g] = (0 * lane, 0 * lane + 4095, 4095 * (lane == 15), k[r, g])[(r + 3 * g) & 3]
            likes = (i >= 0, i < 0, (i & 1) == 0, (i & 1) == 1, rng.random(K) < 0.5)[(r + 2 * g) % 5]
            x = px[r, g][:, v[r, g]]; z[r, g] = np.where(likes[None, :], x, (x + 128) & 255)
    return pack(px, vi, z, f, v, d, w, k)
def setup_inputs_ends(rng):
    def bits(*shape):
        return rng.integers(0, 2, shape)
    pat = 255 * bits(N, 8, 16, 6); pat[..., 0] = 0; pat[..., 1] = 255; pat[..., 3] = 255 - pat[..., 2]
    px = np.take_along_axis(pat, rng.integers(0, 6, (N, 8, 1, V)), 3)
    px[..., 0] = 0; px[..., V - 1] = 255; px[..., V - 613] = 255
    vi = (V - 1) * bits(N, 8, 16, HV); vi = np.concatenate([vi, vi], axis=3)
    z = 255 * bits(N, 8, 16, K); f = (V - 1) * bits(N, 8, 16, K); v = (V - 1) * bits(N, 8, K); d = 3 * bits(N, 8, K)
    w = 255 * bits(N, 8, 16); w[:, 1::2] = 255; k = 4095 * bits(N, 8, 16); k[..., 15] = 4095
    for h in (0, K - 4):
        z[..., h] = 255; v[..., h] = V - 1
        z[..., h + 1] = 255; v[..., h + 1] = 0; d[..., h + 1] = 3
        z[..., h + 2] = 0; z[:, :, 0, h + 2] = 255; z[:, :, 1, h + 2] = 2; v[..., h + 2] = V - 1
        z[..., h + 3] = 0; v[..., h + 3] = V - 1
    return pack(px, vi, z, f, v, d, w, k)
def setup_inputs_spread(rng):
    px = np.minimum((np.exp2(8 * rng.random((N, 8, 1, V))) * rng.random((N, 8, 16, V))).astype(np.int64), 255)
    z = np.minimum((np.exp2(8 * rng.random((N, 8, 1, K))) * rng.random((N, 8, 16, K))).astype(np.int64), 255)
    vi = np.minimum((V * rng.random((N, 8, 16, V)) ** 3).astype(np.int64), V - 1)
    f = np.minimum((V * rng.random((N, 8, 16, K)) ** 4).astype(np.int64), V - 1)
    v = np.minimum((V * rng.random((N, 8, K)) ** 2).astype(np.int64), V - 1)
    d = np.minimum((4 * rng.random((N, 8, K)) ** 2).astype(np.int64), 3)
    w = np.minimum(np.exp2(8 * rng.random((N, 8, 16))).astype(np.int64), 255); k = np.minimum(np.exp2(12 * rng.random((N, 8, 16))).astype(np.int64), 4095)
    return pack(px, vi, z, f, v, d, w, k)
def setup_inputs_ties(rng):
    px, vi, z, f, v, d, w, k = parts(rng)
    pat = np.broadcast_to(rng.integers(0, 256, (1, 8, 16, 8)), (N, 8, 16, 8))
    px = np.take_along_axis(pat, rng.integers(0, 8, (N, 8, 1, V)), 3)
    v = np.take_along_axis(rng.integers(0, V, (N, 8, 24)), rng.integers(0, 24, (N, 8, K)), 2)
    x = pick(px, v); n = LK - rng.integers(0, 2, (N, 8, 1, K)); o = np.argsort(rng.random((N, 8, 16, K)), axis=2)
    far = EPS + (o >= n).astype(np.int64); z = np.where(x + far <= 255, x + far, x - far)
    vi = np.where(rng.random((N, 8, 16, V)) < 0.2, np.arange(V), vi)
    return pack(px, vi, z, f, v, d, w, k)
def check_inputs(d):
    bad = []
    for a, lo, hi in (("px", 0, 255), ("vw", 0, V * V - 1), ("z0", 0, 255), ("f0", 0, V - 1), ("v0", 0, V - 1), ("d0", 0, 3), ("wt", 0, 255), ("kap", 0, 4095)):
        x = np.asarray(d[a]).astype(np.float64)
        if not (np.min(x) >= lo and np.max(x) <= hi): bad.append("range of " + a)
        if not np.all(x == np.rint(x)): bad.append("whole numbers of " + a)
    return bad
def distances(X, ix, q):
    flat = ix.reshape(N, 8, 16 * K); out = np.zeros((N, 8, 16, K), np.int64)
    for i in range(16):
        out += np.abs(np.take_along_axis(X[:, :, i], flat, 2).reshape(N, 8, 16, K) - q[:, :, i][:, :, None, :])
    return out
def place(view, k):
    return np.take_along_axis(view, k[:, :, None, :], 2)[:, :, 0]
def reference(px, vw, z0, f0, v0, d0, wt, kap):
    X = px.astype(np.int64).reshape(N, 8, 16, V); packed = vw.astype(np.int64).reshape(N, 8, 16, HV)
    vi = np.concatenate([packed & (V - 1), packed >> LV], axis=3)
    z = z0.astype(np.int64).reshape(N, 8, 16, K); f = f0.astype(np.int64).reshape(N, 8, 16, K); v = v0.astype(np.int64); dl = d0.astype(np.int64); A = np.zeros((N, 8, K), np.int64)
    wl = wt.astype(np.int64).reshape(N, 8, 16, 1); kl = kap.astype(np.int64).reshape(N, 8, 16, 1); other = np.arange(K) ^ 1
    for t in range(T):
        x = pick(X, v); e = pick(vi, v)
        like = np.add.reduce((np.abs(x - z) <= EPS).astype(np.int64), axis=2) >= LK + (A & 1); L = like[:, :, None, :]
        u = np.add.reduce(wl * z, axis=2) & (V - 1)
        h = np.where(L, f, (((u[:, :, None, :] * kl) >> 5) + 613 * v[:, :, None, :]) & (V - 1))
        de = distances(X, e, x); dh = distances(X, h, np.where(L, x, z))
        e = np.where(L & (dh < de), h, e)
        for r in range(N):
            for g in range(8):
                j = np.flatnonzero(like[r, g]); users, first = np.unique(v[r, g, j], return_index=True)
                vi[r, g][:, users] = e[r, g][:, j[first]]
        z = np.where(L, (z + x) >> 1, z); A = A + like.astype(np.int64); dl = np.where(like, 0, dl + 1)
        s = np.add.reduce(z, axis=2)
        v = np.where(like, place(e, (s + t) & 15), place(h, np.argmin(dh, axis=2)))
        f = e; second = place(e, (s + t + 8) & 15)
        over = like[:, :, other] & (dl >= 2); O = over[:, :, None, :]
        z = np.where(O, z[..., other], z); f = np.where(O, f[..., other], f); A = np.where(over, A[..., other], A)
        v = np.where(over, second[..., other], v); dl = np.where(over, 0, dl)
        if t < T - 1: z, f, v, A, dl = [np.roll(a, S, axis=0) for a in (z, f, v, A, dl)]
    return {"yw": (vi[..., :HV] + V * vi[..., HV:]).reshape(N, 128, HV).astype(np.float32), "yz": z.reshape(N, 128, K).astype(np.float32), "yf": f.reshape(N, 128, K).astype(np.float32),
            "yv": v.astype(np.float32), "yc": (16 * A + dl).astype(np.float32)}

@@ -1,0 +1,569 @@
+from concourse.mybir import AluOpType, ActivationFunctionType
+A = AluOpType
+F = ActivationFunctionType
+N, HOPS, STEP = 4, 4, 3
+HALVES = {"e": 2, "h": 2}
+PIECES = {"e": 2, "h": 1}
+VSHARE = ()
+RELAY = {1: 0, 2: 1, 3: 0}
+MAGIC = 12582912.0
+BONUS = 4.5
+LEAN = {'Vwv': 16, 'Sad': 63, 'NXz': -4, 'Vm': -4, 'TvF': -8, 'Sind': 4, 'Vso': 56, 'VYZ': 15, 'VLL': -14, 'Tsl': 41, 'NXf': -2, 'VLd': -12, 'Tyc': 69, 'GY': 36, 'Ves': -15, 'VKA': 73, 'VYg': 92,
+        'VOO': -48, 'Vc': 13, 'Tdg': -28, 'VfL': 28, 'SYC': 53, 'STs': 6, 'VLst': 38, 'VhN': 18, 'Tpg': 36, 'VOxz': -2, 'Vhu': 10, 'Vvlm': -12, 'ThF': 27, 'Skod': 9, 'SYV': 37, 'VPN': -8,
+        'Txz': -21, 'TY': -29, 'Tzn': 55, 'Vsel': 14, 'Tm': 45, 'SYF': 59, 'Yoz': 17, 'Ten': -34, 'Szt': 21, 'VOD': 14, 'TeD': 44, 'Yof': 51, 'Twl': -10, 'TnP': -5, 'Yoc': 7, 'Yov': 21,
+        'VvFs': -7, 'VEQA': -15, 'Ve': -1, 'Tq': -14, 'Tav': 12, 'TfF': -9, 'VYA': 38, 'VKIm': 14, 'Tvl': -15, 'Tsco': 22, 'Tes': -2, 'Tk': -4, 'VVT': -22, 'Tws': 21, 'Tyv': -45, 'Vvu': 4,
+        'VNN': 28, 'NXv': 44, 'Vkk': 78, 'TkF': -12, 'VLv': 6, 'SYz': 17, 'SheS': 4, 'The': -31, 'VEQ': 3, 'SaB': 2, 'VYp': 14, 'Tau': -1, 'Thh': 23, 'VYf': 61, 'SwS': 24, 'Vuj': 4, 'Voh': 47,
+        'Vhi': -2, 'VP': 5, 'Sw': 51, 'Tnl': 12, 'Sxb': 1, 'Tll': -26, 'VKIs': 88, 'TTF': 26, 'VYv': -9, 'Td': -6, 'Tdist': 5, 'Veu': 16, 'Sks': 5, 'Suk': 3, 'SGe': 1, 'SGh': 1, 'Vti': -11,
+        'VMe': 5, 'Vuh': 57, 'Sc': 2}
+
+SCRATCH = {}
+SEMAPHORES = ["sV", "sS", "sT", "sG", "ls"]
+B16, H16, F32, I32, U16 = "bfloat16", "float16", "float32", "int32", "uint16"
+POOL = {B16: "pB", H16: "pH", F32: "pF", I32: "pI", U16: "pU"}
+PLACE = {}
+used = {}
+
+
+def buf(name, cols, dtype, where="sbuf"):
+    SCRATCH[name] = (where, [128, cols], dtype)
+    PLACE[name] = (name, 0, cols)
+
+
+def tile(name, cols, dtype):
+    o = used.get(dtype, 0)
+    PLACE[name] = (POOL[dtype], o, cols)
+    used[dtype] = o + -(-cols // 32) * 32
+
+
+def at(name, a=0, b=None, s=1, rows=None):
+    p, o, n = PLACE[name]
+    e = n if b is None else b
+    r = slice(None) if rows is None else slice(0, rows)
+    if s == 1:
+        return lambda T: T[p][r, o + a:o + e]
+    return lambda T: T[p][r, o + a:o + e:s]
+
+
+for _n, _c, _d in (("PX", 2048, B16), ("VT", 2304, I32), ("VW", 1024, I32), ("Z0", 256, B16), ("F0", 256, I32), ("VD0", 512, I32), ("WTi", 1, I32), ("KPi", 1, I32),
+                   ("YZ", 256, F32), ("YF", 256, F32), ("YV", 256, F32), ("YC", 256, F32), ("YW", 1024, F32)):
+    buf(_n, _c, _d)
+for _n, _c, _d in (
+        ("VDh", 512, H16), ("VDF", 512, H16), ("WT32", 1, F32), ("KP32", 1, F32), ("MHALF", 1, F32), ("P845", 1, F32), ("PONE", 1, F32),
+        ("ONES", 128, B16), ("ZERO", 384, B16), ("I", 128, B16), ("SWI", 128, B16), ("SW", 128, B16), ("Bt", 128, B16), ("Bk", 128, B16), ("Bh", 128, B16),
+        ("E8", 128, B16), ("C", 144, B16), ("C16", 144, B16), ("CW", 144, B16), ("R", 2048, B16), ("Qi", 16, I32), ("Q", 16, F32), ("Qa", 16, I32),
+        ("KCi", 1, I32), ("KCa", 1, I32), ("KC", 1, F32), ("KC2", 1, F32), ("IF", 128, F32), ("TRF", 8, F32), ("Z1", 384, B16), ("MTWO", 1, F32), ("PMAG", 1, F32), ("NMAG", 1, F32), ("In", 128, B16), ("I2", 128, B16), ("I05", 128, B16), ("I64", 128, B16),
+        ("I2048n", 128, B16), ("I613", 128, H16), ("Forb", 128, B16), ("BROW", 128, B16), ("KCT", 256, B16), ("PEN", 256, B16), ("RH", 64, B16),
+        ("KQ", 128, B16), ("KH", 128, B16), ("K16", 8, B16), ("K1", 8, B16), ("Kh", 8, B16), ("G24", 24, B16), ("TRi", 8, I32), ("TR", 8, H16)):
+    tile(_n, _c, _d)
+for _k in "01":
+    for _n, _c, _d in (
+            ("vu", 8, U16), ("xb", 128, B16), ("ad", 128, B16), ("ind", 128, B16), ("LON", 512, H16), ("vFs", 128, H16), ("Lst", 24, H16), ("ui", 16, I32), ("uj", 16, I32),
+            ("uh", 16, H16), ("es", 128, H16), ("OD", 128, H16), ("Lv", 8, H16), ("vlm", 8, F32), ("aB", 8, B16), ("zt", 128, F32), ("fL", 128, H16), ("hN", 128, H16), ("uk", 128, F32), ("ti", 128, I32), ("hi", 128, I32), ("hu", 128, U16),
+            ("Ld0", 128, B16), ("Oxz", 128, H16), ("e", 128, H16), ("eu", 128, U16), ("Ge", 2048, B16), ("Gh", 2048, B16), ("Me", 2048, B16),
+            ("Mh", 2048, B16), ("heS", 128, F32), ("PN", 128, H16), ("P1", 128, H16), ("T1s", 128, B16), ("kod", 64, F32), ("m1", 64, F32), ("m2", 32, F32), ("m3", 16, F32),
+            ("KI", 16, I32), ("KA", 16, I32), ("kk", 16, B16), ("k8s", 128, B16), ("oh", 128, H16), ("sel", 128, H16), ("EQ", 640, B16), ("EQA", 1024, B16),
+            ("wS", 128, B16), ("w", 8, B16), ("wv", 8, F32), ("so", 8, U16), ("c16", 8, B16)):
+        tile(_n + _k, _c, _d)
+    for _t in range(HOPS + 1):
+        for _x in ("X", "Y"):
+            if (_t < HOPS) if _x == "X" else (_t > 0):
+                buf("%s1_%d" % (_x, _t) + _k, 144, B16)
+                buf("%s2_%d" % (_x, _t) + _k, 24, H16)
+                buf("%s3_%d" % (_x, _t) + _k, 128, H16)
+    for _j in range(4):
+        buf("p" + _k + str(_j), 512, F32, "psum")
+for _dt in used:
+    SCRATCH[POOL[_dt]] = ("sbuf", [128, used[_dt]], _dt)
+for _t in range(1, HOPS):
+    for _k in "01":
+        SEMAPHORES += ["x1_%d" % _t + _k, "x2_%d" % _t + _k, "x3_%d" % _t + _k]
+SEMAPHORES += ["d%d" % _i for _i in range(20)]
+CYC = 0.00083 * 1.2
+
+
+def vc(n, f=1.0):
+    return max(64, n * f) * CYC
+
+
+def build():
+    ops = []
+    nd = [0]
+
+    def op(e, r, w, f, cost, banks=(), dma=False, arg=None):
+        o = dict(e=e, r=r.split(), w=w.split(), f=f, c=cost, b=list(banks), sem=None, arg=arg, i=len(ops), tk=-1)
+        if dma:
+            o["sem"] = "d%d" % nd[0]
+            nd[0] += 1
+        ops.append(o)
+        return o
+
+    def load(e, r, w, fo, fi, cost=2.5):
+        op(e, r, w, lambda g, T, q: q((g.sync if e == "Y" else g.scalar).dma_start(fo(T), fi(T))), cost, dma=True)
+
+    def val(x, T):
+        return x if isinstance(x, (int, float)) else x(T)
+
+    def G(r, w, f, cost):
+        op("G", r, w, lambda g, T, q: q(f(g, T)), cost)
+
+    def cp(r, w, o, i, n, banks=(), half=False):
+        op("V", r, w, lambda g, T, q: q(g.vector.tensor_copy(o(T), i(T))), vc(n, 0.5 if half else 1), banks)
+
+    def ts(r, w, o, i, s1, s2, o1, o2, n, banks=(), half=False):
+        def f(g, T, q):
+            if o2 is None:
+                q(g.vector.tensor_scalar(o(T), i(T), val(s1, T), None, o1))
+            else:
+                q(g.vector.tensor_scalar(o(T), i(T), val(s1, T), s2, o1, o2))
+        op("V", r, w, f, vc(n, 0.5 if half else 1), banks)
+
+    def tt(r, w, o, i0, i1, al, n, banks=(), both=False):
+        op("V", r, w, lambda g, T, q: q(g.vector.tensor_tensor(o(T), i0(T), i1(T), al)), vc(n, 2 if both else 1), banks)
+
+    def ac(r, w, o, i, fn, n, banks=(), **kw):
+        op("S", r, w, lambda g, T, q: q(g.scalar.activation(o(T), i(T), fn, **dict((k, val(x, T)) for k, x in kw.items()))), vc(n) + 0.03, banks)
+
+    def TM(r, w, lst, banks):
+        def f(g, T, q):
+            for (o, a, b, s, p) in lst:
+                q(g.tensor.matmul(o(T), a(T), b(T), bool(s), bool(p)))
+        op("T", r, w, f, 0.04 + len(lst) * 72 * 0.00042 * 1.2, banks)
+
+    def Lb(b, name="C"):
+        return at(name, 15 - b, 143 - b)
+
+    def Rb(b, s=1):
+        return at("R", 128 * b, 128 * b + 128, s)
+
+    cI, cIn, cO, G8 = at("I"), at("In"), at("ONES"), at("Bk", 0, 128, 16)
+    load("Y", "", "VDv", at("VD0", 0, 256, 1, 8), lambda T: T.v0[:, :], 2.0)
+    load("S", "", "VDd", at("VD0", 256, 512, 1, 8), lambda T: T.d0[:, :], 2.0)
+    load("Y", "", "PX", at("PX"), lambda T: T.px[:, :], 4.5)
+    load("S", "", "Z0", at("Z0"), lambda T: T.z0[:, :], 2.3)
+    load("Y", "", "VW", at("VW"), lambda T: T.vw[:, :], 6.0)
+    load("S", "", "F0", at("F0"), lambda T: T.f0[:, :], 2.8)
+    load("S", "", "WTi", at("WTi"), lambda T: T.wt[:, :], 2.5)
+    load("S", "", "KPi", at("KPi"), lambda T: T.kap[:, :], 2.8)
+    for nm, v in (("ONES", 1.0), ("ZERO", 0.0), ("C", 0.0), ("P845", 84.5), ("MHALF", -0.5), ("PONE", 1.0), ("MTWO", -2.0), ("PMAG", MAGIC), ("NMAG", -MAGIC), ("Z1", 0.0), ("KQ", -1.0 / 512), ("KH", 1.0 / 256), ("K16", 16.0), ("K1", 1.0 / 128),
+                  ("Kh", -0.5), ("PEN", 0.0), ("RH", 0.0), ("KCT", 0.0)):
+        op("V", "", nm, lambda g, T, q, nm=nm, v=v: q(g.vector.memset(at(nm)(T), v)), vc(PLACE[nm][2], 0.5))
+
+    op("V", "Z1", "Z1", lambda g, T, q: q(g.vector.memset(at("Z1", 0, 128)(T), 1.0)), vc(64))
+
+    def aff(src, dst, pat, cmp, base, cm, rows=None):
+        G(src, dst, lambda g, T: g.affine_select(at(dst, rows=rows)(T), at(src, rows=rows)(T), pat, cmp, 0.0, base, cm), 0.4)
+    aff("ONES", "E8", [[-1, 8], [0, 16]], A.is_equal, 0, 1, 8)
+    aff("ONES", "Bt", [[-16, 8], [0, 16]], A.is_ge, 0, 1)
+    aff("Bt", "Bk", [[16, 8], [0, 16]], A.is_ge, 15, -1)
+    aff("ONES", "I", [[-1, 128]], A.is_equal, 0, 1)
+    G("", "Qi", lambda g, T: g.iota(at("Qi")(T), [[-1, 16]], 16, 1), 0.2)
+    G("", "KCi", lambda g, T: g.iota(at("KCi")(T), [[1, 1]], 0, 1), 0.2)
+    aff("ONES", "SW", [[-2, 64], [1, 2]], A.is_equal, -1, 1)
+    G("", "BROW", lambda g, T: g.iota(at("BROW")(T), [[0, 8], [1, 16]], 0, 0, allow_small_or_imprecise_dtypes=True), 0.4)
+    G("", "TRi", lambda g, T: g.iota(at("TRi")(T), [[32, 8]], 2048, 0), 0.2)
+    cp("Bk C", "C", at("C", 15, 143, 16), G8, 8)
+    ts("C", "C16", at("C16"), at("C"), 1.0 / 16, 0, A.mult, None, 144, half=True)
+    ts("Qi", "Qa", at("Qa"), at("Qi"), 15, 0, A.bitwise_and, None, 16)
+    ts("Qa", "Q", at("Q"), at("Qa"), 0, 0, A.is_equal, None, 16)
+    ts("KCi", "KCa", at("KCa"), at("KCi"), 15, 0, A.bitwise_and, None, 1)
+    cp("KCa", "KC", at("KC"), at("KCa"), 1)
+    ts("KC", "KC2", at("KC2"), at("KC"), 2.0, 0, A.mult, None, 1)
+    for b in range(16):
+        if b % 2:
+            ac("Bk Q", "R", Rb(b), at("Bk"), F.Copy, 128, scale=at("Q", b, b + 1))
+        else:
+            ts("Bk Q", "R", Rb(b), at("Bk"), at("Q", b, b + 1), 0, A.mult, None, 128, half=True)
+    for nm, src, s in (("In", "I", -1.0), ("I2", "I", 2.0), ("I05", "I", 0.5), ("I64", "I", 64.0), ("I2048n", "I", -2048.0), ("I613", "I", 19616.0), ("Bh", "Bk", 0.5)):
+        ts(src, nm, at(nm), at(src), s, 0, A.mult, None, 128, half=True)
+    tt("SW I", "SWI", at("SWI"), at("SW"), cI, A.subtract, 128, both=True)
+    ts("BROW KC", "Forb", at("Forb"), at("BROW"), at("KC"), 4096.0, A.is_le, A.mult, 128, half=True)
+    ts("BROW KCT", "KCT", at("KCT", 128, 256), at("BROW"), 1.0 / 128, 0, A.mult, None, 128, half=True)
+    ts("Bk PEN", "PEN", at("PEN", 0, 128), at("Bk"), -512.0, 0, A.mult, None, 128, half=True)
+    for c0, s in ((0, 2.0), (16, -1.0), (32, -2.0), (40, 32.0), (48, 1.0), (56, -16.0)):
+        ts("Bk RH", "RH", at("RH", c0, c0 + 8), G8, s, 0, A.mult, None, 8)
+    for c0, s in ((0, 1.0 / 16), (8, -1.0 / 16), (16, 0.5)):
+        ts("Bk", "G24", at("G24", c0, c0 + 8), G8, s, 0, A.mult, None, 8)
+    ts("TRi KC2", "TR", at("TR"), at("TRi"), at("KC2"), 0, A.add, None, 8)
+    ts("TRi KC2", "TRF", at("TRF"), at("TRi"), at("KC2"), 0, A.add, None, 8)
+    ac("I", "IF", at("IF"), cI, F.Copy, 128)
+    ts("WTi", "WT32", at("WT32"), at("WTi"), 32.0, 0, A.mult, None, 1)
+    ts("KPi", "KP32", at("KP32"), at("KPi"), 1.0 / 32, 0, A.mult, None, 1)
+    ts("C WT32", "CW", at("CW"), at("C"), at("WT32"), 0, A.mult, None, 144, half=True)
+    cp("VDv VDd", "VDh", at("VDh", rows=8), at("VD0", rows=8), 512)
+    TM("E8 VDh", "vdF", [(at("p00"), at("E8", rows=8), at("VDh", rows=8), 1, 1)], ["p00"])
+    cp("vdF", "VDF", at("VDF"), at("p00"), 512, ["p00"])
+    TM("VDF C16", "vdL", [(at("p01", 0, 32), Lb(b, "C16"), at("VDF", b, 512, 16), b == 0, b == 15) for b in range(16)], ["p01"])
+    for k in (0, 1):
+        x1, x2 = "X1_0%d" % k, "X2_0%d" % k
+        cp("vdL", x2 + "v", at(x2, 0, 8), at("p01", 8 * k, 8 * k + 8), 8, ["p01"])
+        cp("vdL", x1 + "D", at(x1, 136, 144), at("p01", 16 + 8 * k, 24 + 8 * k), 8, ["p01"])
+        ts(x1 + "D", "Dg%d" % k, at(x2, 16, 24), at(x1, 136, 144), 1.0, 64.0, A.is_ge, A.mult, 8)
+        ts("Dg%d" % k, x2 + "g", at(x2, 8, 16), at(x2, 16, 24), 64.0, 0, A.subtract, None, 8)
+        cp("ZERO", x1 + "A", at(x1, 128, 136), at("ZERO", 0, 8), 8)
+        cp("ZERO Dg%d " % k + x2 + "g", x2 + "p", at(x2, 16, 24), at("ZERO", 0, 8), 8)
+        ops[-1]["w"].append("Dg%d" % k)
+        cp("Z0", x1 + "z", at(x1, 0, 128), at("Z0", 128 * k, 128 * k + 128), 128, half=True)
+        cp("F0", x2 + "f", at("X3_0%d" % k), at("F0", 128 * k, 128 * k + 128), 128)
+    ts("VW", "VT", at("VT", 0, 1024), at("VW"), 2047, 0, A.bitwise_and, None, 1024)
+    ts("VW", "VT2", at("VT", 1024, 2048), at("VW"), 11, 0, A.logical_shift_right, None, 1024)
+
+    cp("ZERO", "VT3", at("VT", 2048, 2304), at("ZERO", 0, 256), 256)
+
+    def send(t, k, part, rd, wr):
+        x = "%d_%d%d" % (part, t + 1, k)
+        o = op("G", rd, "", None, 1.2, arg=("Y" + x, "X" + x, "x" + x, part))
+        r = op("N", "", wr, None, 5.0 - (0.5 if part == 2 else 0.0))
+        r["from"] = o["i"]
+
+    def names(t, k):
+        K = str(k)
+        return (K, "X1_%d" % t + K, "X2_%d" % t + K, "Y1_%d" % (t + 1) + K, "Y2_%d" % (t + 1) + K, "p%d0" % k, "p%d1" % k, "p%d2" % k, "p%d3" % k,
+                lambda s: " ".join(n + K for n in s.split()), lambda n, a=0, b=None, s=1: at(n + K, a, b, s))
+
+    def head(t, k):
+        K, x1, x2, y1, y2, b0, b1, b2, b3, u, tl = names(t, k)
+        zX, fX, vX, AX, DX = at(x1, 0, 128), at("X3_%d" % t + K), at(x2, 0, 8), at(x1, 128, 136), at(x1, 136, 144)
+        zk, fk, vk, Ak, Dk = x1 + "z", x2 + "f", x2 + "v", x1 + "A", x1 + "D"
+        tL, tO, tN = tl("LON", 128, 256), tl("LON", 256, 384), tl("LON", 384, 512)
+        cp(vk, u("vu"), tl("vu"), vX, 8)
+        op("S", u("vu") + " PX", u("xb"), lambda g, T, q: q(g.scalar.activation(tl("xb")(T), T.PX[:, :].indirect(tl("vu")(T)), F.Identity)), 0.1 + 128 * 1.56 * CYC)
+        TM(vk + " %sg %sp R Z1 I" % (x2, x2), "vF" + K + " sco" + K, [(at(b1, 128, 512), cI, at("Z1"), 1, 0)] + [
+            (at(b1, 128 + b, 512, 16), Rb(b), at(x2), 0, 0) for b in range(16)], [b1])
+        TM(zk + " " + vk + " CW I613", "au" + K, [(at(b3, 24, 32), Lb(b, "CW"), at(x1, b, 128, 16), b == 0, b == 15) for b in range(16)] + [
+            (at(b3, 32, 40), at("I613"), vX, 1, 1)], [b3])
+        TM(vk + " " + Ak + " " + Dk + " SWI K1 ONES I In TR", "av" + K, [
+            (at(b3, 48, 56), at("SWI"), AX, 1, 0), (at(b3, 48, 56), cO, at("K1"), 0, 1),
+            (at(b3, 56, 64), cI, DX, 1, 0), (at(b3, 56, 64), cO, at("K1"), 0, 1), (at(b3, 112, 120), cI, vX, 1, 0), (at(b3, 112, 120), cO, at("K1"), 0, 1),
+            (at(b3, 120, 128), cI, vX, 1, 0), (at(b3, 120, 128), cIn, at("TR"), 0, 1)], [b3])
+        TM(u("xb") + " " + zk + " I In", "d0" + K, [(at(b0, 0, 128), cI, tl("xb"), 1, 0), (at(b0, 0, 128), cIn, zX, 0, 1)], [b0])
+        ac("d0" + K, u("ad"), tl("ad"), at(b0, 0, 128), F.Abs, 128, [b0])
+        ac(u("ad") + " P845", u("ind"), tl("ind"), tl("ad"), F.Sign, 128, scale=-1.0, bias=at("P845"))
+        TM(u("ind") + " sco" + K + " Bh", "sco" + K, [(at(b1, 256, 384, 2), at("Bh"), tl("ind", 1, 128, 2), 0, 0), (at(b1, 257, 384, 2), at("Bh"), tl("ind", 0, 128, 2), 0, 0),
+                                                      (at(b1, 384, 512), at("Bh"), tl("ind"), 0, 1)], [b1])
+        TM(fk + " I", "fF" + K, [(at(b2, 0, 128), cI, fX, 1, 1)], [b2])
+        TM(u("xb") + " " + zk + " I In", "xz" + K, [(at(b2, 256, 384), cIn, zX, 1, 0), (at(b2, 256, 384), cIn, zX, 0, 0)] + [
+            (at(b2, 256 + r, 384, 2), cI, at(src, 1 - r, 128, 2), 0, r and src == x1) for r in (0, 1) for src in ("xb" + K, x1)], [b2])
+        cp("au" + K, u("ui"), tl("ui"), at(b3, 24, 40), 16, [b3])
+        ts(u("ui"), u("uj"), tl("uj"), tl("ui"), 65535, 0, A.bitwise_and, None, 16)
+        cp(u("uj"), u("uh"), tl("uh"), tl("uj"), 16)
+        TM(u("uh") + " ZERO R I", "hF" + K, [(at(b3, 128, 384), cI, at("ZERO", 0, 256), 1, 0)] + [
+            (at(b3, 128 + b, 384, 16), Rb(b), tl("uh"), 0, b == 15) for b in range(16)], [b3])
+        ac("hF" + K + " KP32", u("uk"), tl("uk"), at(b3, 128, 256), F.Identity, 128, [b3], scale=at("KP32"))
+        tt(u("uk") + " hF" + K, u("ti"), tl("ti"), tl("uk"), at(b3, 256, 384), A.add, 128, [b3])
+        ts(u("ti"), u("hi"), tl("hi"), tl("ti"), 5, 2047, A.logical_shift_right, A.bitwise_and, 128)
+        ts("sco" + K, "LL" + K, tl("LON", 0, 256), at(b1, 256, 512), 1.5, 0, A.is_ge, None, 256, [b1])
+        TM("LL" + K + " I2 I", "m" + K, [(at(b1, 0, 128), at("I2"), tL, 1, 0), (at(b1, 0, 128), cI, tl("LON", 0, 128), 0, 1)], [b1])
+        ts("m" + K, "OO" + K, tO, at(b1, 0, 128), 1.0, 0, A.is_equal, None, 128, [b1])
+        ts("m" + K, "NN" + K, tN, at(b1, 0, 128), 0.5, 0, A.is_lt, None, 128, [b1])
+        cp("vF" + K, u("vFs"), tl("vFs"), at(b1, 128, 256), 128, [b1])
+        tt("LL" + K + " fF" + K, u("fL"), tl("fL"), tL, at(b2, 0, 128), A.mult, 128, [b2])
+        TM("NN" + K + " I", "nP" + K, [(at(b1, 128, 256), cI, tN, 1, 1)], [b1])
+        tt("nP" + K + " " + u("hi"), u("hN"), tl("hN"), tl("hi"), at(b1, 128, 256), A.mult, 128, [b1])
+        hs = [(cI, tl("fL"), 1, 0), (cI, tl("hN"), 0, 1)]
+        TM(u("fL hN") + " I", "hh" + K, [(at(b1, 0, 128), a, b, s, p) for a, b, s, p in hs], [b1])
+        cp("hh" + K, u("hu"), tl("hu"), at(b1, 0, 128), 128, [b1])
+        tt("LL" + K + " d0" + K, u("Ld0"), tl("Ld0"), tL, at(b0, 0, 128), A.mult, 128, [b0])
+        tt("OO" + K + " xz" + K, u("Oxz"), tl("Oxz"), tO, at(b2, 256, 384), A.mult, 128, [b2])
+        TM(zk + " " + u("Ld0") + " I", "q" + K, [(at(b0, 128, 256), cI, zX, 1, 0), (at(b0, 128, 256), cI, tl("Ld0"), 0, 1)], [b0])
+        zr, hf = at(b0, 256, 384), at("I05")
+        TM(zk + " " + u("Ld0 Oxz") + " I I05 KQ ONES", "zn" + K, [(zr, cI, zX, 1, 0), (zr, hf, tl("Ld0"), 0, 0), (zr, hf, tl("Oxz"), 0, 0), (zr, cO, at("KQ"), 0, 1)], [b0])
+        ac("zn" + K + " PMAG", u("zt"), tl("zt"), zr, F.Identity, 128, [b0], bias=at("PMAG"))
+        ac(u("zt") + " NMAG", y1 + "z", at(y1, 0, 128), tl("zt"), F.Identity, 128, bias=at("NMAG"))
+        TM("LL%s OO%s NN%s C16" % (K, K, K), "ll" + K, [(at(b3, 0, 24), Lb(b, "C16"), tl("LON", 128 + b, 512, 16), b == 0, b == 15) for b in range(16)], [b3])
+        lL, lO, lN = tl("Lst", 0, 8), tl("Lst", 8, 16), tl("Lst", 16, 24)
+        cp("ll" + K, u("Lst"), tl("Lst"), at(b3, 0, 24), 24, [b3])
+        op("V", u("vu") + " VT VT2", u("e"), lambda g, T, q: q(g.vector.tensor_copy(tl("e")(T), T.VT[:, 0:2048].indirect(tl("vu")(T)))), 0.05 + 128 * 1.56 * CYC)
+        cp(u("e"), u("eu"), tl("eu"), tl("e"), 128, half=True)
+        TM(u("fL hN e") + " I In", "he" + K, [(at(b1, 0, 128), a, b, s, 0) for a, b, s, p in hs] + [(at(b1, 0, 128), cIn, tl("e"), 0, 1)], [b1])
+        ac("he" + K, u("heS"), tl("heS"), at(b1, 0, 128), F.Copy, 128, [b1])
+        tt("NN" + K + " he" + K, u("PN"), tl("PN"), tN, at(b1, 0, 128), A.mult, 128, [b1])
+        tt("av" + K + " " + u("Lst"), y1 + "A " + y1 + "D", at(y1, 128, 144), tl("Lst", 8, 24), at(b3, 48, 64), A.mult, 16, [b3])
+        TM(u("Lst") + " " + y1 + "A " + Ak + " I", "nl" + K, [(at(b3, 72, 80), cI, AX, 1, 0), (at(b3, 72, 80), cI, lL, 0, 0), (at(b3, 72, 80), cI, at(y1, 128, 136), 0, 1)], [b3])
+        cp("nl" + K, y1 + "A", at(y1, 128, 136), at(b3, 72, 80), 8, [b3])
+        if t < HOPS - 1:
+            send(t, k, 1, " ".join((y1 + "z", y1 + "A", y1 + "D")), " ".join("X1_%d" % (t + 1) + K + s for s in "zAD"))
+            ac("nl" + K + " MTWO", u("aB"), tl("aB"), at(b3, 72, 80), F.Abs, 8, [b3], bias=at("MTWO"))
+            ts(u("aB"), y2 + "p", at(y2, 16, 24), tl("aB"), 1.0, -1.0, A.is_equal, A.mult, 8)
+            ac(y1 + "D", u("c16"), tl("c16"), at(y1, 136, 144), F.Sign, 8)
+            TM(y2 + "p " + u("c16") + " SW I64 ONES Kh", "pg" + K, [(at(b3, 104, 112), at("SW"), at(y2, 16, 24), 1, 0), (at(b3, 104, 112), at("I64"), tl("c16"), 0, 0),
+                                                              (at(b3, 104, 112), cO, at("Kh"), 0, 1)], [b3])
+            cp("pg" + K, y2 + "g", at(y2, 8, 16), at(b3, 104, 112), 8, [b3])
+        else:
+            r8 = at(b3, 128, 256, 1, 8)
+            ts(y1 + "A", u("c16"), tl("c16"), at(y1, 128, 136), 16.0, 0, A.mult, None, 8)
+            TM(u("c16") + " " + y1 + "D R Bk ZERO", "yc" + K, [(r8, G8, at("ZERO", 0, 128), 1, 0)] + [
+                (at(b3, 128 + b, 256, 16, 8), Rb(b, 16), s, 0, b == 15 and j == 1) for b in range(16) for j, s in enumerate((tl("c16"), at(y1, 136, 144)))], [b3])
+            ac("yc" + K, "YC" + K, at("YC", 128 * k, 128 * k + 128, 1, 8), r8, F.Copy, 128, [b3])
+            load("Y", "YC" + K, "oc" + K, lambda T: T.yc[:, 128 * k:128 * k + 128], at("YC", 128 * k, 128 * k + 128, 1, 8))
+        tt("av" + K + " " + u("Lst"), u("Lv"), tl("Lv"), lL, at(b3, 112, 120), A.mult, 8, [b3])
+        cp(u("Lv"), u("vlm"), tl("vlm"), tl("Lv"), 8)
+        TM(u("vFs Lv") + " I Forb In", "dg" + K, [(at(b3, 384, 512), cI, tl("vFs"), 1, 0), (at(b3, 384, 512), cI, at("Forb"), 0, 0)] + [
+            (at(b3, 384 + b, 512, 16), cIn, tl("Lv"), 0, b == 15) for b in range(16)], [b3])
+        ts("dg" + K, "EQ" + K, tl("EQ", 0, 128), at(b3, 384, 512), 0.0, 0, A.is_equal, None, 128, [b3])
+        mm = [(at(b3, 384, 512), cI, tl("EQ", 0, 128), 1, 0)]
+        eqs = ["EQ" + K]
+        o = 128
+        for c in range(7):
+            s0 = 16 * (c + 1)
+            n = 128 - s0
+            eqs.append("EQ%d_" % c + K)
+            ts(u("vFs vlm"), eqs[-1], tl("EQ", o, o + n), tl("vFs", s0, 128), tl("vlm", c, c + 1), 0, A.is_equal, None, n, half=True)
+            mm.append((at(b3, 384 + s0, 512), cI, tl("EQ", o, o + n), 0, c == 6 and not k))
+            o += n
+        for c in range(8 if k else 0):
+            eqs.append("EQA%d_" % c)
+            ts(u("vFs") + " vlm0", eqs[-1], tl("EQA", 128 * c, 128 * c + 128), tl("vFs"), at("vlm0", c, c + 1), 0, A.is_equal, None, 128, half=True)
+            mm.append((at(b3, 384, 512), cI, tl("EQA", 128 * c, 128 * c + 128), 0, c == 7))
+        TM(" ".join(eqs) + " I", "ws" + K, mm, [b3])
+        ac("ws" + K, u("wS"), tl("wS"), at(b3, 384, 512), F.Copy, 128, [b3])
+        TM(u("wS Lst") + " C K16 I2048n ONES", "wl" + K, [(at(b3, 88, 96), cO, at("K16"), 1, 0), (at(b3, 88, 96), at("I2048n"), lL, 0, 0)] + [
+            (at(b3, 88, 96), Lb(b), tl("wS", b, 128, 16), 0, b == 15) for b in range(16)], [b3])
+        ac("wl" + K + " PONE", u("w"), tl("w"), at(b3, 88, 96), F.Relu, 8, [b3], scale=-1.0, bias=at("PONE"))
+        tt(u("w") + " av" + K, u("wv"), tl("wv"), tl("w"), at(b3, 120, 128), A.mult, 8, [b3])
+        TM(u("wv") + " TRF IF", "sl" + K, [(at(b3, 96, 104), at("IF"), at("TRF"), 1, 0), (at(b3, 96, 104), at("IF"), tl("wv"), 0, 1)], [b3])
+        cp("sl" + K, u("so"), tl("so"), at(b3, 96, 104), 8, [b3])
+
+    def tail(t, k):
+        K, x1, x2, y1, y2, b0, b1, b2, b3, u, tl = names(t, k)
+        last = t == HOPS - 1
+        tO, tN = tl("LON", 256, 384), tl("LON", 384, 512)
+        for nm in ("e", "h"):
+            n = 128 // HALVES[nm]
+            for j in range(HALVES[nm]):
+                gk = " ".join("G%s%d%d_" % (nm, j, i) + K for i in range(PIECES[nm]))
+                for i, gi in enumerate(gk.split()):
+                    c0, c1 = n * j + n * i // PIECES[nm], n * j + n * (i + 1) // PIECES[nm]
+                    if (nm, j, i) in VSHARE:
+                        op("V", u(nm + "u") + " PX", gi, lambda g, T, q, nm=nm, c0=c0, c1=c1: q(g.vector.tensor_copy(tl("G" + nm, 16 * c0, 16 * c1)(T),
+                           T.PX[:, :].indirect(tl(nm + "u", c0, c1)(T)))), 0.1 + 16 * (c1 - c0) * 1.56 * CYC)
+                        continue
+                    op("S", u(nm + "u") + " PX", gi, lambda g, T, q, nm=nm, c0=c0, c1=c1: q(g.scalar.activation(tl("G" + nm, 16 * c0, 16 * c1)(T),
+                       T.PX[:, :].indirect(tl(nm + "u", c0, c1)(T)), F.Identity)), 0.1 + 16 * (c1 - c0) * 1.56 * CYC)
+                for kq in range(0, 16, 2):
+                    def f(g, T, q, nm=nm, j=j, n=n, kq=kq):
+                        for i in (kq, kq + 1):
+                            q(g.vector.tensor_tensor(tl("M" + nm, i * 128 + n * j, i * 128 + n * (j + 1))(T), tl("G" + nm, 16 * n * j + i, 16 * n * (j + 1), 16)(T),
+                                                     at(b0, 128 + n * j, 128 + n * (j + 1))(T), A.max))
+                    op("V", gk + " q" + K, "M%s%d_%d_" % (nm, j, kq) + K, f, 2 * vc(n), [b0])
+        dk = "dist" + K
+        TM("NN" + K + " KCT PEN ONES", dk, [(at(b2, 0, 256), cO, at("KCT"), 1, 0), (at(b2, 0, 256), tN, at("PEN"), 0, 0)], [b2])
+        for nm in ("e", "h"):
+            gs = " ".join("G%s%d%d_" % (nm, j, i) + K for j in range(HALVES[nm]) for i in range(PIECES[nm]))
+            for kq in range(0, 16, 4):
+                ms = " ".join("M%s%d_%d_" % (nm, j, kk) + K for j in range(HALVES[nm]) for kk in (kq, kq + 2))
+                l = []
+                for i in range(kq, kq + 4):
+                    ou = at(b2, i, 256 if nm == "h" else 128, 16)
+                    r0, r1 = (at("RH", 48, 64), at("RH", 32, 48)) if nm == "h" else (at("RH", 16, 24), at("RH", 0, 8))
+                    l += [(ou, tl("G" + nm, i, 2048, 16), r0, 0, 0), (ou, tl("M" + nm, 128 * i, 128 * i + 128), r1, 0, nm == "h" and i == 15)]
+                TM(gs + " " + ms + " " + dk + " RH", dk, l, [b2])
+        ac(dk, u("kod"), tl("kod"), at(b2, 129, 256, 2), F.Copy, 64, [b2])
+        ac(dk + " MHALF", u("T1s"), tl("T1s"), at(b2, 0, 128), F.Sign, 128, [b2], bias=at("MHALF"))
+        tt(dk + " " + u("kod"), u("m1"), tl("m1"), tl("kod"), at(b2, 128, 256, 2), A.min, 64, [b2])
+        tt(u("m1"), u("m2"), tl("m2"), tl("m1", 0, 64, 2), tl("m1", 1, 64, 2), A.min, 32, both=True)
+        tt(u("m2"), u("m3"), tl("m3"), tl("m2", 0, 32, 2), tl("m2", 1, 32, 2), A.min, 16, both=True)
+        tt(u("m3"), u("KIm"), tl("KI", 8, 16), tl("m3", 0, 16, 2), tl("m3", 1, 16, 2), A.min, 8)
+        TM(y1 + "z OO" + K + " NN" + K + " Bk G24 K1 ONES", "sm" + K, [
+            (at(b1, 128, 136), at(y1, 0, 128), G8, 1, 0), (at(b1, 128, 136), tO, at("G24", 16, 24), 0, 1),
+            (at(b1, 136, 144), cO, at("K1"), 1, 0), (at(b1, 136, 144), tN, at("G24", 8, 16), 0, 1), (at(b1, 144, 152), tN, at("G24", 0, 8), 1, 1)], [b1])
+        ts("sm" + K, u("KIs"), tl("KI", 0, 8), at(b1, 128, 136), float(t), 0, A.add, None, 8, [b1])
+        ts(u("KIm KIs"), u("KA"), tl("KA"), tl("KI"), 15, 0, A.bitwise_and, None, 16)
+        tt(u("KA") + " sm" + K, u("kk"), tl("kk"), tl("KA"), at(b1, 136, 152), A.mult, 16, [b1])
+        k8 = at(b1, 256, 384, 1, 8)
+        TM(u("kk") + " I", "k8" + K, [(k8, tl("kk", 0, 8), cI, 1, 0), (k8, tl("kk", 8, 16), cI, 0, 1)], [b1])
+        ac("k8" + K, u("k8s"), at("k8s" + K, rows=8), k8, F.Copy, 128, [b1])
+        TM(u("k8s") + " E8", "kF" + K, [(at(b1, 384, 512), at("E8", rows=8), at("k8s" + K, rows=8), 1, 1)], [b1])
+        ts("kF" + K + " KC", u("oh"), tl("oh"), at(b1, 384, 512), at("KC"), 0, A.is_equal, None, 128, [b1])
+        TM(u("T1s") + " I05 KH ONES", "T1F" + K, [(at(b2, 256, 384), tl("T1s"), at("I05"), 1, 0), (at(b2, 256, 384), cO, at("KH"), 0, 1)], [b2])
+        tt(u("heS") + " T1F" + K, u("P1"), tl("P1"), tl("heS"), at(b2, 256, 384), A.mult, 128, [b2])
+        TM(u("e P1") + " I", "es" + K, [(at(b2, 384, 512), cI, tl("e"), 1, 0), (at(b2, 384, 512), cI, tl("P1"), 0, 1)], [b2])
+        cp("es" + K, u("es"), tl("es"), at(b2, 384, 512), 128, [b2])
+        TM(u("es") + " I In", "eD" + K, [(at(b2, 256, 384), cIn, tl("es"), 1, 0), (at(b2, 256, 384, 2), cI, tl("es", 1, 128, 2), 0, 0), (at(b2, 257, 384, 2), cI, tl("es", 0, 128, 2), 0, 1)], [b2])
+        tt("OO" + K + " eD" + K, u("OD"), tl("OD"), tO, at(b2, 256, 384), A.mult, 128, [b2])
+        TM(u("es OD PN") + " I", "Y" + K, [(at(b3, 384, 512), cI, tl("es"), 1, 0), (at(b3, 384, 512), cI, tl("OD"), 0, 0), (at(b3, 384, 512), cI, tl("PN"), 0, 1)], [b3])
+        TM(u("es OD") + " I", "en" + K, [(at(b2, 384, 512), cI, tl("es"), 1, 0), (at(b2, 384, 512), cI, tl("OD"), 0, 1)], [b2])
+        if not last:
+            cp("en" + K, y2 + "f", at("Y3_%d" % (t + 1) + K), at(b2, 384, 512), 128, [b2])
+        tt(u("oh") + " Y" + K, u("sel"), tl("sel"), tl("oh"), at(b3, 384, 512), A.mult, 128, [b3])
+        if not last:
+            TM(u("sel") + " C", "vl" + K, [(at(b3, 80, 88), Lb(b), tl("sel", b, 128, 16), b == 0, b == 15) for b in range(16)], [b3])
+            cp("vl" + K, y2 + "v", at(y2, 0, 8), at(b3, 80, 88), 8, [b3])
+            send(t, k, 2, " ".join(y2 + s for s in "vpg"), " ".join("X2_%d" % (t + 1) + K + s for s in "vpg"))
+            send(t, k, 3, " ".join(y2 + s for s in "fv"), "X2_%d" % (t + 1) + K + "f")
+        else:
+            c0, c1 = 128 * k, 128 * k + 128
+            c = slice(c0, c1)
+            cp(y1 + "z", "YZ" + K, at("YZ", c0, c1), at(y1, 0, 128), 128)
+            load("Y", "YZ" + K, "oz" + K, lambda T: T.yz[:, c], at("YZ", c0, c1))
+            ac("en" + K, "YF" + K, at("YF", c0, c1), at(b2, 384, 512), F.Copy, 128, [b2])
+            load("Y", "YF" + K, "of" + K, lambda T: T.yf[:, c], at("YF", c0, c1))
+            TM(u("sel") + " Bk", "yv" + K, [(at(b1, 128, 256, 1, 8), G8, tl("sel"), 1, 1)], [b1])
+            ac("yv" + K, "YV" + K, at("YV", c0, c1, 1, 8), at(b1, 128, 256, 1, 8), F.Copy, 128, [b1])
+            load("Y", "YV" + K, "ov" + K, lambda T: T.yv[:, c], at("YV", c0, c1, 1, 8))
+        op("V", u("es so") + " VT VT2 VT3", "VT", lambda g, T, q: q(g.vector.tensor_copy(T.VT[:, 0:2304].indirect(tl("so")(T)), tl("es")(T))), 0.05 + 128 * 3.8 * CYC)
+
+    for t in range(HOPS):
+        for fn, k in ((head, 0), (head, 1), (tail, 0), (tail, 1)):
+            i0 = len(ops)
+            fn(t, k)
+            for o in ops[i0:]:
+                o["tk"] = 2 * t + k
+    for j in (0, 1):
+        pj, c0 = "p0%d" % j, 512 * j
+        ts("VT VT2", "yh%d " % j + ("zn0 q0 d00", "yc0 yv0 kF0")[j], at(pj), at("VT", 1024 + c0, 1536 + c0), 2048.0, 0, A.mult, None, 512, [pj])
+        tt("VT VT2 yh%d" % j, "YW%d" % j, at("YW", c0, c0 + 512), at("VT", c0, c0 + 512), at(pj), A.add, 512, [pj])
+        load("Y", "YW%d" % j, "ow%d" % j, lambda T, c0=c0: T.yw[:, c0:c0 + 512], at("YW", c0, c0 + 512))
+    return ops
+
+
+def dag(ops):
+    writer, readers, bank = {}, {}, {}
+    for o in ops:
+        i, p = o["i"], set()
+        if "from" in o:
+            p.add(o["from"])
+        for k in o["r"]:
+            p.update(writer.get(k, []))
+            readers.setdefault(k, []).append(i)
+        for k in o["w"]:
+            if k in ("R", "G24") and not readers.get(k):
+                writer.setdefault(k, []).append(i)
+                continue
+            p.update(writer.get(k, []))
+            p.update(readers.get(k, []))
+            writer[k], readers[k] = [i], []
+        for k in o["b"]:
+            cur = bank.get(k)
+            if cur is None:
+                bank[k] = (o["e"], [i], [])
+            elif cur[0] == o["e"]:
+                cur[1].append(i)
+                p.update(cur[2])
+            else:
+                p.update(cur[1])
+                bank[k] = (o["e"], [i], list(cur[1]))
+        p.discard(i)
+        o["p"] = p
+    return ops
+
+
+def plan():
+    ops = dag(build())
+    succ = [[] for _ in ops]
+    for o in ops:
+        for p in o["p"]:
+            succ[p].append(o["i"])
+    lat = 0.08
+    prio = [0.0] * len(ops)
+    for o in reversed(ops):
+        prio[o["i"]] = o["c"] + lat + max([prio[s] for s in succ[o["i"]]] + [0.0])
+    for o in ops:
+        if o["tk"] >= 0:
+            w = (o["w"] or [o["arg"][0] if o["arg"] else "?"])[0]
+            kind = o["e"] + "".join(ch for ch in w if ch not in "0123456789_")[:5]
+            prio[o["i"]] += LEAN.get(kind, 0.0) - (BONUS if o["tk"] % 2 else 0.0)
+    left = [len(o["p"]) for o in ops]
+    ready = [0.0] * len(ops)
+    free = dict((e, 0.0) for e in "VSTGYN")
+    avail = dict((e, []) for e in "VSTGYN")
+    for o in ops:
+        if not left[o["i"]]:
+            avail[o["e"]].append(o["i"])
+    order = []
+    while len(order) < len(ops):
+        t0, e = min((min(max(free[e], ready[i]) for i in avail[e]), e) for e in avail if avail[e])
+        i = max((j for j in avail[e] if max(free[e], ready[j]) <= t0 + 1e-9), key=lambda j: (prio[j], -j))
+        o = ops[i]
+        avail[e].remove(i)
+        if e != "N":
+            free[e] = t0 + (0.1 if o["sem"] else o["c"])
+        o["start"] = t0
+        order.append(i)
+        for s in succ[i]:
+            ready[s] = max(ready[s], t0 + o["c"] + lat)
+            left[s] -= 1
+            if not left[s]:
+                avail[ops[s]["e"]].append(s)
+    return ops, order
+
+
+PLAN = {}
+
+
+def relays(core, T, topo):
+    dst = T.cores[(T.rank_of(core) + STEP) % N]
+    return [c for c in topo.cores_of(core) if c != core and topo.die(c) == topo.die(core) and topo.may_write(c, dst)][:2], dst
+
+
+def relay_program(g, core, T, topo, which, src, dst):
+    rid, pid = topo.addr(dst, core)
+    sent = 0
+    ops, order = PLAN["p"]
+    for a, x, s, part in [ops[i]["arg"] for i in order if ops[i]["arg"]]:
+        if RELAY[part] == which:
+            g.wait_ge(T.sem[s], len(topo.engines(src, core)))
+            g.remote_dma(T[x][:, :], T[x][:, :], T.sem[s], T.sem.ls, pid, rid, topo.mask(core, dst))
+            sent += len(topo.engines(core, dst))
+    g.wait_ge(T.sem.ls, sent)
+
+
+def rank_program(g, core, T, topo):
+    rank = T.rank_of(core)
+    if "p" not in PLAN:
+        PLAN["p"] = plan()
+    if rank is None:
+        for c in T.cores:
+            rl, dst = relays(c, T, topo)
+            if core in rl:
+                relay_program(g, core, T, topo, rl.index(core), c, dst)
+        return
+    ops, order = PLAN["p"]
+    rl, dst = relays(core, T, topo)
+    rsrc, _d = relays(T.cores[(rank - STEP) % N], T, topo)
+    queue = {"V": g.vector, "S": g.scalar, "T": g.tensor, "G": g, "Y": g.sync}
+    count = {"sV": 0, "sS": 0, "sT": 0, "sG": 0}
+    known = dict((e, {}) for e in queue)
+    done = {}
+    sent = 0
+    for i in order:
+        o = ops[i]
+        e = o["e"]
+        if e == "N":
+            arg = ops[o["from"]]["arg"]
+            done[i] = (arg[2], len(topo.engines(rsrc[RELAY[arg[3]]], core)), {})
+            continue
+        need = {}
+        for p in o["p"]:
+            if p in done and not (e == "T" and ops[p]["e"] == "T"):
+                s, v, kn = done[p]
+                if v > known[e].get(s, 0) and v > need.get(s, (0, 0))[0]:
+                    need[s] = (v, kn)
+        for s in sorted(need):
+            v, kn = need[s]
+            if v <= known[e].get(s, 0):
+                continue
+            queue[e].wait_ge(T.sem[s], v)
+            known[e][s] = v
+            for a in kn:
+                known[e][a] = max(known[e].get(a, 0), kn[a])
+        if o["arg"]:
+            a, b, s, part = o["arg"]
+            r = rl[RELAY[part]]
+            rid, pid = topo.addr(r, core)
+            g.remote_dma(T[b][:, :], T[a][:, :], T.sem[s], T.sem.ls, pid, rid, topo.mask(core, r))
+            sent += len(topo.engines(core, r))
+        elif o["sem"]:
+            o["f"](g, T, lambda x, s=o["sem"]: x.then_inc(T.sem[s], 16))
+            done[i] = (o["sem"], 16, dict(known[e]))
+        else:
+            def q(x, s="s" + e):
+                x.then_inc(T.sem[s], 1)
+                count[s] += 1
+            o["f"](g, T, q)
+            done[i] = ("s" + e, count["s" + e], dict(known[e]))
+    for s in sorted(count):
+        g.wait_ge(T.sem[s], count[s])
+    for o in ops:
+        if o["sem"]:
+            g.wait_ge(T.sem[o["sem"]], 16)
+    g.wait_ge(T.sem.ls, sent)

@@ -2,19 +2,13 @@ from concourse.mybir import AluOpType, ActivationFunctionType
 A = AluOpType
 F = ActivationFunctionType
 N, HOPS, STEP = 4, 4, 3
-HALVES = {"e": 2, "h": 2}
-PIECES = {"e": 2, "h": 1}
-VSHARE = ()
+FIRST = ("h", "e")
+PIECE = 32
 RELAY = {1: 0, 2: 1, 3: 0}
 MAGIC = 12582912.0
-BONUS = 4.5
-LEAN = {'Vwv': 16, 'Sad': 63, 'NXz': -4, 'Vm': -4, 'TvF': -8, 'Sind': 4, 'Vso': 56, 'VYZ': 15, 'VLL': -14, 'Tsl': 41, 'NXf': -2, 'VLd': -12, 'Tyc': 69, 'GY': 36, 'Ves': -15, 'VKA': 73, 'VYg': 92,
-        'VOO': -48, 'Vc': 13, 'Tdg': -28, 'VfL': 28, 'SYC': 53, 'STs': 6, 'VLst': 38, 'VhN': 18, 'Tpg': 36, 'VOxz': -2, 'Vhu': 10, 'Vvlm': -12, 'ThF': 27, 'Skod': 9, 'SYV': 37, 'VPN': -8,
-        'Txz': -21, 'TY': -29, 'Tzn': 55, 'Vsel': 14, 'Tm': 45, 'SYF': 59, 'Yoz': 17, 'Ten': -34, 'Szt': 21, 'VOD': 14, 'TeD': 44, 'Yof': 51, 'Twl': -10, 'TnP': -5, 'Yoc': 7, 'Yov': 21,
-        'VvFs': -7, 'VEQA': -15, 'Ve': -1, 'Tq': -14, 'Tav': 12, 'TfF': -9, 'VYA': 38, 'VKIm': 14, 'Tvl': -15, 'Tsco': 22, 'Tes': -2, 'Tk': -4, 'VVT': -22, 'Tws': 21, 'Tyv': -45, 'Vvu': 4,
-        'VNN': 28, 'NXv': 44, 'Vkk': 78, 'TkF': -12, 'VLv': 6, 'SYz': 17, 'SheS': 4, 'The': -31, 'VEQ': 3, 'SaB': 2, 'VYp': 14, 'Tau': -1, 'Thh': 23, 'VYf': 61, 'SwS': 24, 'Vuj': 4, 'Voh': 47,
-        'Vhi': -2, 'VP': 5, 'Sw': 51, 'Tnl': 12, 'Sxb': 1, 'Tll': -26, 'VKIs': 88, 'TTF': 26, 'VYv': -9, 'Td': -6, 'Tdist': 5, 'Veu': 16, 'Sks': 5, 'Suk': 3, 'SGe': 1, 'SGh': 1, 'Vti': -11,
-        'VMe': 5, 'Vuh': 57, 'Sc': 2}
+BIG = 2.0 ** 25
+BONUS = 4.0
+LEAN = {}
 
 SCRATCH = {}
 SEMAPHORES = ["sV", "sS", "sT", "sG", "ls"]
@@ -37,38 +31,46 @@ def tile(name, cols, dtype):
 
 def at(name, a=0, b=None, s=1, rows=None):
     p, o, n = PLACE[name]
-    e = n if b is None else b
-    r = slice(None) if rows is None else slice(0, rows)
-    if s == 1:
-        return lambda T: T[p][r, o + a:o + e]
-    return lambda T: T[p][r, o + a:o + e:s]
+    r = (0, 128) if rows is None else rows if isinstance(rows, tuple) else (0, rows)
+    return (p, r, o + a, o + (n if b is None else b), s)
 
 
-for _n, _c, _d in (("PX", 2048, B16), ("VT", 2304, I32), ("VW", 1024, I32), ("Z0", 256, B16), ("F0", 256, I32), ("VD0", 512, I32), ("WTi", 1, I32), ("KPi", 1, I32),
-                   ("YZ", 256, F32), ("YF", 256, F32), ("YV", 256, F32), ("YC", 256, F32), ("YW", 1024, F32)):
+def ap(T, x):
+    if not isinstance(x, tuple):
+        return x
+    p, r, a, b, s = x
+    return T[p][r[0]:r[1], a:b] if s == 1 else T[p][r[0]:r[1], a:b:s]
+
+
+def width(x):
+    return len(range(x[2], x[3], x[4]))
+
+
+for _n, _c, _d in (("PX", 2048, B16), ("VT", 2064, I32), ("TH", 2048, F32), ("VW", 1024, I32), ("Z0", 256, B16), ("F0", 256, I32), ("VD0", 512, I32), ("WTi", 1, I32),
+                   ("KPi", 1, I32), ("YZ", 256, F32), ("YF", 256, F32), ("YV", 256, F32), ("YC", 256, F32), ("YW", 1024, F32)):
     buf(_n, _c, _d)
 for _n, _c, _d in (
-        ("VDh", 512, H16), ("VDF", 512, H16), ("WT32", 1, F32), ("KP32", 1, F32), ("MHALF", 1, F32), ("P845", 1, F32), ("PONE", 1, F32),
-        ("ONES", 128, B16), ("ZERO", 384, B16), ("I", 128, B16), ("SWI", 128, B16), ("SW", 128, B16), ("Bt", 128, B16), ("Bk", 128, B16), ("Bh", 128, B16),
-        ("E8", 128, B16), ("C", 144, B16), ("C16", 144, B16), ("CW", 144, B16), ("R", 2048, B16), ("Qi", 16, I32), ("Q", 16, F32), ("Qa", 16, I32),
-        ("KCi", 1, I32), ("KCa", 1, I32), ("KC", 1, F32), ("KC2", 1, F32), ("IF", 128, F32), ("TRF", 8, F32), ("Z1", 384, B16), ("MTWO", 1, F32), ("PMAG", 1, F32), ("NMAG", 1, F32), ("In", 128, B16), ("I2", 128, B16), ("I05", 128, B16), ("I64", 128, B16),
-        ("I2048n", 128, B16), ("I613", 128, H16), ("Forb", 128, B16), ("BROW", 128, B16), ("KCT", 256, B16), ("PEN", 256, B16), ("RH", 64, B16),
-        ("KQ", 128, B16), ("KH", 128, B16), ("K16", 8, B16), ("K1", 8, B16), ("Kh", 8, B16), ("G24", 24, B16), ("TRi", 8, I32), ("TR", 8, H16)):
+        ("VDh", 512, H16), ("WTa", 1, F32), ("WTb", 1, F32), ("KP", 1, F32), ("PMAG", 1, F32), ("NMAG", 1, F32), ("ONES", 144, B16), ("ZERO", 128, B16),
+        ("I", 128, B16), ("SWI", 128, B16), ("SWn", 128, B16), ("SW", 128, B16), ("Bt", 128, B16), ("Bk", 128, B16), ("B25", 128, B16), ("B32", 128, B16), ("SW32", 128, B16), ("Wa", 128, B16), ("Wb", 128, B16),
+        ("E8", 128, B16), ("CT", 144, B16), ("C", 144, B16), ("C16", 144, B16), ("R", 2048, B16), ("Qi", 16, I32), ("Q", 16, F32), ("Qa", 16, I32),
+        ("KCi", 1, I32), ("KCa", 1, I32), ("KC", 1, F32), ("Z1", 384, B16), ("In", 128, B16), ("I2", 128, B16), ("I2n", 128, B16), ("I05", 128, B16), ("I32", 128, B16),
+        ("I16", 128, B16), ("I25", 128, B16), ("I2048n", 128, B16), ("Forb", 128, B16), ("BROW", 128, B16), ("RSTH", 128, B16), ("KCT", 264, B16),
+        ("PEN", 128, B16), ("RH", 64, B16), ("KQ", 128, B16), ("KU", 128, B16), ("K1", 128, B16), ("KS", 40, B16), ("KV", 40, B16), ("GL", 16, B16), ("KT", 32, B16),
+        ("THi", 128, F32), ("THb", 16, F32)):
     tile(_n, _c, _d)
 for _k in "01":
     for _n, _c, _d in (
-            ("vu", 8, U16), ("xb", 128, B16), ("ad", 128, B16), ("ind", 128, B16), ("LON", 512, H16), ("vFs", 128, H16), ("Lst", 24, H16), ("ui", 16, I32), ("uj", 16, I32),
-            ("uh", 16, H16), ("es", 128, H16), ("OD", 128, H16), ("Lv", 8, H16), ("vlm", 8, F32), ("aB", 8, B16), ("zt", 128, F32), ("fL", 128, H16), ("hN", 128, H16), ("uk", 128, F32), ("ti", 128, I32), ("hi", 128, I32), ("hu", 128, U16),
-            ("Ld0", 128, B16), ("Oxz", 128, H16), ("e", 128, H16), ("eu", 128, U16), ("Ge", 2048, B16), ("Gh", 2048, B16), ("Me", 2048, B16),
-            ("Mh", 2048, B16), ("heS", 128, F32), ("PN", 128, H16), ("P1", 128, H16), ("T1s", 128, B16), ("kod", 64, F32), ("m1", 64, F32), ("m2", 32, F32), ("m3", 16, F32),
-            ("KI", 16, I32), ("KA", 16, I32), ("kk", 16, B16), ("k8s", 128, B16), ("oh", 128, H16), ("sel", 128, H16), ("EQ", 640, B16), ("EQA", 1024, B16),
-            ("wS", 128, B16), ("w", 8, B16), ("wv", 8, F32), ("so", 8, U16), ("c16", 8, B16)):
+            ("d0", 128, B16), ("ab", 256, B16), ("LO", 256, B16), ("m", 128, H16), ("uk", 128, F32), ("t1", 128, I32), ("t2", 128, I32), ("hi", 128, I32), ("hu", 128, U16),
+            ("Ld0", 128, B16), ("Oxz", 128, H16), ("zt", 128, F32), ("e", 128, H16), ("eu", 128, U16), ("hme", 128, H16), ("Oe", 128, H16), ("Oh", 128, H16), ("PN", 128, H16),
+            ("Lst", 256, B16), ("v16", 8, F32), ("pA", 8, B16), ("pD", 16, B16), ("pP", 16, B16), ("c16", 8, B16), ("v1", 8, F32), ("Lv", 8, H16), ("pr", 128, F32), ("w", 8, F32), ("wv", 8, F32),
+            ("so", 16, U16), ("Ge", 2048, B16), ("Gh", 2048, B16), ("Me", 2048, B16), ("Mh", 2048, B16), ("T1", 128, B16), ("PA", 128, H16), ("PB", 128, H16),
+            ("pm", 128, F32), ("KI", 8, I32), ("KA", 8, I32), ("kk", 8, B16), ("k8s", 128, B16), ("oh", 128, B16), ("sel", 128, H16)):
         tile(_n + _k, _c, _d)
     for _t in range(HOPS + 1):
         for _x in ("X", "Y"):
             if (_t < HOPS) if _x == "X" else (_t > 0):
-                buf("%s1_%d" % (_x, _t) + _k, 144, B16)
-                buf("%s2_%d" % (_x, _t) + _k, 24, H16)
+                buf("%s1_%d" % (_x, _t) + _k, 168, B16)
+                buf("%s2_%d" % (_x, _t) + _k, 8, U16)
                 buf("%s3_%d" % (_x, _t) + _k, 128, H16)
     for _j in range(4):
         buf("p" + _k + str(_j), 512, F32, "psum")
@@ -97,117 +99,151 @@ def build():
         ops.append(o)
         return o
 
+    def banks(*xs):
+        return sorted(set(x[0] for x in xs if isinstance(x, tuple) and SCRATCH[x[0]][0] == "psum"))
+
+    def short(*xs):
+        return 0.5 if all(SCRATCH[x[0]][2] in (B16, H16, U16) for x in xs) else 1.0
+
     def load(e, r, w, fo, fi, cost=2.5):
         op(e, r, w, lambda g, T, q: q((g.sync if e == "Y" else g.scalar).dma_start(fo(T), fi(T))), cost, dma=True)
-
-    def val(x, T):
-        return x if isinstance(x, (int, float)) else x(T)
 
     def G(r, w, f, cost):
         op("G", r, w, lambda g, T, q: q(f(g, T)), cost)
 
-    def cp(r, w, o, i, n, banks=(), half=False):
-        op("V", r, w, lambda g, T, q: q(g.vector.tensor_copy(o(T), i(T))), vc(n, 0.5 if half else 1), banks)
+    def ms(w, o, v, r=""):
+        op("V", r, w, lambda g, T, q: q(g.vector.memset(ap(T, o), v)), vc(width(o), short(o)))
 
-    def ts(r, w, o, i, s1, s2, o1, o2, n, banks=(), half=False):
+    def cp(r, w, o, i):
+        op("V", r, w, lambda g, T, q: q(g.vector.tensor_copy(ap(T, o), ap(T, i))), vc(width(o), short(o, i)), banks(o, i))
+
+    def ts(r, w, o, i, s1, o1, s2=None, o2=None):
         def f(g, T, q):
             if o2 is None:
-                q(g.vector.tensor_scalar(o(T), i(T), val(s1, T), None, o1))
+                q(g.vector.tensor_scalar(ap(T, o), ap(T, i), ap(T, s1), None, o1))
             else:
-                q(g.vector.tensor_scalar(o(T), i(T), val(s1, T), s2, o1, o2))
-        op("V", r, w, f, vc(n, 0.5 if half else 1), banks)
+                q(g.vector.tensor_scalar(ap(T, o), ap(T, i), ap(T, s1), ap(T, s2), o1, o2))
+        op("V", r, w, f, vc(width(o), short(o, i)), banks(o, i))
 
-    def tt(r, w, o, i0, i1, al, n, banks=(), both=False):
-        op("V", r, w, lambda g, T, q: q(g.vector.tensor_tensor(o(T), i0(T), i1(T), al)), vc(n, 2 if both else 1), banks)
+    def tt(r, w, o, i0, i1, al):
+        op("V", r, w, lambda g, T, q: q(g.vector.tensor_tensor(ap(T, o), ap(T, i0), ap(T, i1), al)), vc(width(o), 1 if banks(i0, i1) else 2), banks(o, i0, i1))
 
-    def ac(r, w, o, i, fn, n, banks=(), **kw):
-        op("S", r, w, lambda g, T, q: q(g.scalar.activation(o(T), i(T), fn, **dict((k, val(x, T)) for k, x in kw.items()))), vc(n) + 0.03, banks)
+    def scan(r, w, o, d0, d1, o0, o1):
+        op("V", r, w, lambda g, T, q: q(g.vector.tensor_tensor_scan(ap(T, o), ap(T, d0), ap(T, d1), 0.0, o0, o1)), vc(width(o)), banks(o, d0, d1))
 
-    def TM(r, w, lst, banks):
+    def pick(r, w, o, win, off, i1=None, al=None):
+        def f(g, T, q):
+            x = ap(T, win).indirect(ap(T, off))
+            q(g.vector.tensor_copy(ap(T, o), x) if al is None else g.vector.tensor_tensor(ap(T, o), x, ap(T, i1), al))
+        op("V", r, w, f, 0.05 + width(o) * 1.56 * CYC)
+
+    def ac(r, w, o, i, fn, **kw):
+        op("S", r, w, lambda g, T, q: q(g.scalar.activation(ap(T, o), ap(T, i), fn, **dict((k, ap(T, x)) for k, x in kw.items()))), vc(width(o)) + 0.03, banks(o, i))
+
+    def TM(r, w, lst):
         def f(g, T, q):
             for (o, a, b, s, p) in lst:
-                q(g.tensor.matmul(o(T), a(T), b(T), bool(s), bool(p)))
-        op("T", r, w, f, 0.04 + len(lst) * 72 * 0.00042 * 1.2, banks)
+                q(g.tensor.matmul(ap(T, o), ap(T, a), ap(T, b), bool(s), bool(p)))
+        bk = banks(*[x[0] for x in lst])
+        op("T", r, w + "".join(" T" + b for b in bk), f, 0.04 + sum(max(min(64, width(a)), width(b)) for (o, a, b, s, p) in lst) * 0.00042 * 1.25, bk)
 
-    def Lb(b, name="C"):
-        return at(name, 15 - b, 143 - b)
+    def Lb(b, name="C", rows=None):
+        return at(name, 15 - b, 143 - b, 1, rows)
 
     def Rb(b, s=1):
         return at("R", 128 * b, 128 * b + 128, s)
 
-    cI, cIn, cO, G8 = at("I"), at("In"), at("ONES"), at("Bk", 0, 128, 16)
-    load("Y", "", "VDv", at("VD0", 0, 256, 1, 8), lambda T: T.v0[:, :], 2.0)
-    load("S", "", "VDd", at("VD0", 256, 512, 1, 8), lambda T: T.d0[:, :], 2.0)
-    load("Y", "", "PX", at("PX"), lambda T: T.px[:, :], 4.5)
-    load("S", "", "Z0", at("Z0"), lambda T: T.z0[:, :], 2.3)
-    load("Y", "", "VW", at("VW"), lambda T: T.vw[:, :], 6.0)
-    load("S", "", "F0", at("F0"), lambda T: T.f0[:, :], 2.8)
-    load("S", "", "WTi", at("WTi"), lambda T: T.wt[:, :], 2.5)
-    load("S", "", "KPi", at("KPi"), lambda T: T.kap[:, :], 2.8)
-    for nm, v in (("ONES", 1.0), ("ZERO", 0.0), ("C", 0.0), ("P845", 84.5), ("MHALF", -0.5), ("PONE", 1.0), ("MTWO", -2.0), ("PMAG", MAGIC), ("NMAG", -MAGIC), ("Z1", 0.0), ("KQ", -1.0 / 512), ("KH", 1.0 / 256), ("K16", 16.0), ("K1", 1.0 / 128),
-                  ("Kh", -0.5), ("PEN", 0.0), ("RH", 0.0), ("KCT", 0.0)):
-        op("V", "", nm, lambda g, T, q, nm=nm, v=v: q(g.vector.memset(at(nm)(T), v)), vc(PLACE[nm][2], 0.5))
+    def swap(o, lhs, src, stop=0):
+        p, r, a, b, s = o
+        p2, r2, a2, b2, s2 = src
+        return [((p, r, a + j, b, 2), lhs, (p2, r2, a2 + 1 - j, b2, 2), 0, stop and j) for j in (0, 1)]
 
-    op("V", "Z1", "Z1", lambda g, T, q: q(g.vector.memset(at("Z1", 0, 128)(T), 1.0)), vc(64))
+    cI, cIn, cO, G8 = at("I"), at("In"), at("ONES", 0, 128), at("Bk", 0, 128, 16)
+    users = at("VT", 16, 2064)
+    load("Y", "", "VDv", lambda T: ap(T, at("VD0", 0, 256, 1, 8)), lambda T: T.v0[:, :], 2.0)
+    load("S", "", "VDd", lambda T: ap(T, at("VD0", 256, 512, 1, 8)), lambda T: T.d0[:, :], 2.0)
+    load("Y", "", "PX", lambda T: T.PX[:, :], lambda T: T.px[:, :], 4.5)
+    load("S", "", "WTi", lambda T: T.WTi[:, :], lambda T: T.wt[:, :], 2.2)
+    load("S", "", "Z0", lambda T: T.Z0[:, :], lambda T: T.z0[:, :], 2.3)
+    load("S", "", "KPi", lambda T: T.KPi[:, :], lambda T: T.kap[:, :], 2.4)
+    load("S", "", "F0", lambda T: T.F0[:, :], lambda T: T.f0[:, :], 2.8)
+    load("Y", "", "VW", lambda T: T.VW[:, :], lambda T: T.vw[:, :], 6.0)
+    for nm, v in (("ONES", 1.0), ("ZERO", 0.0), ("C", 0.0), ("PMAG", MAGIC), ("NMAG", -MAGIC), ("KQ", -1.0 / 512), ("K1", 1.0 / 128)):
+        ms(nm, at(nm), v)
+    for nm, parts in (("Z1", ((128, -25.5 / 128), (128, -25.5 * BIG / 128), (128, -57.5 / 4096))), ("KS", ((8, 0.0), (8, 1.0 / 128), (16, 0.0), (8, 1.0 / 128))),
+                      ("KV", ((24, 1.0 / 128), (16, -1.0 / 128))), ("KT", [(8, t / 128.0) for t in range(HOPS)]), ("RH", ((24, 0.0), (40, 0.0)))):
+        c0 = 0
+        for n, v in parts:
+            ms(nm, at(nm, c0, c0 + n), v)
+            c0 += n
+    for rows, v in (((0, 32), -1.0 / 64), ((32, 64), 2.0 ** -17), ((64, 128), 0.0)):
+        ms("KU", at("KU", rows=rows), v)
+    ms("KCT", at("KCT", 0, 128), -64.0)
+    ms("KCT", at("KCT", 256, 264), 2048.0)
+    ms("VT0", at("VT", 0, 16), 0)
 
     def aff(src, dst, pat, cmp, base, cm, rows=None):
-        G(src, dst, lambda g, T: g.affine_select(at(dst, rows=rows)(T), at(src, rows=rows)(T), pat, cmp, 0.0, base, cm), 0.4)
-    aff("ONES", "E8", [[-1, 8], [0, 16]], A.is_equal, 0, 1, 8)
+        n = PLACE[dst][2]
+        G(src, dst, lambda g, T: g.affine_select(ap(T, at(dst, rows=rows)), ap(T, at(src, 0, n, 1, rows)), pat, cmp, 0.0, base, cm), 0.45)
+
+    def iota(dst, pat, base, cm, cost, small=False):
+        if small:
+            G("", dst, lambda g, T: g.iota(ap(T, at(dst)), pat, base, cm, allow_small_or_imprecise_dtypes=True), cost)
+        else:
+            G("", dst, lambda g, T: g.iota(ap(T, at(dst)), pat, base, cm), cost)
+    iota("THb", [[19616, 16]], 0, 0, 0.2, True)
+    iota("THi", [[-13824, 128]], 2097152, 0, 0.4, True)
+    aff("ONES", "CT", [[1, 144]], A.is_equal, -15, -16, 8)
     aff("ONES", "Bt", [[-16, 8], [0, 16]], A.is_ge, 0, 1)
     aff("Bt", "Bk", [[16, 8], [0, 16]], A.is_ge, 15, -1)
     aff("ONES", "I", [[-1, 128]], A.is_equal, 0, 1)
-    G("", "Qi", lambda g, T: g.iota(at("Qi")(T), [[-1, 16]], 16, 1), 0.2)
-    G("", "KCi", lambda g, T: g.iota(at("KCi")(T), [[1, 1]], 0, 1), 0.2)
+    iota("Qi", [[-1, 16]], 16, 1, 0.2)
+    iota("KCi", [[1, 1]], 0, 1, 0.2)
     aff("ONES", "SW", [[-2, 64], [1, 2]], A.is_equal, -1, 1)
-    G("", "BROW", lambda g, T: g.iota(at("BROW")(T), [[0, 8], [1, 16]], 0, 0, allow_small_or_imprecise_dtypes=True), 0.4)
-    G("", "TRi", lambda g, T: g.iota(at("TRi")(T), [[32, 8]], 2048, 0), 0.2)
-    cp("Bk C", "C", at("C", 15, 143, 16), G8, 8)
-    ts("C", "C16", at("C16"), at("C"), 1.0 / 16, 0, A.mult, None, 144, half=True)
-    ts("Qi", "Qa", at("Qa"), at("Qi"), 15, 0, A.bitwise_and, None, 16)
-    ts("Qa", "Q", at("Q"), at("Qa"), 0, 0, A.is_equal, None, 16)
-    ts("KCi", "KCa", at("KCa"), at("KCi"), 15, 0, A.bitwise_and, None, 1)
-    cp("KCa", "KC", at("KC"), at("KCa"), 1)
-    ts("KC", "KC2", at("KC2"), at("KC"), 2.0, 0, A.mult, None, 1)
+    iota("BROW", [[0, 8], [1, 16]], 0, 0, 0.4, True)
+    aff("ONES", "E8", [[-1, 8], [0, 16]], A.is_equal, 0, 1, 8)
+    for j in range(16):
+        ac("THi THb", "TH", at("TH", j, 2048, 16), at("THi"), F.Identity, bias=at("THb", j, j + 1))
+    cp("Bk C", "C", at("C", 15, 143, 16), G8)
+    ts("C", "C16", at("C16"), at("C"), 1.0 / 16, A.mult)
+    ts("Qi", "Qa", at("Qa"), at("Qi"), 15, A.bitwise_and)
+    ts("Qa", "Q", at("Q"), at("Qa"), 0, A.is_equal)
+    ts("KCi", "KCa", at("KCa"), at("KCi"), 15, A.bitwise_and)
+    cp("KCa", "KC", at("KC"), at("KCa"))
     for b in range(16):
-        if b % 2:
-            ac("Bk Q", "R", Rb(b), at("Bk"), F.Copy, 128, scale=at("Q", b, b + 1))
-        else:
-            ts("Bk Q", "R", Rb(b), at("Bk"), at("Q", b, b + 1), 0, A.mult, None, 128, half=True)
-    for nm, src, s in (("In", "I", -1.0), ("I2", "I", 2.0), ("I05", "I", 0.5), ("I64", "I", 64.0), ("I2048n", "I", -2048.0), ("I613", "I", 19616.0), ("Bh", "Bk", 0.5)):
-        ts(src, nm, at(nm), at(src), s, 0, A.mult, None, 128, half=True)
-    tt("SW I", "SWI", at("SWI"), at("SW"), cI, A.subtract, 128, both=True)
-    ts("BROW KC", "Forb", at("Forb"), at("BROW"), at("KC"), 4096.0, A.is_le, A.mult, 128, half=True)
-    ts("BROW KCT", "KCT", at("KCT", 128, 256), at("BROW"), 1.0 / 128, 0, A.mult, None, 128, half=True)
-    ts("Bk PEN", "PEN", at("PEN", 0, 128), at("Bk"), -512.0, 0, A.mult, None, 128, half=True)
+        ts("Bk Q", "R", Rb(b), at("Bk"), at("Q", b, b + 1), A.mult)
+    for nm, src, s in (("In", "I", -1.0), ("I2", "I", 2.0), ("I2n", "I", -2.0), ("I05", "I", 0.5), ("I32", "I", 32.0), ("I16", "I", 16.0), ("I25", "I", BIG),
+                       ("I2048n", "I", -2048.0), ("B25", "Bk", BIG), ("B32", "Bk", 1.0 / 32), ("SW32", "SW", 1.0 / 32), ("PEN", "Bk", 512.0)):
+        ac(src, nm, at(nm), at(src), F.Copy, scale=s)
+    tt("SW I", "SWI", at("SWI"), at("SW"), cI, A.subtract)
+    tt("SW In", "SWn", at("SWn"), cIn, at("SW"), A.subtract)
+    ts("BROW KC", "Forb", at("Forb"), at("BROW"), at("KC"), A.is_gt, 64.0, A.mult)
+    ts("BROW", "RSTH", at("RSTH"), at("BROW"), 0.0, A.is_equal, 2.0 ** 20, A.mult)
+    ts("BROW", "KCT", at("KCT", 128, 256), at("BROW"), 1.0 / 128, A.mult)
     for c0, s in ((0, 2.0), (16, -1.0), (32, -2.0), (40, 32.0), (48, 1.0), (56, -16.0)):
-        ts("Bk RH", "RH", at("RH", c0, c0 + 8), G8, s, 0, A.mult, None, 8)
-    for c0, s in ((0, 1.0 / 16), (8, -1.0 / 16), (16, 0.5)):
-        ts("Bk", "G24", at("G24", c0, c0 + 8), G8, s, 0, A.mult, None, 8)
-    ts("TRi KC2", "TR", at("TR"), at("TRi"), at("KC2"), 0, A.add, None, 8)
-    ts("TRi KC2", "TRF", at("TRF"), at("TRi"), at("KC2"), 0, A.add, None, 8)
-    ac("I", "IF", at("IF"), cI, F.Copy, 128)
-    ts("WTi", "WT32", at("WT32"), at("WTi"), 32.0, 0, A.mult, None, 1)
-    ts("KPi", "KP32", at("KP32"), at("KPi"), 1.0 / 32, 0, A.mult, None, 1)
-    ts("C WT32", "CW", at("CW"), at("C"), at("WT32"), 0, A.mult, None, 144, half=True)
-    cp("VDv VDd", "VDh", at("VDh", rows=8), at("VD0", rows=8), 512)
-    TM("E8 VDh", "vdF", [(at("p00"), at("E8", rows=8), at("VDh", rows=8), 1, 1)], ["p00"])
-    cp("vdF", "VDF", at("VDF"), at("p00"), 512, ["p00"])
-    TM("VDF C16", "vdL", [(at("p01", 0, 32), Lb(b, "C16"), at("VDF", b, 512, 16), b == 0, b == 15) for b in range(16)], ["p01"])
+        ts("Bk RH", "RH2", at("RH", c0, c0 + 8), G8, s, A.mult)
+    for c0, s in ((0, -32768.0), (8, 0.5)):
+        ts("Bk", "GL", at("GL", c0, c0 + 8), G8, s, A.mult)
+    cp("WTi", "WTa", at("WTa"), at("WTi"))
+    ts("WTi", "WTb", at("WTb"), at("WTi"), 1.0 / 2048, A.mult)
+    cp("KPi", "KP", at("KP"), at("KPi"))
+    ts("Bk WTa", "Wa", at("Wa"), at("Bk"), at("WTa"), A.mult)
+    ts("Bk WTb", "Wb", at("Wb"), at("Bk"), at("WTb"), A.mult)
+    cp("VDv", "VDh", at("VDh", 0, 256, 1, 8), at("VD0", 0, 256, 1, 8))
+    cp("VDd", "VDh", at("VDh", 256, 512, 1, 8), at("VD0", 256, 512, 1, 8))
+    TM("VDh CT", "vdL", [(at("p03", 0, 32), Lb(b, "CT", 8), at("VDh", b, 512, 16, 8), b == 0, b == 15) for b in range(16)])
     for k in (0, 1):
-        x1, x2 = "X1_0%d" % k, "X2_0%d" % k
-        cp("vdL", x2 + "v", at(x2, 0, 8), at("p01", 8 * k, 8 * k + 8), 8, ["p01"])
-        cp("vdL", x1 + "D", at(x1, 136, 144), at("p01", 16 + 8 * k, 24 + 8 * k), 8, ["p01"])
-        ts(x1 + "D", "Dg%d" % k, at(x2, 16, 24), at(x1, 136, 144), 1.0, 64.0, A.is_ge, A.mult, 8)
-        ts("Dg%d" % k, x2 + "g", at(x2, 8, 16), at(x2, 16, 24), 64.0, 0, A.subtract, None, 8)
-        cp("ZERO", x1 + "A", at(x1, 128, 136), at("ZERO", 0, 8), 8)
-        cp("ZERO Dg%d " % k + x2 + "g", x2 + "p", at(x2, 16, 24), at("ZERO", 0, 8), 8)
-        ops[-1]["w"].append("Dg%d" % k)
-        cp("Z0", x1 + "z", at(x1, 0, 128), at("Z0", 128 * k, 128 * k + 128), 128, half=True)
-        cp("F0", x2 + "f", at("X3_0%d" % k), at("F0", 128 * k, 128 * k + 128), 128)
-    ts("VW", "VT", at("VT", 0, 1024), at("VW"), 2047, 0, A.bitwise_and, None, 1024)
-    ts("VW", "VT2", at("VT", 1024, 2048), at("VW"), 11, 0, A.logical_shift_right, None, 1024)
-
-    cp("ZERO", "VT3", at("VT", 2048, 2304), at("ZERO", 0, 256), 256)
+        x1, o = "X1_0%d" % k, 8 * (1 - k)
+        cp("vdL", "X2_0%d" % k, at("X2_0%d" % k), at("p03", o, o + 8))
+        cp("vdL", x1 + "c", at(x1, 136, 144), at("p03", 16 + o, 24 + o))
+        ts("vdL", x1 + "c", at(x1, 160, 168), at("p03", 16 + o, 24 + o), 1.0, A.is_ge)
+        ms("Lst%d" % k, at("Lst%d" % k), 0.0)
+        ms(x1 + "c", at(x1, 128, 136), 0.0)
+        ms(x1 + "c", at(x1, 144, 160), 0.0)
+        cp("Z0", x1 + "z", at(x1, 0, 128), at("Z0", 16 * o, 16 * o + 128))
+        cp("F0", "X3_0%d" % k, at("X3_0%d" % k), at("F0", 16 * o, 16 * o + 128))
+    ts("VW", "VT1", at("VT", 16, 1040), at("VW"), 2047, A.bitwise_and)
+    ts("VW", "VT2", at("VT", 1040, 2064), at("VW"), 11, A.logical_shift_right)
 
     def send(t, k, part, rd, wr):
         x = "%d_%d%d" % (part, t + 1, k)
@@ -217,190 +253,163 @@ def build():
 
     def names(t, k):
         K = str(k)
-        return (K, "X1_%d" % t + K, "X2_%d" % t + K, "Y1_%d" % (t + 1) + K, "Y2_%d" % (t + 1) + K, "p%d0" % k, "p%d1" % k, "p%d2" % k, "p%d3" % k,
-                lambda s: " ".join(n + K for n in s.split()), lambda n, a=0, b=None, s=1: at(n + K, a, b, s))
+        return (K, "X1_%d" % t + K, "X2_%d" % t + K, "X3_%d" % t + K, "Y1_%d" % (t + 1) + K, "Y2_%d" % (t + 1) + K, "Y3_%d" % (t + 1) + K,
+                lambda s: "".join(" " + (n + K if n[-1] != "!" else n[:-1]) for n in s.split()), lambda n, a=0, b=None, s=1, rows=None: at(n + K, a, b, s, rows),
+                lambda j, a, b, s=1, rows=None: at("p%d%d" % (k, j), a, b, s, rows))
 
     def head(t, k):
-        K, x1, x2, y1, y2, b0, b1, b2, b3, u, tl = names(t, k)
-        zX, fX, vX, AX, DX = at(x1, 0, 128), at("X3_%d" % t + K), at(x2, 0, 8), at(x1, 128, 136), at(x1, 136, 144)
-        zk, fk, vk, Ak, Dk = x1 + "z", x2 + "f", x2 + "v", x1 + "A", x1 + "D"
-        tL, tO, tN = tl("LON", 128, 256), tl("LON", 256, 384), tl("LON", 384, 512)
-        cp(vk, u("vu"), tl("vu"), vX, 8)
-        op("S", u("vu") + " PX", u("xb"), lambda g, T, q: q(g.scalar.activation(tl("xb")(T), T.PX[:, :].indirect(tl("vu")(T)), F.Identity)), 0.1 + 128 * 1.56 * CYC)
-        TM(vk + " %sg %sp R Z1 I" % (x2, x2), "vF" + K + " sco" + K, [(at(b1, 128, 512), cI, at("Z1"), 1, 0)] + [
-            (at(b1, 128 + b, 512, 16), Rb(b), at(x2), 0, 0) for b in range(16)], [b1])
-        TM(zk + " " + vk + " CW I613", "au" + K, [(at(b3, 24, 32), Lb(b, "CW"), at(x1, b, 128, 16), b == 0, b == 15) for b in range(16)] + [
-            (at(b3, 32, 40), at("I613"), vX, 1, 1)], [b3])
-        TM(vk + " " + Ak + " " + Dk + " SWI K1 ONES I In TR", "av" + K, [
-            (at(b3, 48, 56), at("SWI"), AX, 1, 0), (at(b3, 48, 56), cO, at("K1"), 0, 1),
-            (at(b3, 56, 64), cI, DX, 1, 0), (at(b3, 56, 64), cO, at("K1"), 0, 1), (at(b3, 112, 120), cI, vX, 1, 0), (at(b3, 112, 120), cO, at("K1"), 0, 1),
-            (at(b3, 120, 128), cI, vX, 1, 0), (at(b3, 120, 128), cIn, at("TR"), 0, 1)], [b3])
-        TM(u("xb") + " " + zk + " I In", "d0" + K, [(at(b0, 0, 128), cI, tl("xb"), 1, 0), (at(b0, 0, 128), cIn, zX, 0, 1)], [b0])
-        ac("d0" + K, u("ad"), tl("ad"), at(b0, 0, 128), F.Abs, 128, [b0])
-        ac(u("ad") + " P845", u("ind"), tl("ind"), tl("ad"), F.Sign, 128, scale=-1.0, bias=at("P845"))
-        TM(u("ind") + " sco" + K + " Bh", "sco" + K, [(at(b1, 256, 384, 2), at("Bh"), tl("ind", 1, 128, 2), 0, 0), (at(b1, 257, 384, 2), at("Bh"), tl("ind", 0, 128, 2), 0, 0),
-                                                      (at(b1, 384, 512), at("Bh"), tl("ind"), 0, 1)], [b1])
-        TM(fk + " I", "fF" + K, [(at(b2, 0, 128), cI, fX, 1, 1)], [b2])
-        TM(u("xb") + " " + zk + " I In", "xz" + K, [(at(b2, 256, 384), cIn, zX, 1, 0), (at(b2, 256, 384), cIn, zX, 0, 0)] + [
-            (at(b2, 256 + r, 384, 2), cI, at(src, 1 - r, 128, 2), 0, r and src == x1) for r in (0, 1) for src in ("xb" + K, x1)], [b2])
-        cp("au" + K, u("ui"), tl("ui"), at(b3, 24, 40), 16, [b3])
-        ts(u("ui"), u("uj"), tl("uj"), tl("ui"), 65535, 0, A.bitwise_and, None, 16)
-        cp(u("uj"), u("uh"), tl("uh"), tl("uj"), 16)
-        TM(u("uh") + " ZERO R I", "hF" + K, [(at(b3, 128, 384), cI, at("ZERO", 0, 256), 1, 0)] + [
-            (at(b3, 128 + b, 384, 16), Rb(b), tl("uh"), 0, b == 15) for b in range(16)], [b3])
-        ac("hF" + K + " KP32", u("uk"), tl("uk"), at(b3, 128, 256), F.Identity, 128, [b3], scale=at("KP32"))
-        tt(u("uk") + " hF" + K, u("ti"), tl("ti"), tl("uk"), at(b3, 256, 384), A.add, 128, [b3])
-        ts(u("ti"), u("hi"), tl("hi"), tl("ti"), 5, 2047, A.logical_shift_right, A.bitwise_and, 128)
-        ts("sco" + K, "LL" + K, tl("LON", 0, 256), at(b1, 256, 512), 1.5, 0, A.is_ge, None, 256, [b1])
-        TM("LL" + K + " I2 I", "m" + K, [(at(b1, 0, 128), at("I2"), tL, 1, 0), (at(b1, 0, 128), cI, tl("LON", 0, 128), 0, 1)], [b1])
-        ts("m" + K, "OO" + K, tO, at(b1, 0, 128), 1.0, 0, A.is_equal, None, 128, [b1])
-        ts("m" + K, "NN" + K, tN, at(b1, 0, 128), 0.5, 0, A.is_lt, None, 128, [b1])
-        cp("vF" + K, u("vFs"), tl("vFs"), at(b1, 128, 256), 128, [b1])
-        tt("LL" + K + " fF" + K, u("fL"), tl("fL"), tL, at(b2, 0, 128), A.mult, 128, [b2])
-        TM("NN" + K + " I", "nP" + K, [(at(b1, 128, 256), cI, tN, 1, 1)], [b1])
-        tt("nP" + K + " " + u("hi"), u("hN"), tl("hN"), tl("hi"), at(b1, 128, 256), A.mult, 128, [b1])
-        hs = [(cI, tl("fL"), 1, 0), (cI, tl("hN"), 0, 1)]
-        TM(u("fL hN") + " I", "hh" + K, [(at(b1, 0, 128), a, b, s, p) for a, b, s, p in hs], [b1])
-        cp("hh" + K, u("hu"), tl("hu"), at(b1, 0, 128), 128, [b1])
-        tt("LL" + K + " d0" + K, u("Ld0"), tl("Ld0"), tL, at(b0, 0, 128), A.mult, 128, [b0])
-        tt("OO" + K + " xz" + K, u("Oxz"), tl("Oxz"), tO, at(b2, 256, 384), A.mult, 128, [b2])
-        TM(zk + " " + u("Ld0") + " I", "q" + K, [(at(b0, 128, 256), cI, zX, 1, 0), (at(b0, 128, 256), cI, tl("Ld0"), 0, 1)], [b0])
-        zr, hf = at(b0, 256, 384), at("I05")
-        TM(zk + " " + u("Ld0 Oxz") + " I I05 KQ ONES", "zn" + K, [(zr, cI, zX, 1, 0), (zr, hf, tl("Ld0"), 0, 0), (zr, hf, tl("Oxz"), 0, 0), (zr, cO, at("KQ"), 0, 1)], [b0])
-        ac("zn" + K + " PMAG", u("zt"), tl("zt"), zr, F.Identity, 128, [b0], bias=at("PMAG"))
-        ac(u("zt") + " NMAG", y1 + "z", at(y1, 0, 128), tl("zt"), F.Identity, 128, bias=at("NMAG"))
-        TM("LL%s OO%s NN%s C16" % (K, K, K), "ll" + K, [(at(b3, 0, 24), Lb(b, "C16"), tl("LON", 128 + b, 512, 16), b == 0, b == 15) for b in range(16)], [b3])
-        lL, lO, lN = tl("Lst", 0, 8), tl("Lst", 8, 16), tl("Lst", 16, 24)
-        cp("ll" + K, u("Lst"), tl("Lst"), at(b3, 0, 24), 24, [b3])
-        op("V", u("vu") + " VT VT2", u("e"), lambda g, T, q: q(g.vector.tensor_copy(tl("e")(T), T.VT[:, 0:2048].indirect(tl("vu")(T)))), 0.05 + 128 * 1.56 * CYC)
-        cp(u("e"), u("eu"), tl("eu"), tl("e"), 128, half=True)
-        TM(u("fL hN e") + " I In", "he" + K, [(at(b1, 0, 128), a, b, s, 0) for a, b, s, p in hs] + [(at(b1, 0, 128), cIn, tl("e"), 0, 1)], [b1])
-        ac("he" + K, u("heS"), tl("heS"), at(b1, 0, 128), F.Copy, 128, [b1])
-        tt("NN" + K + " he" + K, u("PN"), tl("PN"), tN, at(b1, 0, 128), A.mult, 128, [b1])
-        tt("av" + K + " " + u("Lst"), y1 + "A " + y1 + "D", at(y1, 128, 144), tl("Lst", 8, 24), at(b3, 48, 64), A.mult, 16, [b3])
-        TM(u("Lst") + " " + y1 + "A " + Ak + " I", "nl" + K, [(at(b3, 72, 80), cI, AX, 1, 0), (at(b3, 72, 80), cI, lL, 0, 0), (at(b3, 72, 80), cI, at(y1, 128, 136), 0, 1)], [b3])
-        cp("nl" + K, y1 + "A", at(y1, 128, 136), at(b3, 72, 80), 8, [b3])
+        K, x1, x2, x3, y1, y2, y3, u, tl, ps = names(t, k)
+        zX, fX, vX, AX, DX, PX_ = at(x1, 0, 128), at(x3), at(x2), at(x1, 128, 136), at(x1, 136, 144), at(x1, 144, 152)
+        zk, ck = x1 + "z ", x1 + "c "
+        tL, tO, ta, tb = tl("LO", 0, 128), tl("LO", 128, 256), tl("ab", 0, 128), tl("ab", 128, 256)
+        lL, lO, lst = tl("Lst", 0, 128, 16), tl("Lst", 128, 256, 16), tl("Lst", 0, 256, 16)
+        TM(zk + "Wb KU ONES", u("U"), [(ps(2, 0, 128), at("Wb"), zX, 1, 0), (ps(2, 0, 128), cO, at("KU"), 0, 1)])
+        ts(u("U"), u("m"), tl("m"), ps(2, 0, 128), MAGIC, A.add, MAGIC, A.subtract)
+        TM(zk + u("m Wa! I2048n!"), u("u"), [(ps(2, 128, 256), at("Wa"), zX, 1, 0), (ps(2, 128, 256), at("I2048n"), tl("m"), 0, 1)])
+        ac(u("u KP!"), u("uk"), tl("uk"), ps(2, 128, 256), F.Identity, scale=at("KP"))
+        TM(ck + "R Z1 ONES", u("sc B"), [(ps(1, 0, 384), cO, at("Z1"), 1, 0)] + [(ps(1, b, 384, 16), Rb(b), at(x1, 144, 168), 0, 0) for b in range(16)])
+        pick(x2 + " PX " + zk, u("d0"), tl("d0"), at("PX"), vX, zX, A.subtract)
+        ts(u("d0"), u("a"), ta, tl("d0"), 84.0, A.is_le)
+        ts(u("d0"), u("b"), tb, tl("d0"), -84.0, A.is_ge)
+        pick(x2 + " TH " + u("uk"), u("t1"), tl("t1"), at("TH"), vX, tl("uk"), A.add)
+
+        def liked():
+            ts(u("sc"), u("L"), tL, ps(1, 0, 128), 0.0, A.is_ge)
+            tt(u("sc L"), u("O"), tO, tL, ps(1, 256, 384), A.is_lt)
+
+        def second():
+            tt(u("t1 B"), u("t2"), tl("t2"), tl("t1"), ps(1, 128, 256), A.max)
+            ts(u("t2"), u("hi"), tl("hi"), tl("t2"), 5, A.logical_shift_right, 2047, A.bitwise_and)
+            cp(u("hi"), u("hu"), tl("hu"), tl("hi"))
+
+        for n, x in (("a", ta), ("b", tb)):
+            TM(u(n + " sc B Bk! B25! B32!"), u("sc B"), [(ps(1, 128, 256), at("B25"), x, 0, 0), (ps(1, 0, 128), at("Bk"), x, 0, 0)] + swap(ps(1, 256, 384), at("B32"), x))
+        TM(x3 + u("sc B I32!"), u("sc B"), [(ps(1, 128, 256), at("I32"), fX, 0, 1)])
+        for step in ((second, liked) if FIRST[k] == "h" else (liked, second)):
+            step()
+        TM(u("d0 I!"), u("D0"), [(ps(0, 0, 128), cI, tl("d0"), 1, 1)])
+        TM(zk + u("d0 I! I2! I2n!"), u("xz"), [(ps(0, 384, 512), at("I2n"), zX, 1, 0)] + swap(ps(0, 384, 512), cI, tl("d0")) + swap(ps(0, 384, 512), at("I2"), zX, 1))
+        tt(u("L D0"), u("Ld0"), tl("Ld0"), tL, ps(0, 0, 128), A.mult)
+        tt(u("O xz"), u("Oxz"), tl("Oxz"), tO, ps(0, 384, 512), A.mult)
+        TM(zk + u("Ld0 I!"), u("q"), [(ps(0, 128, 256), cI, zX, 1, 0), (ps(0, 128, 256), cI, tl("Ld0"), 0, 1)])
+        zr, hf = ps(0, 256, 384), at("I05")
+        TM(zk + u("Ld0 Oxz I! I05! KQ! ONES!"), u("zn"), [(zr, cI, zX, 1, 0), (zr, hf, tl("Ld0"), 0, 0), (zr, hf, tl("Oxz"), 0, 0), (zr, cO, at("KQ"), 0, 1)])
+        ac(u("zn PMAG!"), u("zt"), tl("zt"), zr, F.Identity, bias=at("PMAG"))
+        ac(u("zt NMAG!"), y1 + "z", at(y1, 0, 128), tl("zt"), F.Identity, bias=at("NMAG"))
+        pick(x2 + " VT1 VT2 VT", u("e"), tl("e"), users, vX)
+        cp(u("e"), u("eu"), tl("eu"), tl("e"))
+        TM(u("e I! In!"), u("eP"), [(ps(1, 0, 128), cI, tl("e"), 1, 1), (ps(1, 128, 256), cIn, tl("e"), 1, 0)] + swap(ps(1, 128, 256), cI, tl("e"), 1))
+        TM(u("L O I! In! ONES! K1! ZERO!"), u("oP"), [(ps(1, 256, 384), cI, at("ZERO"), 1, 0)] + swap(ps(1, 256, 384), cI, tO, 1) + [
+            (ps(1, 384, 512), cO, at("K1"), 1, 0), (ps(1, 384, 512), cIn, tL, 0, 0), (ps(1, 384, 512), cIn, tO, 0, 1)])
+        tt(u("hi eP"), u("hme"), tl("hme"), tl("hi"), ps(1, 0, 128), A.subtract)
+        tt(u("O eP"), u("Oe"), tl("Oe"), tO, ps(1, 128, 256), A.mult)
+        tt(u("hme oP"), u("Oh"), tl("Oh"), tl("hme"), ps(1, 256, 384), A.mult)
+        tt(u("hme oP"), u("PN"), tl("PN"), tl("hme"), ps(1, 384, 512), A.mult)
+        TM(u("hme Oh I!"), u("H"), [(ps(1, 0, 128), tl("hme"), cI, 1, 1), (ps(1, 128, 256), tl("Oh"), cI, 1, 1)])
+        TM(u("L O C16!"), u("ll"), [(ps(3, 0, 16), Lb(b, "C16"), tl("LO", b, 256, 16), b == 0, b == 15) for b in range(16)])
+        TM(ck + "KV SWI SWn I I2n ONES", u("val"), [
+            (ps(3, 16, 56), cO, at("KV"), 1, 0), (ps(3, 16, 24), at("SWI"), AX, 0, 0), (ps(3, 24, 32), cI, DX, 0, 0), (ps(3, 32, 40), cI, DX, 0, 0),
+            (ps(3, 40, 48), at("I2n"), PX_, 0, 0), (ps(3, 48, 56), at("SWn"), PX_, 0, 1)])
+        cp(u("ll"), u("Lst"), lst, ps(3, 0, 16))
+        tt(u("Lst val"), u("pA"), tl("pA"), lO, ps(3, 16, 24), A.mult)
+        tt(u("Lst val"), u("pD"), tl("pD"), lst, ps(3, 24, 40), A.mult)
+        dL, dO, pL, pO = tl("pD", 0, 8), tl("pD", 8, 16), tl("pP", 0, 8), tl("pP", 8, 16)
         if t < HOPS - 1:
-            send(t, k, 1, " ".join((y1 + "z", y1 + "A", y1 + "D")), " ".join("X1_%d" % (t + 1) + K + s for s in "zAD"))
-            ac("nl" + K + " MTWO", u("aB"), tl("aB"), at(b3, 72, 80), F.Abs, 8, [b3], bias=at("MTWO"))
-            ts(u("aB"), y2 + "p", at(y2, 16, 24), tl("aB"), 1.0, -1.0, A.is_equal, A.mult, 8)
-            ac(y1 + "D", u("c16"), tl("c16"), at(y1, 136, 144), F.Sign, 8)
-            TM(y2 + "p " + u("c16") + " SW I64 ONES Kh", "pg" + K, [(at(b3, 104, 112), at("SW"), at(y2, 16, 24), 1, 0), (at(b3, 104, 112), at("I64"), tl("c16"), 0, 0),
-                                                              (at(b3, 104, 112), cO, at("Kh"), 0, 1)], [b3])
-            cp("pg" + K, y2 + "g", at(y2, 8, 16), at(b3, 104, 112), 8, [b3])
+            tt(u("Lst val"), u("pP"), tl("pP"), lst, ps(3, 40, 56), A.mult)
+            mm = [(ps(3, 64, 104), cO, at("KS"), 1, 0), (ps(3, 64, 88), cI, at(x1, 128, 152), 0, 0)]
+            for c0, lhs, srcs in ((64, cI, (lL, tl("pA"))), (72, cIn, (dL, dO)), (80, cI, (pL, pO)), (88, at("I25"), (PX_, pL, pO)), (96, at("SW32"), (PX_, pL, pO)),
+                                  (96, cIn, (lL, lO))):
+                mm += [(ps(3, c0, c0 + 8), lhs, s, 0, s is lO) for s in srcs]
+            TM(ck + u("Lst pA pD pP I! In! I25! SW32! KS! ONES!"), u("nl"), mm)
+            cp(u("nl"), y1 + "c", at(y1, 128, 168), ps(3, 64, 104))
+            send(t, k, 1, y1 + "z " + y1 + "c", " ".join("X1_%d" % (t + 1) + K + s for s in "zc"))
         else:
-            r8 = at(b3, 128, 256, 1, 8)
-            ts(y1 + "A", u("c16"), tl("c16"), at(y1, 128, 136), 16.0, 0, A.mult, None, 8)
-            TM(u("c16") + " " + y1 + "D R Bk ZERO", "yc" + K, [(r8, G8, at("ZERO", 0, 128), 1, 0)] + [
-                (at(b3, 128 + b, 256, 16, 8), Rb(b, 16), s, 0, b == 15 and j == 1) for b in range(16) for j, s in enumerate((tl("c16"), at(y1, 136, 144)))], [b3])
-            ac("yc" + K, "YC" + K, at("YC", 128 * k, 128 * k + 128, 1, 8), r8, F.Copy, 128, [b3])
-            load("Y", "YC" + K, "oc" + K, lambda T: T.yc[:, 128 * k:128 * k + 128], at("YC", 128 * k, 128 * k + 128, 1, 8))
-        tt("av" + K + " " + u("Lst"), u("Lv"), tl("Lv"), lL, at(b3, 112, 120), A.mult, 8, [b3])
-        cp(u("Lv"), u("vlm"), tl("vlm"), tl("Lv"), 8)
-        TM(u("vFs Lv") + " I Forb In", "dg" + K, [(at(b3, 384, 512), cI, tl("vFs"), 1, 0), (at(b3, 384, 512), cI, at("Forb"), 0, 0)] + [
-            (at(b3, 384 + b, 512, 16), cIn, tl("Lv"), 0, b == 15) for b in range(16)], [b3])
-        ts("dg" + K, "EQ" + K, tl("EQ", 0, 128), at(b3, 384, 512), 0.0, 0, A.is_equal, None, 128, [b3])
-        mm = [(at(b3, 384, 512), cI, tl("EQ", 0, 128), 1, 0)]
-        eqs = ["EQ" + K]
-        o = 128
-        for c in range(7):
-            s0 = 16 * (c + 1)
-            n = 128 - s0
-            eqs.append("EQ%d_" % c + K)
-            ts(u("vFs vlm"), eqs[-1], tl("EQ", o, o + n), tl("vFs", s0, 128), tl("vlm", c, c + 1), 0, A.is_equal, None, n, half=True)
-            mm.append((at(b3, 384 + s0, 512), cI, tl("EQ", o, o + n), 0, c == 6 and not k))
-            o += n
-        for c in range(8 if k else 0):
-            eqs.append("EQA%d_" % c)
-            ts(u("vFs") + " vlm0", eqs[-1], tl("EQA", 128 * c, 128 * c + 128), tl("vFs"), at("vlm0", c, c + 1), 0, A.is_equal, None, 128, half=True)
-            mm.append((at(b3, 384, 512), cI, tl("EQA", 128 * c, 128 * c + 128), 0, c == 7))
-        TM(" ".join(eqs) + " I", "ws" + K, mm, [b3])
-        ac("ws" + K, u("wS"), tl("wS"), at(b3, 384, 512), F.Copy, 128, [b3])
-        TM(u("wS Lst") + " C K16 I2048n ONES", "wl" + K, [(at(b3, 88, 96), cO, at("K16"), 1, 0), (at(b3, 88, 96), at("I2048n"), lL, 0, 0)] + [
-            (at(b3, 88, 96), Lb(b), tl("wS", b, 128, 16), 0, b == 15) for b in range(16)], [b3])
-        ac("wl" + K + " PONE", u("w"), tl("w"), at(b3, 88, 96), F.Relu, 8, [b3], scale=-1.0, bias=at("PONE"))
-        tt(u("w") + " av" + K, u("wv"), tl("wv"), tl("w"), at(b3, 120, 128), A.mult, 8, [b3])
-        TM(u("wv") + " TRF IF", "sl" + K, [(at(b3, 96, 104), at("IF"), at("TRF"), 1, 0), (at(b3, 96, 104), at("IF"), tl("wv"), 0, 1)], [b3])
-        cp("sl" + K, u("so"), tl("so"), at(b3, 96, 104), 8, [b3])
+            cc, r8, c0 = ps(3, 64, 72), ps(3, 128, 256, 1, 8), 128 * (1 - k)
+            TM(ck + u("Lst pA pD I! In! I16! K1! ONES!"), u("nl"), [(cc, cO, at("K1", 0, 8), 1, 0), (cc, cI, DX, 0, 0), (cc, cIn, dL, 0, 0), (cc, cIn, dO, 0, 0)] + [
+                (cc, at("I16"), s, 0, s is lL) for s in (AX, tl("pA"), lL)])
+            cp(u("nl"), u("c16"), tl("c16"), cc)
+            TM(u("c16 R! Bk! ZERO!"), u("yc"), [(r8, G8, at("ZERO"), 1, 0)] + [(ps(3, 128 + b, 256, 16, 8), Rb(b, 16), tl("c16"), 0, b == 15) for b in range(16)])
+            ac(u("yc"), u("YC"), at("YC", c0, c0 + 128, 1, 8), r8, F.Copy)
+            load("Y", u("YC"), u("oc"), lambda T: T.yc[:, c0:c0 + 128], lambda T: ap(T, at("YC", c0, c0 + 128, 1, 8)))
+        ts(x2, u("v1"), tl("v1"), vX, 1.0, A.add, 1.0 / 64, A.mult)
+        ts(x2, u("v16"), tl("v16"), vX, 16.0, A.add)
+        tt(u("v1 Lst"), u("Lv"), tl("Lv"), tl("v1"), lL, A.mult)
+        mm = [(ps(3, 256, 384), cI, at("Forb"), 1, 0)]
+        for j in range(1, 16):
+            mm += [(ps(3, 256 + j, 384, 16), Rb(j - 1), tl("Lv"), 0, 0), (ps(3, 256 + j, 384, 16), cIn, tl("Lv"), 0, j == 15)]
+        TM(u("Lv I! In! Forb! R!"), u("dg"), mm)
+        scan(u("dg Lst"), u("pr"), tl("pr"), ps(3, 256, 384), tl("Lst", 0, 128), A.mult, A.add)
+        ts(u("pr"), u("w"), tl("w"), tl("pr", 15, 128, 16), 0.0, A.not_equal)
+        tt(u("w v16"), u("wv"), tl("wv"), tl("w"), tl("v16"), A.mult)
+        ts(u("wv KC!"), u("so"), tl("so", 0, 16, 2), tl("wv"), at("KC"), A.max)
+        TM(u("e Oe PN I!"), u("Y"), [(ps(3, 384, 512), cI, tl(n), n == "e", 0) for n in ("e", "Oe", "PN")])
 
     def tail(t, k):
-        K, x1, x2, y1, y2, b0, b1, b2, b3, u, tl = names(t, k)
+        K, x1, x2, x3, y1, y2, y3, u, tl, ps = names(t, k)
         last = t == HOPS - 1
-        tO, tN = tl("LON", 256, 384), tl("LON", 384, 512)
-        for nm in ("e", "h"):
-            n = 128 // HALVES[nm]
-            for j in range(HALVES[nm]):
-                gk = " ".join("G%s%d%d_" % (nm, j, i) + K for i in range(PIECES[nm]))
+        tL, tO = tl("LO", 0, 128), tl("LO", 128, 256)
+        both = (FIRST[k], "h" if FIRST[k] == "e" else "e")
+        per = 64 // PIECE
+        for nm in both:
+            for j in (0, 1):
+                gk = " ".join("G%s%d%d_" % (nm, j, i) + K for i in range(per))
                 for i, gi in enumerate(gk.split()):
-                    c0, c1 = n * j + n * i // PIECES[nm], n * j + n * (i + 1) // PIECES[nm]
-                    if (nm, j, i) in VSHARE:
-                        op("V", u(nm + "u") + " PX", gi, lambda g, T, q, nm=nm, c0=c0, c1=c1: q(g.vector.tensor_copy(tl("G" + nm, 16 * c0, 16 * c1)(T),
-                           T.PX[:, :].indirect(tl(nm + "u", c0, c1)(T)))), 0.1 + 16 * (c1 - c0) * 1.56 * CYC)
-                        continue
-                    op("S", u(nm + "u") + " PX", gi, lambda g, T, q, nm=nm, c0=c0, c1=c1: q(g.scalar.activation(tl("G" + nm, 16 * c0, 16 * c1)(T),
-                       T.PX[:, :].indirect(tl(nm + "u", c0, c1)(T)), F.Identity)), 0.1 + 16 * (c1 - c0) * 1.56 * CYC)
+                    c0 = 64 * j + PIECE * i
+                    op("S", u(nm + "u PX!"), gi, lambda g, T, q, nm=nm, c0=c0: q(g.scalar.activation(ap(T, tl("G" + nm, 16 * c0, 16 * (c0 + PIECE))),
+                       T.PX[:, :].indirect(ap(T, tl(nm + "u", c0, c0 + PIECE))), F.Identity)), 0.08 + 16 * PIECE * 1.56 * CYC)
                 for kq in range(0, 16, 2):
-                    def f(g, T, q, nm=nm, j=j, n=n, kq=kq):
+                    def f(g, T, q, nm=nm, j=j, kq=kq):
                         for i in (kq, kq + 1):
-                            q(g.vector.tensor_tensor(tl("M" + nm, i * 128 + n * j, i * 128 + n * (j + 1))(T), tl("G" + nm, 16 * n * j + i, 16 * n * (j + 1), 16)(T),
-                                                     at(b0, 128 + n * j, 128 + n * (j + 1))(T), A.max))
-                    op("V", gk + " q" + K, "M%s%d_%d_" % (nm, j, kq) + K, f, 2 * vc(n), [b0])
-        dk = "dist" + K
-        TM("NN" + K + " KCT PEN ONES", dk, [(at(b2, 0, 256), cO, at("KCT"), 1, 0), (at(b2, 0, 256), tN, at("PEN"), 0, 0)], [b2])
-        for nm in ("e", "h"):
-            gs = " ".join("G%s%d%d_" % (nm, j, i) + K for j in range(HALVES[nm]) for i in range(PIECES[nm]))
+                            q(g.vector.tensor_tensor(ap(T, tl("M" + nm, i * 128 + 64 * j, i * 128 + 64 * (j + 1))), ap(T, tl("G" + nm, 1024 * j + i, 1024 * (j + 1), 16)),
+                                                     ap(T, ps(0, 128 + 64 * j, 192 + 64 * j)), A.max))
+                    op("V", gk + u(" q"), "M%s%d_%d_" % (nm, j, kq) + K, f, 2 * vc(64), ["p%d0" % k])
+        dk, lk = u("dist"), ps(2, 256, 264)
+        TM(y1 + "z " + u("L O KCT! KT! PEN! GL! ONES! Bk!"), dk, [
+            (ps(2, 0, 264), cO, at("KCT"), 1, 0), (ps(2, 0, 128), tL, at("PEN"), 0, 0), (lk, cO, at("KT", 8 * t, 8 * t + 8), 0, 0), (lk, at(y1, 0, 128), G8, 0, 0),
+            (lk, tL, at("GL", 0, 8), 0, 0), (lk, tO, at("GL", 0, 8), 0, 0), (lk, tO, at("GL", 8, 16), 0, 0)])
+        for nm in both:
+            gs = " ".join("G%s%d%d_" % (nm, j, i) + K for j in (0, 1) for i in range(per))
+            ou = [ps(2, i, 256 if nm == "h" else 128, 16) for i in range(16)]
+            r0, r1 = (at("RH", 48, 64), at("RH", 32, 48)) if nm == "h" else (at("RH", 16, 24), at("RH", 0, 8))
+            TM(gs + " " + dk + " RH2", dk, [(ou[i], tl("G" + nm, i, 2048, 16), r0, 0, 0) for i in range(16)])
             for kq in range(0, 16, 4):
-                ms = " ".join("M%s%d_%d_" % (nm, j, kk) + K for j in range(HALVES[nm]) for kk in (kq, kq + 2))
-                l = []
-                for i in range(kq, kq + 4):
-                    ou = at(b2, i, 256 if nm == "h" else 128, 16)
-                    r0, r1 = (at("RH", 48, 64), at("RH", 32, 48)) if nm == "h" else (at("RH", 16, 24), at("RH", 0, 8))
-                    l += [(ou, tl("G" + nm, i, 2048, 16), r0, 0, 0), (ou, tl("M" + nm, 128 * i, 128 * i + 128), r1, 0, nm == "h" and i == 15)]
-                TM(gs + " " + ms + " " + dk + " RH", dk, l, [b2])
-        ac(dk, u("kod"), tl("kod"), at(b2, 129, 256, 2), F.Copy, 64, [b2])
-        ac(dk + " MHALF", u("T1s"), tl("T1s"), at(b2, 0, 128), F.Sign, 128, [b2], bias=at("MHALF"))
-        tt(dk + " " + u("kod"), u("m1"), tl("m1"), tl("kod"), at(b2, 128, 256, 2), A.min, 64, [b2])
-        tt(u("m1"), u("m2"), tl("m2"), tl("m1", 0, 64, 2), tl("m1", 1, 64, 2), A.min, 32, both=True)
-        tt(u("m2"), u("m3"), tl("m3"), tl("m2", 0, 32, 2), tl("m2", 1, 32, 2), A.min, 16, both=True)
-        tt(u("m3"), u("KIm"), tl("KI", 8, 16), tl("m3", 0, 16, 2), tl("m3", 1, 16, 2), A.min, 8)
-        TM(y1 + "z OO" + K + " NN" + K + " Bk G24 K1 ONES", "sm" + K, [
-            (at(b1, 128, 136), at(y1, 0, 128), G8, 1, 0), (at(b1, 128, 136), tO, at("G24", 16, 24), 0, 1),
-            (at(b1, 136, 144), cO, at("K1"), 1, 0), (at(b1, 136, 144), tN, at("G24", 8, 16), 0, 1), (at(b1, 144, 152), tN, at("G24", 0, 8), 1, 1)], [b1])
-        ts("sm" + K, u("KIs"), tl("KI", 0, 8), at(b1, 128, 136), float(t), 0, A.add, None, 8, [b1])
-        ts(u("KIm KIs"), u("KA"), tl("KA"), tl("KI"), 15, 0, A.bitwise_and, None, 16)
-        tt(u("KA") + " sm" + K, u("kk"), tl("kk"), tl("KA"), at(b1, 136, 152), A.mult, 16, [b1])
-        k8 = at(b1, 256, 384, 1, 8)
-        TM(u("kk") + " I", "k8" + K, [(k8, tl("kk", 0, 8), cI, 1, 0), (k8, tl("kk", 8, 16), cI, 0, 1)], [b1])
-        ac("k8" + K, u("k8s"), at("k8s" + K, rows=8), k8, F.Copy, 128, [b1])
-        TM(u("k8s") + " E8", "kF" + K, [(at(b1, 384, 512), at("E8", rows=8), at("k8s" + K, rows=8), 1, 1)], [b1])
-        ts("kF" + K + " KC", u("oh"), tl("oh"), at(b1, 384, 512), at("KC"), 0, A.is_equal, None, 128, [b1])
-        TM(u("T1s") + " I05 KH ONES", "T1F" + K, [(at(b2, 256, 384), tl("T1s"), at("I05"), 1, 0), (at(b2, 256, 384), cO, at("KH"), 0, 1)], [b2])
-        tt(u("heS") + " T1F" + K, u("P1"), tl("P1"), tl("heS"), at(b2, 256, 384), A.mult, 128, [b2])
-        TM(u("e P1") + " I", "es" + K, [(at(b2, 384, 512), cI, tl("e"), 1, 0), (at(b2, 384, 512), cI, tl("P1"), 0, 1)], [b2])
-        cp("es" + K, u("es"), tl("es"), at(b2, 384, 512), 128, [b2])
-        TM(u("es") + " I In", "eD" + K, [(at(b2, 256, 384), cIn, tl("es"), 1, 0), (at(b2, 256, 384, 2), cI, tl("es", 1, 128, 2), 0, 0), (at(b2, 257, 384, 2), cI, tl("es", 0, 128, 2), 0, 1)], [b2])
-        tt("OO" + K + " eD" + K, u("OD"), tl("OD"), tO, at(b2, 256, 384), A.mult, 128, [b2])
-        TM(u("es OD PN") + " I", "Y" + K, [(at(b3, 384, 512), cI, tl("es"), 1, 0), (at(b3, 384, 512), cI, tl("OD"), 0, 0), (at(b3, 384, 512), cI, tl("PN"), 0, 1)], [b3])
-        TM(u("es OD") + " I", "en" + K, [(at(b2, 384, 512), cI, tl("es"), 1, 0), (at(b2, 384, 512), cI, tl("OD"), 0, 1)], [b2])
+                mx = " ".join("M%s%d_%d_" % (nm, j, kk) + K for j in (0, 1) for kk in (kq, kq + 2))
+                TM(mx + " " + dk + " RH2", dk, [(ou[i], tl("M" + nm, 128 * i, 128 * i + 128), r1, 0, nm == both[1] and i == 15) for i in range(kq, kq + 4)])
+        scan(dk + " RSTH", u("pm"), tl("pm"), at("RSTH"), ps(2, 128, 256), A.add, A.min)
+        ts(dk, u("T1"), tl("T1"), ps(2, 0, 128), 0.0, A.is_gt)
+        tt(dk + u(" pm"), u("KI"), tl("KI"), tl("pm", 15, 128, 16), lk, A.min)
+        tt(u("T1 H"), u("PA"), tl("PA"), tl("T1"), ps(1, 0, 128), A.mult)
+        ts(u("KI"), u("KA"), tl("KA"), tl("KI"), 15, A.bitwise_and)
+        tt(u("T1 H"), u("PB"), tl("PB"), tl("T1"), ps(1, 128, 256), A.mult)
+        cp(u("KA"), u("kk"), tl("kk"), tl("KA"))
+        k8 = ps(1, 256, 384, 1, 8)
+        TM(u("kk I!"), u("k8"), [(k8, tl("kk"), cI, 1, 1)])
+        cp(u("k8"), u("k8s"), tl("k8s", rows=8), k8)
+        TM(u("k8s E8!"), u("kF"), [(ps(1, 384, 512), at("E8", rows=8), tl("k8s", rows=8), 1, 1)])
+        ts(u("kF KC!"), u("oh"), tl("oh"), ps(1, 384, 512), at("KC"), A.is_equal)
+        TM(u("PA PB Y I! SW!"), u("Y"), [(ps(3, 384, 512), tl("PA"), cI, 0, 0), (ps(3, 384, 512), tl("PB"), at("SW"), 0, 1)])
+        en = ps(0, 0, 128)
+        TM(u("PA PB e Oe I! SW!"), u("en"), [(en, cI, tl("e"), 1, 0), (en, cI, tl("Oe"), 0, 0), (en, tl("PA"), cI, 0, 0), (en, tl("PB"), at("SW"), 0, 1)])
+        cp(u("en"), y3, at(y3), en)
+        tt(u("oh Y"), u("sel"), tl("sel"), tl("oh"), ps(3, 384, 512), A.mult)
         if not last:
-            cp("en" + K, y2 + "f", at("Y3_%d" % (t + 1) + K), at(b2, 384, 512), 128, [b2])
-        tt(u("oh") + " Y" + K, u("sel"), tl("sel"), tl("oh"), at(b3, 384, 512), A.mult, 128, [b3])
-        if not last:
-            TM(u("sel") + " C", "vl" + K, [(at(b3, 80, 88), Lb(b), tl("sel", b, 128, 16), b == 0, b == 15) for b in range(16)], [b3])
-            cp("vl" + K, y2 + "v", at(y2, 0, 8), at(b3, 80, 88), 8, [b3])
-            send(t, k, 2, " ".join(y2 + s for s in "vpg"), " ".join("X2_%d" % (t + 1) + K + s for s in "vpg"))
-            send(t, k, 3, " ".join(y2 + s for s in "fv"), "X2_%d" % (t + 1) + K + "f")
+            TM(u("sel C!"), u("vl"), [(ps(3, 0, 8), Lb(b), tl("sel", b, 128, 16), b == 0, b == 15) for b in range(16)])
+            cp(u("vl"), y2, at(y2), ps(3, 0, 8))
+            send(t, k, 3, y3, "X3_%d" % (t + 1) + K)
+            send(t, k, 2, y2, "X2_%d" % (t + 1) + K)
         else:
-            c0, c1 = 128 * k, 128 * k + 128
-            c = slice(c0, c1)
-            cp(y1 + "z", "YZ" + K, at("YZ", c0, c1), at(y1, 0, 128), 128)
-            load("Y", "YZ" + K, "oz" + K, lambda T: T.yz[:, c], at("YZ", c0, c1))
-            ac("en" + K, "YF" + K, at("YF", c0, c1), at(b2, 384, 512), F.Copy, 128, [b2])
-            load("Y", "YF" + K, "of" + K, lambda T: T.yf[:, c], at("YF", c0, c1))
-            TM(u("sel") + " Bk", "yv" + K, [(at(b1, 128, 256, 1, 8), G8, tl("sel"), 1, 1)], [b1])
-            ac("yv" + K, "YV" + K, at("YV", c0, c1, 1, 8), at(b1, 128, 256, 1, 8), F.Copy, 128, [b1])
-            load("Y", "YV" + K, "ov" + K, lambda T: T.yv[:, c], at("YV", c0, c1, 1, 8))
-        op("V", u("es so") + " VT VT2 VT3", "VT", lambda g, T, q: q(g.vector.tensor_copy(T.VT[:, 0:2304].indirect(tl("so")(T)), tl("es")(T))), 0.05 + 128 * 3.8 * CYC)
+            c0 = 128 * (1 - k)
+            c1 = c0 + 128
+            ac(y1 + "z", u("YZ"), at("YZ", c0, c1), at(y1, 0, 128), F.Copy)
+            load("Y", u("YZ"), u("oz"), lambda T: T.yz[:, c0:c1], lambda T: ap(T, at("YZ", c0, c1)))
+            ac(u("en"), u("YF"), at("YF", c0, c1), en, F.Copy)
+            load("Y", u("YF"), u("of"), lambda T: T.yf[:, c0:c1], lambda T: ap(T, at("YF", c0, c1)))
+            TM(u("sel Bk!"), u("yv"), [(ps(1, 0, 128, 1, 8), G8, tl("sel"), 1, 1)])
+            ac(u("yv"), u("YV"), at("YV", c0, c1, 1, 8), ps(1, 0, 128, 1, 8), F.Copy)
+            load("Y", u("YV"), u("ov"), lambda T: T.yv[:, c0:c1], lambda T: ap(T, at("YV", c0, c1, 1, 8)))
+        for c in range(7, -1, -1):
+            op("V", y3 + u(" so VT0! VT1! VT2! VT!"), "VT", lambda g, T, q, c=c: q(g.vector.tensor_copy(
+                T.VT[:, 0:2064].indirect(ap(T, tl("so", 2 * c, 2 * c + 1))), ap(T, at(y3, 16 * c, 16 * c + 16)))), 0.05 + 16 * 3.8 * CYC)
 
     for t in range(HOPS):
         for fn, k in ((head, 0), (head, 1), (tail, 0), (tail, 1)):
@@ -409,11 +418,14 @@ def build():
             for o in ops[i0:]:
                 o["tk"] = 2 * t + k
     for j in (0, 1):
-        pj, c0 = "p0%d" % j, 512 * j
-        ts("VT VT2", "yh%d " % j + ("zn0 q0 d00", "yc0 yv0 kF0")[j], at(pj), at("VT", 1024 + c0, 1536 + c0), 2048.0, 0, A.mult, None, 512, [pj])
-        tt("VT VT2 yh%d" % j, "YW%d" % j, at("YW", c0, c0 + 512), at("VT", c0, c0 + 512), at(pj), A.add, 512, [pj])
-        load("Y", "YW%d" % j, "ow%d" % j, lambda T, c0=c0: T.yw[:, c0:c0 + 512], at("YW", c0, c0 + 512))
+        pj, c0 = "p0%d" % (j + 1), 512 * j
+        ts("VT", "yh%d T%s" % (j, pj), at(pj), at("VT", 1040 + c0, 1552 + c0), 2048.0, A.mult)
+        tt("VT yh%d" % j, "YW%d" % j, at("YW", c0, c0 + 512), at("VT", 16 + c0, 528 + c0), at(pj), A.add)
+        load("Y", "YW%d" % j, "ow%d" % j, lambda T, c0=c0: T.yw[:, c0:c0 + 512], lambda T, c0=c0: ap(T, at("YW", c0, c0 + 512)))
     return ops
+
+
+PARTS = ("R", "TH", "Z1", "KS", "KV", "KT", "RH", "RH2", "KU", "KCT", "GL", "VDh", "X1_00c", "X1_01c")
 
 
 def dag(ops):
@@ -426,7 +438,7 @@ def dag(ops):
             p.update(writer.get(k, []))
             readers.setdefault(k, []).append(i)
         for k in o["w"]:
-            if k in ("R", "G24") and not readers.get(k):
+            if k in PARTS and not readers.get(k):
                 writer.setdefault(k, []).append(i)
                 continue
             p.update(writer.get(k, []))
@@ -453,14 +465,17 @@ def plan():
     for o in ops:
         for p in o["p"]:
             succ[p].append(o["i"])
-    lat = 0.08
+
+    def lat(a, b):
+        return 0.0 if ops[a]["e"] == "T" and ops[b]["e"] == "T" else 0.08
     prio = [0.0] * len(ops)
     for o in reversed(ops):
-        prio[o["i"]] = o["c"] + lat + max([prio[s] for s in succ[o["i"]]] + [0.0])
+        prio[o["i"]] = o["c"] + max([prio[s] + lat(o["i"], s) for s in succ[o["i"]]] + [0.0])
     for o in ops:
         if o["tk"] >= 0:
             w = (o["w"] or [o["arg"][0] if o["arg"] else "?"])[0]
-            kind = o["e"] + "".join(ch for ch in w if ch not in "0123456789_")[:5]
+            kind = o["e"] + "".join(ch for ch in w[:-1] if ch != "_")[:3]
+            o["kind"] = kind
             prio[o["i"]] += LEAN.get(kind, 0.0) - (BONUS if o["tk"] % 2 else 0.0)
     left = [len(o["p"]) for o in ops]
     ready = [0.0] * len(ops)
@@ -480,7 +495,7 @@ def plan():
         o["start"] = t0
         order.append(i)
         for s in succ[i]:
-            ready[s] = max(ready[s], t0 + o["c"] + lat)
+            ready[s] = max(ready[s], t0 + o["c"] + lat(i, s))
             left[s] -= 1
             if not left[s]:
                 avail[ops[s]["e"]].append(s)

@@ -5,10 +5,13 @@ N, HOPS, STEP = 4, 4, 3
 FIRST = ("h", "e")
 PIECE = 32
 RELAY = {1: 0, 2: 1, 3: 0}
+ON_SCALAR = (("like", "ks", "k8"), ("k8", "ks"))
+SEND, WAY = 0.9, 3.9
+FARS = ""
+FAR = 4
 MAGIC = 12582912.0
 BIG = 2.0 ** 25
-BONUS = 4.0
-LEAN = {}
+PASSES = 6
 
 SCRATCH = {}
 SEMAPHORES = ["sV", "sS", "sT", "sG", "ls"]
@@ -50,28 +53,30 @@ for _n, _c, _d in (("PX", 2048, B16), ("VT", 2064, I32), ("TH", 2048, F32), ("VW
                    ("KPi", 1, I32), ("YZ", 256, F32), ("YF", 256, F32), ("YV", 256, F32), ("YC", 256, F32), ("YW", 1024, F32)):
     buf(_n, _c, _d)
 for _n, _c, _d in (
-        ("VDh", 512, H16), ("WTa", 1, F32), ("WTb", 1, F32), ("KP", 1, F32), ("PMAG", 1, F32), ("NMAG", 1, F32), ("ONES", 144, B16), ("ZERO", 128, B16),
-        ("I", 128, B16), ("SWI", 128, B16), ("SWn", 128, B16), ("SW", 128, B16), ("Bt", 128, B16), ("Bk", 128, B16), ("B25", 128, B16), ("B32", 128, B16), ("SW32", 128, B16), ("Wa", 128, B16), ("Wb", 128, B16),
-        ("E8", 128, B16), ("CT", 144, B16), ("C", 144, B16), ("C16", 144, B16), ("R", 2048, B16), ("Qi", 16, I32), ("Q", 16, F32), ("Qa", 16, I32),
-        ("KCi", 1, I32), ("KCa", 1, I32), ("KC", 1, F32), ("Z1", 384, B16), ("In", 128, B16), ("I2", 128, B16), ("I2n", 128, B16), ("I05", 128, B16), ("I32", 128, B16),
-        ("I16", 128, B16), ("I25", 128, B16), ("I2048n", 128, B16), ("Forb", 128, B16), ("BROW", 128, B16), ("RSTH", 128, B16), ("KCT", 264, B16),
-        ("PEN", 128, B16), ("RH", 64, B16), ("KQ", 128, B16), ("KU", 128, B16), ("K1", 128, B16), ("KS", 40, B16), ("KV", 40, B16), ("GL", 16, B16), ("KT", 32, B16),
-        ("THi", 128, F32), ("THb", 16, F32)):
+        ("VDh", 512, H16), ("WTa", 1, F32), ("WTb", 1, F32), ("KP", 1, F32), ("PMAG", 1, F32), ("NMAG", 1, F32), ("P845", 1, F32), ("MHALF", 1, F32),
+        ("ONES", 144, B16), ("ZERO", 256, B16), ("I", 128, B16), ("SWI", 128, B16), ("SWn", 128, B16), ("SW", 128, B16), ("Bt", 128, B16), ("Bk", 128, B16),
+        ("QA", 128, B16), ("QB", 128, B16), ("KN", 128, B16), ("SWX", 128, B16), ("Wa", 128, B16), ("Wb", 128, B16), ("E8", 128, B16), ("CT", 144, B16), ("C", 144, B16), ("C16", 144, B16),
+        ("R", 2048, B16), ("RI", 1920, B16), ("Qi", 16, I32), ("Q", 16, F32), ("Qa", 16, I32), ("KCi", 1, I32), ("KCa", 1, I32), ("KC", 1, F32), ("In", 128, B16),
+        ("I2", 128, B16), ("I2n", 128, B16), ("I05", 128, B16), ("SW05", 128, B16), ("I32", 128, B16), ("I16", 128, B16), ("I2048n", 128, B16), ("Forb", 128, B16),
+        ("BROW", 128, B16), ("KL", 1, F32), ("RSTH", 128, B16), ("KCT", 136, B16), ("PEN", 128, B16), ("RH", 24, B16), ("KQ", 128, B16), ("KU", 128, B16), ("K1", 128, B16),
+        ("KS", 64, B16), ("KV", 80, B16), ("GL", 16, B16), ("KT", 32, B16), ("THi", 128, F32), ("THb", 16, F32),
+        ("LO", 512, B16), ("Lst", 512, B16), ("pA", 16, B16), ("pD", 32, B16), ("pP", 32, B16), ("c16", 16, B16), ("v1", 16, F32), ("v16", 16, F32), ("Lv", 16, H16),
+        ("pr", 256, F32), ("w", 16, F32), ("wv", 16, F32), ("so", 32, U16)):
     tile(_n, _c, _d)
 for _k in "01":
     for _n, _c, _d in (
-            ("d0", 128, B16), ("ab", 256, B16), ("LO", 256, B16), ("m", 128, H16), ("uk", 128, F32), ("t1", 128, I32), ("t2", 128, I32), ("hi", 128, I32), ("hu", 128, U16),
-            ("Ld0", 128, B16), ("Oxz", 128, H16), ("zt", 128, F32), ("e", 128, H16), ("eu", 128, U16), ("hme", 128, H16), ("Oe", 128, H16), ("Oh", 128, H16), ("PN", 128, H16),
-            ("Lst", 256, B16), ("v16", 8, F32), ("pA", 8, B16), ("pD", 16, B16), ("pP", 16, B16), ("c16", 8, B16), ("v1", 8, F32), ("Lv", 8, H16), ("pr", 128, F32), ("w", 8, F32), ("wv", 8, F32),
-            ("so", 16, U16), ("Ge", 2048, B16), ("Gh", 2048, B16), ("Me", 2048, B16), ("Mh", 2048, B16), ("T1", 128, B16), ("PA", 128, H16), ("PB", 128, H16),
+            ("Z1", 384, B16), ("BB", 128, B16), ("BX", 128, B16), ("ks", 128, F32), ("Ab", 512, B16), ("d0", 128, B16), ("ab", 256, B16), ("m", 128, H16), ("uk", 128, F32), ("t1", 128, I32), ("t2", 128, I32), ("hi", 128, I32), ("hu", 128, U16),
+            ("Ld0", 128, B16), ("Oxz", 128, H16), ("zt", 128, F32), ("e", 128, H16), ("eu", 128, U16), ("hme", 128, H16), ("OD", 128, H16), ("PN", 128, H16),
+            ("Ge", 2048, B16), ("Gh", 2048, B16), ("Me", 2048, B16), ("Mh", 2048, B16), ("T1", 128, B16), ("PA", 128, H16), ("PB", 128, H16),
             ("pm", 128, F32), ("KI", 8, I32), ("KA", 8, I32), ("kk", 8, B16), ("k8s", 128, B16), ("oh", 128, B16), ("sel", 128, H16)):
         tile(_n + _k, _c, _d)
     for _t in range(HOPS + 1):
         for _x in ("X", "Y"):
             if (_t < HOPS) if _x == "X" else (_t > 0):
-                buf("%s1_%d" % (_x, _t) + _k, 168, B16)
-                buf("%s2_%d" % (_x, _t) + _k, 8, U16)
+                buf("%s1_%d" % (_x, _t) + _k, 128 + 64 * int(_k), B16)
                 buf("%s3_%d" % (_x, _t) + _k, 128, H16)
+                if _k == "0":
+                    buf("%s2_%d" % (_x, _t), 16, U16)
     for _j in range(4):
         buf("p" + _k + str(_j), 512, F32, "psum")
 for _dt in used:
@@ -140,12 +145,13 @@ def build():
     def ac(r, w, o, i, fn, **kw):
         op("S", r, w, lambda g, T, q: q(g.scalar.activation(ap(T, o), ap(T, i), fn, **dict((k, ap(T, x)) for k, x in kw.items()))), vc(width(o)) + 0.03, banks(o, i))
 
-    def TM(r, w, lst):
-        def f(g, T, q):
-            for (o, a, b, s, p) in lst:
-                q(g.tensor.matmul(ap(T, o), ap(T, a), ap(T, b), bool(s), bool(p)))
+    def TM(r, w, lst, piece=8):
         bk = banks(*[x[0] for x in lst])
-        op("T", r, w + "".join(" T" + b for b in bk), f, 0.04 + sum(max(min(64, width(a)), width(b)) for (o, a, b, s, p) in lst) * 0.00042 * 1.25, bk)
+        for a in range(0, len(lst), piece):
+            def f(g, T, q, part=lst[a:a + piece]):
+                for (o, l, m, s, p) in part:
+                    q(g.tensor.matmul(ap(T, o), ap(T, l), ap(T, m), bool(s), bool(p)))
+            op("T", r, w + "".join(" T" + b for b in bk), f, 0.02 + sum(max(min(64, width(l)), width(m)) for (o, l, m, s, p) in lst[a:a + piece]) * 0.00042 * 1.25, bk)
 
     def Lb(b, name="C", rows=None):
         return at(name, 15 - b, 143 - b, 1, rows)
@@ -159,71 +165,86 @@ def build():
         return [((p, r, a + j, b, 2), lhs, (p2, r2, a2 + 1 - j, b2, 2), 0, stop and j) for j in (0, 1)]
 
     cI, cIn, cO, G8 = at("I"), at("In"), at("ONES", 0, 128), at("Bk", 0, 128, 16)
-    users = at("VT", 16, 2064)
+    users = at("VT", 0, 2048)
+    lanes = [(0.5, -1.5) if "like" in on else (1.0, -25.5) for on in ON_SCALAR]
     load("Y", "", "VDv", lambda T: ap(T, at("VD0", 0, 256, 1, 8)), lambda T: T.v0[:, :], 2.0)
     load("S", "", "VDd", lambda T: ap(T, at("VD0", 256, 512, 1, 8)), lambda T: T.d0[:, :], 2.0)
     load("Y", "", "PX", lambda T: T.PX[:, :], lambda T: T.px[:, :], 4.5)
     load("S", "", "WTi", lambda T: T.WTi[:, :], lambda T: T.wt[:, :], 2.2)
-    load("S", "", "Z0", lambda T: T.Z0[:, :], lambda T: T.z0[:, :], 2.3)
+    for k in (0, 1):
+        load("S", "", "X1_0%dz" % k, lambda T, k=k: ap(T, at("X1_0%d" % k, 0, 128)), lambda T, k=k: T.z0[:, 128 - 128 * k:256 - 128 * k], 2.3)
     load("S", "", "KPi", lambda T: T.KPi[:, :], lambda T: T.kap[:, :], 2.4)
     load("S", "", "F0", lambda T: T.F0[:, :], lambda T: T.f0[:, :], 2.8)
     load("Y", "", "VW", lambda T: T.VW[:, :], lambda T: T.vw[:, :], 6.0)
-    for nm, v in (("ONES", 1.0), ("ZERO", 0.0), ("C", 0.0), ("PMAG", MAGIC), ("NMAG", -MAGIC), ("KQ", -1.0 / 512), ("K1", 1.0 / 128)):
+    for nm, v in (("ONES", 1.0), ("C", 0.0), ("PMAG", MAGIC), ("NMAG", -MAGIC), ("KQ", -1.0 / 512), ("K1", 1.0 / 128), ("P845", 84.5)):
         ms(nm, at(nm), v)
-    for nm, parts in (("Z1", ((128, -25.5 / 128), (128, -25.5 * BIG / 128), (128, -57.5 / 4096))), ("KS", ((8, 0.0), (8, 1.0 / 128), (16, 0.0), (8, 1.0 / 128))),
-                      ("KV", ((24, 1.0 / 128), (16, -1.0 / 128))), ("KT", [(8, t / 128.0) for t in range(HOPS)]), ("RH", ((24, 0.0), (40, 0.0)))):
-        c0 = 0
-        for n, v in parts:
-            ms(nm, at(nm, c0, c0 + n), v)
-            c0 += n
     for rows, v in (((0, 32), -1.0 / 64), ((32, 64), 2.0 ** -17), ((64, 128), 0.0)):
         ms("KU", at("KU", rows=rows), v)
-    ms("KCT", at("KCT", 0, 128), -64.0)
-    ms("KCT", at("KCT", 256, 264), 2048.0)
-    ms("VT0", at("VT", 0, 16), 0)
 
-    def aff(src, dst, pat, cmp, base, cm, rows=None):
+    def aff(src, dst, pat, cmp, base, cm, rows=None, fill=0.0):
         n = PLACE[dst][2]
-        G(src, dst, lambda g, T: g.affine_select(ap(T, at(dst, rows=rows)), ap(T, at(src, 0, n, 1, rows)), pat, cmp, 0.0, base, cm), 0.45)
+        G(src, dst, lambda g, T: g.affine_select(ap(T, at(dst, rows=rows)), ap(T, at(src, 0, n, 1, rows)), pat, cmp, fill, base, cm), 0.17 + 2 * n * CYC)
 
-    def iota(dst, pat, base, cm, cost, small=False):
+    def fill(dst, a, b, v):
+        G("ONES", dst, lambda g, T: g.affine_select(ap(T, at(dst, a, b)), ap(T, at("ONES", 0, b - a)), [[0, b - a]], A.is_ge, v, -1, 0), 0.17 + 2 * (b - a) * CYC)
+    odd = [(8, (2 * lanes[k][1] - 1) * BIG / 128) for k in (1, 0)]
+    for nm, parts in (("KS", ((16, 0.0), (16, 1.0 / 128), (32, 0.0))), ("KV", [(48, 1.0 / 128)] + odd + odd), ("KT", [(8, t / 128.0) for t in range(HOPS)]),
+                      ("KN", ((128, -2048.0),)), ("ZERO", ((128, 0.0),))):
+        c0 = 0
+        for n, v in parts:
+            fill(nm, c0, c0 + n, v)
+            c0 += n
+    fill("KCT", 128, 136, 2048.0)
+
+    def iota(dst, pat, base, cm, small=False):
+        cost = 0.13 + 2 * PLACE[dst][2] * CYC
         if small:
             G("", dst, lambda g, T: g.iota(ap(T, at(dst)), pat, base, cm, allow_small_or_imprecise_dtypes=True), cost)
         else:
             G("", dst, lambda g, T: g.iota(ap(T, at(dst)), pat, base, cm), cost)
-    iota("THb", [[19616, 16]], 0, 0, 0.2, True)
-    iota("THi", [[-13824, 128]], 2097152, 0, 0.4, True)
+    iota("THb", [[19616, 16]], 0, 0, True)
+    iota("THi", [[-13824, 128]], 2097152, 0, True)
     aff("ONES", "CT", [[1, 144]], A.is_equal, -15, -16, 8)
     aff("ONES", "Bt", [[-16, 8], [0, 16]], A.is_ge, 0, 1)
     aff("Bt", "Bk", [[16, 8], [0, 16]], A.is_ge, 15, -1)
     aff("ONES", "I", [[-1, 128]], A.is_equal, 0, 1)
-    iota("Qi", [[-1, 16]], 16, 1, 0.2)
-    iota("KCi", [[1, 1]], 0, 1, 0.2)
+    iota("Qi", [[-1, 16]], 16, 1)
+    iota("KCi", [[1, 1]], 0, 1)
     aff("ONES", "SW", [[-2, 64], [1, 2]], A.is_equal, -1, 1)
-    iota("BROW", [[0, 8], [1, 16]], 0, 0, 0.4, True)
+    iota("BROW", [[0, 8], [1, 16]], 0, 0, True)
+    iota("Lst", [[0, 512]], 0, 0, True)
+    G("", "VT0", lambda g, T: g.iota(ap(T, at("VT", 2048, 2064)), [[0, 16]], 0, 0), 0.17)
+    aff("SW", "SWI", [[-1, 128]], A.not_equal, 0, 1, None, -1.0)
+    aff("ZERO", "RSTH", [[0, 8], [1, 16]], A.not_equal, 0, 0, None, 2.0 ** 20)
     aff("ONES", "E8", [[-1, 8], [0, 16]], A.is_equal, 0, 1, 8)
     for j in range(16):
         ac("THi THb", "TH", at("TH", j, 2048, 16), at("THi"), F.Identity, bias=at("THb", j, j + 1))
     cp("Bk C", "C", at("C", 15, 143, 16), G8)
-    ts("C", "C16", at("C16"), at("C"), 1.0 / 16, A.mult)
+    ac("C", "C16", at("C16"), at("C"), F.Copy, scale=1.0 / 16)
     ts("Qi", "Qa", at("Qa"), at("Qi"), 15, A.bitwise_and)
     ts("Qa", "Q", at("Q"), at("Qa"), 0, A.is_equal)
     ts("KCi", "KCa", at("KCa"), at("KCi"), 15, A.bitwise_and)
     cp("KCa", "KC", at("KC"), at("KCa"))
+    ts("KCa", "KL", at("KL"), at("KCa"), 2049.0, A.add, 1.0 / 64, A.mult)
     for b in range(16):
         ts("Bk Q", "R", Rb(b), at("Bk"), at("Q", b, b + 1), A.mult)
-    for nm, src, s in (("In", "I", -1.0), ("I2", "I", 2.0), ("I2n", "I", -2.0), ("I05", "I", 0.5), ("I32", "I", 32.0), ("I16", "I", 16.0), ("I25", "I", BIG),
-                       ("I2048n", "I", -2048.0), ("B25", "Bk", BIG), ("B32", "Bk", 1.0 / 32), ("SW32", "SW", 1.0 / 32), ("PEN", "Bk", 512.0)):
+    for b in range(15):
+        G("R", "RI", lambda g, T, b=b: g.affine_select(ap(T, at("RI", 128 * b, 128 * b + 128)), ap(T, Rb(b)), [[-1, 128]], A.not_equal, -1.0, 0, 1), 0.17 + 256 * CYC)
+    for nm, src, s in (("In", "I", -1.0), ("I2", "I", 2.0), ("I2n", "I", -2.0), ("I05", "I", 0.5), ("I32", "I", 32.0), ("I2048n", "I", -2048.0),
+                       ("BB0", "Bk", lanes[0][0] * BIG), ("BX0", "Bk", lanes[0][0] / 32), ("BB1", "Bk", lanes[1][0] * BIG), ("BX1", "Bk", lanes[1][0] / 32)):
+        ts(src, nm, at(nm), at(src), s, A.mult)
+    for nm, src, s in (("I16", "I", 16.0), ("SWX", "SW", 1.0 / 32 / BIG), ("PEN", "Bk", 16384.0)):
         ac(src, nm, at(nm), at(src), F.Copy, scale=s)
-    tt("SW I", "SWI", at("SWI"), at("SW"), cI, A.subtract)
-    tt("SW In", "SWn", at("SWn"), cIn, at("SW"), A.subtract)
+    aff("In", "SWn", [[-2, 64], [1, 2]], A.not_equal, -1, 1, None, -1.0)
     ts("BROW KC", "Forb", at("Forb"), at("BROW"), at("KC"), A.is_gt, 64.0, A.mult)
-    ts("BROW", "RSTH", at("RSTH"), at("BROW"), 0.0, A.is_equal, 2.0 ** 20, A.mult)
-    ts("BROW", "KCT", at("KCT", 128, 256), at("BROW"), 1.0 / 128, A.mult)
-    for c0, s in ((0, 2.0), (16, -1.0), (32, -2.0), (40, 32.0), (48, 1.0), (56, -16.0)):
-        ts("Bk RH", "RH2", at("RH", c0, c0 + 8), G8, s, A.mult)
+    ac("BROW", "KCT", at("KCT", 0, 128), at("BROW"), F.Copy, scale=1.0 / 128)
+    for c0, s in ((0, -16.0), (8, 32.0), (16, 16.0)):
+        ac("Bk", "RH", at("RH", c0, c0 + 8), G8, F.Copy, scale=s)
+    if FARS:
+        ts("BROW", "QB", at("QB"), at("BROW", 0, 128), FAR - 0.5, A.is_lt, 16.0, A.mult)
+        tt("QB Bk", "QA", at("QA"), at("QB"), at("Bk"), A.mult)
     for c0, s in ((0, -32768.0), (8, 0.5)):
-        ts("Bk", "GL", at("GL", c0, c0 + 8), G8, s, A.mult)
+        ac("Bk", "GL", at("GL", c0, c0 + 8), G8, F.Copy, scale=s)
     cp("WTi", "WTa", at("WTa"), at("WTi"))
     ts("WTi", "WTb", at("WTb"), at("WTi"), 1.0 / 2048, A.mult)
     cp("KPi", "KP", at("KP"), at("KPi"))
@@ -231,123 +252,144 @@ def build():
     ts("Bk WTb", "Wb", at("Wb"), at("Bk"), at("WTb"), A.mult)
     cp("VDv", "VDh", at("VDh", 0, 256, 1, 8), at("VD0", 0, 256, 1, 8))
     cp("VDd", "VDh", at("VDh", 256, 512, 1, 8), at("VD0", 256, 512, 1, 8))
-    TM("VDh CT", "vdL", [(at("p03", 0, 32), Lb(b, "CT", 8), at("VDh", b, 512, 16, 8), b == 0, b == 15) for b in range(16)])
+    TM("VDh CT", "vdL", [(at("p03", 0, 32), Lb(b, "CT", 8), at("VDh", b, 512, 16, 8), b == 0, b == 15) for b in range(16)], 16)
+    cp("vdL", "X2_00 X2_01", at("X2_0"), at("p03", 0, 16))
+    cp("vdL", "X1_0c", at("X1_01", 144, 160), at("p03", 16, 32))
+    ms("X1_0c", at("X1_01", 128, 144), 0.0)
     for k in (0, 1):
-        x1, o = "X1_0%d" % k, 8 * (1 - k)
-        cp("vdL", "X2_0%d" % k, at("X2_0%d" % k), at("p03", o, o + 8))
-        cp("vdL", x1 + "c", at(x1, 136, 144), at("p03", 16 + o, 24 + o))
-        ts("vdL", x1 + "c", at(x1, 160, 168), at("p03", 16 + o, 24 + o), 1.0, A.is_ge)
-        ms("Lst%d" % k, at("Lst%d" % k), 0.0)
-        ms(x1 + "c", at(x1, 128, 136), 0.0)
-        ms(x1 + "c", at(x1, 144, 160), 0.0)
-        cp("Z0", x1 + "z", at(x1, 0, 128), at("Z0", 16 * o, 16 * o + 128))
-        cp("F0", "X3_0%d" % k, at("X3_0%d" % k), at("F0", 16 * o, 16 * o + 128))
-    ts("VW", "VT1", at("VT", 16, 1040), at("VW"), 2047, A.bitwise_and)
-    ts("VW", "VT2", at("VT", 1040, 2064), at("VW"), 11, A.logical_shift_right)
+        o8, o = 8 * (1 - k), 128 * (1 - k)
+        ms("X1_0c", at("X1_01", 160 + o8, 168 + o8), lanes[k][1] * BIG)
+        ts("vdL", "X1_0c", at("X1_01", 176 + o8, 184 + o8), at("p03", 16 + o8, 24 + o8), 1.0, A.is_ge, lanes[k][1] / 32 - 1, A.add)
+        cp("F0", "X3_0%d" % k, at("X3_0%d" % k), at("F0", o, o + 128))
+    for c0 in range(0, 1024, 128):
+        ts("VW", "VT1", at("VT", c0, 128 + c0), at("VW", c0, c0 + 128), 2047, A.bitwise_and)
+        ts("VW", "VT1", at("VT", 1024 + c0, 1152 + c0), at("VW", c0, c0 + 128), 11, A.logical_shift_right)
 
-    def send(t, k, part, rd, wr):
-        x = "%d_%d%d" % (part, t + 1, k)
-        o = op("G", rd, "", None, 1.2, arg=("Y" + x, "X" + x, "x" + x, part))
-        r = op("N", "", wr, None, 5.0 - (0.5 if part == 2 else 0.0))
+    def send(t, k, part, rd, wr, cols=None):
+        x = "%d_%d" % (part, t + 1) + ("" if cols else str(k))
+        cols = cols or (0, None)
+        o = op("G", rd, "", None, SEND, arg=(at("Y" + x, *cols), at("X" + x, *cols), "x%d_%d%d" % (part, t + 1, k), part))
+        r = op("N", "", wr, None, WAY - (0.5 if part == 2 else 0.0))
         r["from"] = o["i"]
 
     def names(t, k):
         K = str(k)
-        return (K, "X1_%d" % t + K, "X2_%d" % t + K, "X3_%d" % t + K, "Y1_%d" % (t + 1) + K, "Y2_%d" % (t + 1) + K, "Y3_%d" % (t + 1) + K,
+        return (K, "X1_%d" % t + K, "X2_%d" % t, "X3_%d" % t + K, "Y1_%d" % (t + 1) + K, "Y2_%d" % (t + 1), "Y3_%d" % (t + 1) + K,
                 lambda s: "".join(" " + (n + K if n[-1] != "!" else n[:-1]) for n in s.split()), lambda n, a=0, b=None, s=1, rows=None: at(n + K, a, b, s, rows),
                 lambda j, a, b, s=1, rows=None: at("p%d%d" % (k, j), a, b, s, rows))
 
     def head(t, k):
         K, x1, x2, x3, y1, y2, y3, u, tl, ps = names(t, k)
-        zX, fX, vX, AX, DX, PX_ = at(x1, 0, 128), at(x3), at(x2), at(x1, 128, 136), at(x1, 136, 144), at(x1, 144, 152)
-        zk, ck = x1 + "z ", x1 + "c "
-        tL, tO, ta, tb = tl("LO", 0, 128), tl("LO", 128, 256), tl("ab", 0, 128), tl("ab", 128, 256)
-        lL, lO, lst = tl("Lst", 0, 128, 16), tl("Lst", 128, 256, 16), tl("Lst", 0, 256, 16)
+        o8, o = 8 * (1 - k), 128 * (1 - k)
+        zX, fX, vX = at(x1, 0, 128), at(x3), at(x2, o8, o8 + 8)
+        zk, vk = x1 + "z ", x2 + K + " "
+        tL, tO, ta, tb = at("LO", o, o + 128), at("LO", 256 + o, 384 + o), tl("ab", 0, 128), tl("ab", 128, 256)
         TM(zk + "Wb KU ONES", u("U"), [(ps(2, 0, 128), at("Wb"), zX, 1, 0), (ps(2, 0, 128), cO, at("KU"), 0, 1)])
         ts(u("U"), u("m"), tl("m"), ps(2, 0, 128), MAGIC, A.add, MAGIC, A.subtract)
         TM(zk + u("m Wa! I2048n!"), u("u"), [(ps(2, 128, 256), at("Wa"), zX, 1, 0), (ps(2, 128, 256), at("I2048n"), tl("m"), 0, 1)])
         ac(u("u KP!"), u("uk"), tl("uk"), ps(2, 128, 256), F.Identity, scale=at("KP"))
-        TM(ck + "R Z1 ONES", u("sc B"), [(ps(1, 0, 384), cO, at("Z1"), 1, 0)] + [(ps(1, b, 384, 16), Rb(b), at(x1, 144, 168), 0, 0) for b in range(16)])
-        pick(x2 + " PX " + zk, u("d0"), tl("d0"), at("PX"), vX, zX, A.subtract)
-        ts(u("d0"), u("a"), ta, tl("d0"), 84.0, A.is_le)
-        ts(u("d0"), u("b"), tb, tl("d0"), -84.0, A.is_ge)
-        pick(x2 + " TH " + u("uk"), u("t1"), tl("t1"), at("TH"), vX, tl("uk"), A.add)
+        pB, pX = ps(1, 0, 128), ps(1, 256, 384)
+        TM("X1_%dc R" % t, u("B"), [(ps(1, b, 384, 16), Rb(b), at("X1_%d1" % t, 160 + o8, 184 + o8), b == 0, 0) for b in range(16)])
+        signs, plain = "like" in ON_SCALAR[k], "x" in ON_SCALAR[k]
+        if plain:
+            op("S", vk + "PX", u("d0"), lambda g, T, q: q(g.scalar.activation(ap(T, tl("d0")), T.PX[:, :].indirect(ap(T, vX)), F.Identity)), 0.08 + 128 * 1.56 * CYC)
+            TM(zk + u("d0 I! In!"), u("D0"), [(ps(0, 0, 128), cIn, zX, 1, 0), (ps(0, 0, 128), cI, tl("d0"), 0, 1)])
+        else:
+            pick(vk + "PX " + zk, u("d0"), tl("d0"), at("PX"), vX, zX, A.subtract)
+        if signs:
+            ac(u("D0" if plain else "d0"), u("a"), ta, ps(0, 0, 128) if plain else tl("d0"), F.Abs)
+            ac(u("a P845!"), u("b"), tb, ta, F.Sign, scale=-1.0, bias=at("P845"))
+        else:
+            ts(u("d0"), u("a"), ta, tl("d0"), 84.0, A.is_le)
+            ts(u("d0"), u("b"), tb, tl("d0"), -84.0, A.is_ge)
+        pick(vk + "TH " + u("uk"), u("t1"), tl("t1"), at("TH"), vX, tl("uk"), A.add)
+        for n, x in ((("b", tb),) if signs else (("a", ta), ("b", tb))):
+            TM(u(n + " B BB BX"), u("B"), [(pB, tl("BB"), x, 0, 0)] + swap(pX, tl("BX"), x))
+        TM(x3 + u("B I32!"), u("B"), [(pB, at("I32"), fX, 0, 1)])
 
         def liked():
-            ts(u("sc"), u("L"), tL, ps(1, 0, 128), 0.0, A.is_ge)
-            tt(u("sc L"), u("O"), tO, tL, ps(1, 256, 384), A.is_lt)
+            ts(u("B"), u("L"), tL, pB, 0.0, A.is_ge)
+            tt(u("B L"), u("O"), tO, tL, pX, A.is_lt)
 
         def second():
-            tt(u("t1 B"), u("t2"), tl("t2"), tl("t1"), ps(1, 128, 256), A.max)
+            tt(u("t1 B"), u("t2"), tl("t2"), tl("t1"), pB, A.max)
             ts(u("t2"), u("hi"), tl("hi"), tl("t2"), 5, A.logical_shift_right, 2047, A.bitwise_and)
             cp(u("hi"), u("hu"), tl("hu"), tl("hi"))
-
-        for n, x in (("a", ta), ("b", tb)):
-            TM(u(n + " sc B Bk! B25! B32!"), u("sc B"), [(ps(1, 128, 256), at("B25"), x, 0, 0), (ps(1, 0, 128), at("Bk"), x, 0, 0)] + swap(ps(1, 256, 384), at("B32"), x))
-        TM(x3 + u("sc B I32!"), u("sc B"), [(ps(1, 128, 256), at("I32"), fX, 0, 1)])
         for step in ((second, liked) if FIRST[k] == "h" else (liked, second)):
             step()
-        TM(u("d0 I!"), u("D0"), [(ps(0, 0, 128), cI, tl("d0"), 1, 1)])
-        TM(zk + u("d0 I! I2! I2n!"), u("xz"), [(ps(0, 384, 512), at("I2n"), zX, 1, 0)] + swap(ps(0, 384, 512), cI, tl("d0")) + swap(ps(0, 384, 512), at("I2"), zX, 1))
+        if not plain:
+            TM(u("d0 I!"), u("D0"), [(ps(0, 0, 128), cI, tl("d0"), 1, 1)])
+        TM(zk + u("d0 I! I2! I2n!"), u("xz"), [(ps(0, 384, 512), at("I2n"), zX, 1, 0)] + swap(ps(0, 384, 512), cI, tl("d0")) + swap(
+            ps(0, 384, 512), cI if plain else at("I2"), zX, 1))
         tt(u("L D0"), u("Ld0"), tl("Ld0"), tL, ps(0, 0, 128), A.mult)
         tt(u("O xz"), u("Oxz"), tl("Oxz"), tO, ps(0, 384, 512), A.mult)
         TM(zk + u("Ld0 I!"), u("q"), [(ps(0, 128, 256), cI, zX, 1, 0), (ps(0, 128, 256), cI, tl("Ld0"), 0, 1)])
-        zr, hf = ps(0, 256, 384), at("I05")
+        zr, hf = ps(2, 256, 384), at("I05")
         TM(zk + u("Ld0 Oxz I! I05! KQ! ONES!"), u("zn"), [(zr, cI, zX, 1, 0), (zr, hf, tl("Ld0"), 0, 0), (zr, hf, tl("Oxz"), 0, 0), (zr, cO, at("KQ"), 0, 1)])
-        ac(u("zn PMAG!"), u("zt"), tl("zt"), zr, F.Identity, bias=at("PMAG"))
-        ac(u("zt NMAG!"), y1 + "z", at(y1, 0, 128), tl("zt"), F.Identity, bias=at("NMAG"))
-        pick(x2 + " VT1 VT2 VT", u("e"), tl("e"), users, vX)
-        cp(u("e"), u("eu"), tl("eu"), tl("e"))
-        TM(u("e I! In!"), u("eP"), [(ps(1, 0, 128), cI, tl("e"), 1, 1), (ps(1, 128, 256), cIn, tl("e"), 1, 0)] + swap(ps(1, 128, 256), cI, tl("e"), 1))
-        TM(u("L O I! In! ONES! K1! ZERO!"), u("oP"), [(ps(1, 256, 384), cI, at("ZERO"), 1, 0)] + swap(ps(1, 256, 384), cI, tO, 1) + [
-            (ps(1, 384, 512), cO, at("K1"), 1, 0), (ps(1, 384, 512), cIn, tL, 0, 0), (ps(1, 384, 512), cIn, tO, 0, 1)])
-        tt(u("hi eP"), u("hme"), tl("hme"), tl("hi"), ps(1, 0, 128), A.subtract)
-        tt(u("O eP"), u("Oe"), tl("Oe"), tO, ps(1, 128, 256), A.mult)
-        tt(u("hme oP"), u("Oh"), tl("Oh"), tl("hme"), ps(1, 256, 384), A.mult)
-        tt(u("hme oP"), u("PN"), tl("PN"), tl("hme"), ps(1, 384, 512), A.mult)
-        TM(u("hme Oh I!"), u("H"), [(ps(1, 0, 128), tl("hme"), cI, 1, 1), (ps(1, 128, 256), tl("Oh"), cI, 1, 1)])
-        TM(u("L O C16!"), u("ll"), [(ps(3, 0, 16), Lb(b, "C16"), tl("LO", b, 256, 16), b == 0, b == 15) for b in range(16)])
-        TM(ck + "KV SWI SWn I I2n ONES", u("val"), [
-            (ps(3, 16, 56), cO, at("KV"), 1, 0), (ps(3, 16, 24), at("SWI"), AX, 0, 0), (ps(3, 24, 32), cI, DX, 0, 0), (ps(3, 32, 40), cI, DX, 0, 0),
-            (ps(3, 40, 48), at("I2n"), PX_, 0, 0), (ps(3, 48, 56), at("SWn"), PX_, 0, 1)])
-        cp(u("ll"), u("Lst"), lst, ps(3, 0, 16))
-        tt(u("Lst val"), u("pA"), tl("pA"), lO, ps(3, 16, 24), A.mult)
-        tt(u("Lst val"), u("pD"), tl("pD"), lst, ps(3, 24, 40), A.mult)
-        dL, dO, pL, pO = tl("pD", 0, 8), tl("pD", 8, 16), tl("pP", 0, 8), tl("pP", 8, 16)
-        if t < HOPS - 1:
-            tt(u("Lst val"), u("pP"), tl("pP"), lst, ps(3, 40, 56), A.mult)
-            mm = [(ps(3, 64, 104), cO, at("KS"), 1, 0), (ps(3, 64, 88), cI, at(x1, 128, 152), 0, 0)]
-            for c0, lhs, srcs in ((64, cI, (lL, tl("pA"))), (72, cIn, (dL, dO)), (80, cI, (pL, pO)), (88, at("I25"), (PX_, pL, pO)), (96, at("SW32"), (PX_, pL, pO)),
-                                  (96, cIn, (lL, lO))):
-                mm += [(ps(3, c0, c0 + 8), lhs, s, 0, s is lO) for s in srcs]
-            TM(ck + u("Lst pA pD pP I! In! I25! SW32! KS! ONES!"), u("nl"), mm)
-            cp(u("nl"), y1 + "c", at(y1, 128, 168), ps(3, 64, 104))
-            send(t, k, 1, y1 + "z " + y1 + "c", " ".join("X1_%d" % (t + 1) + K + s for s in "zc"))
+        if "z" in ON_SCALAR[k]:
+            ac(u("zn PMAG!"), u("zt"), tl("zt"), zr, F.Identity, bias=at("PMAG"))
+            ac(u("zt NMAG!"), y1 + "z", at(y1, 0, 128), tl("zt"), F.Identity, bias=at("NMAG"))
         else:
-            cc, r8, c0 = ps(3, 64, 72), ps(3, 128, 256, 1, 8), 128 * (1 - k)
-            TM(ck + u("Lst pA pD I! In! I16! K1! ONES!"), u("nl"), [(cc, cO, at("K1", 0, 8), 1, 0), (cc, cI, DX, 0, 0), (cc, cIn, dL, 0, 0), (cc, cIn, dO, 0, 0)] + [
-                (cc, at("I16"), s, 0, s is lL) for s in (AX, tl("pA"), lL)])
-            cp(u("nl"), u("c16"), tl("c16"), cc)
-            TM(u("c16 R! Bk! ZERO!"), u("yc"), [(r8, G8, at("ZERO"), 1, 0)] + [(ps(3, 128 + b, 256, 16, 8), Rb(b, 16), tl("c16"), 0, b == 15) for b in range(16)])
-            ac(u("yc"), u("YC"), at("YC", c0, c0 + 128, 1, 8), r8, F.Copy)
-            load("Y", u("YC"), u("oc"), lambda T: T.yc[:, c0:c0 + 128], lambda T: ap(T, at("YC", c0, c0 + 128, 1, 8)))
-        ts(x2, u("v1"), tl("v1"), vX, 1.0, A.add, 1.0 / 64, A.mult)
-        ts(x2, u("v16"), tl("v16"), vX, 16.0, A.add)
-        tt(u("v1 Lst"), u("Lv"), tl("Lv"), tl("v1"), lL, A.mult)
-        mm = [(ps(3, 256, 384), cI, at("Forb"), 1, 0)]
+            ts(u("zn"), y1 + "z", at(y1, 0, 128), zr, MAGIC, A.add, MAGIC, A.subtract)
+        if t < HOPS - 1 and k == 0:
+            send(t, k, 1, y1 + "z", "X1_%d0z" % (t + 1))
+        pick(vk + "VT1 VT", u("e"), tl("e"), users, vX)
+        cp(u("e"), u("eu"), tl("eu"), tl("e"))
+        TM(u("e I!"), u("eP"), [(ps(1, 0, 128), cI, tl("e"), 1, 1)])
+        TM(u("L O In! ONES! K1!"), u("oP"), [(ps(1, 384, 512), cO, at("K1"), 1, 0), (ps(1, 384, 512), cIn, tL, 0, 0), (ps(1, 384, 512), cIn, tO, 0, 1)])
+        tt(u("hi eP"), u("hme"), tl("hme"), tl("hi"), ps(1, 0, 128), A.subtract)
+        tt(u("hme oP"), u("PN"), tl("PN"), tl("hme"), ps(1, 384, 512), A.mult)
+        TM(u("hme I!"), u("H"), [(ps(1, 0, 128), tl("hme"), cI, 1, 1)])
+
+    def joint(t):
+        x1, y1, ck = "X1_%d1" % t, "Y1_%d1" % (t + 1), "X1_%dc " % t
+        AX, DX, PX_ = at(x1, 128, 144), at(x1, 144, 160), at(x1, 160, 176)
+        lL, lO, lst = at("Lst", 0, 256, 16), at("Lst", 256, 512, 16), at("Lst", 0, 512, 16)
+
+        def ps(a, b, s=1, rows=None):
+            return at("p03", a, b, s, rows)
+        TM("L0 O0 L1 O1 C16", "ll", [(ps(0, 32), Lb(b, "C16"), at("LO", b, 512, 16), b == 0, b == 15) for b in range(16)])
+        TM(ck + "KV SWI SWn I I2n ONES", "val", [
+            (ps(32, 112), cO, at("KV"), 1, 0), (ps(32, 48), at("SWI"), AX, 0, 0), (ps(48, 64), cI, DX, 0, 0), (ps(64, 80), cI, DX, 0, 0),
+            (ps(80, 96), at("I2n"), PX_, 0, 0), (ps(96, 112), at("SWn"), PX_, 0, 1)])
+        cp("ll", "Lst", lst, ps(0, 32))
+        tt("Lst val", "pA", at("pA"), lO, ps(32, 48), A.mult)
+        tt("Lst val", "pD", at("pD"), lst, ps(48, 80), A.mult)
+        dL, dO, pL, pO = at("pD", 0, 16), at("pD", 16, 32), at("pP", 0, 16), at("pP", 16, 32)
+        if t < HOPS - 1:
+            tt("Lst val", "pP", at("pP"), lst, ps(80, 112), A.mult)
+            mm = [(ps(112, 176), cO, at("KS"), 1, 0), (ps(112, 160), cI, at(x1, 128, 176), 0, 0)]
+            for c0, lhs, srcs in ((112, cI, (lL, at("pA"))), (128, cIn, (dL, dO)), (144, cI, (pL, pO)), (160, at("SWX"), (PX_, pL, pO)), (160, cIn, (lL, lO))):
+                mm += [(ps(c0, c0 + 16), lhs, s, 0, s is lO) for s in srcs]
+            TM(ck + "Lst pA pD pP I In SWX KS ONES", "nl", mm)
+            cp("nl", y1 + "c", at(y1, 128, 192), ps(112, 176))
+            send(t, 1, 1, y1 + "z " + y1 + "c", "X1_%d1z X1_%dc" % (t + 1, t + 1))
+        else:
+            cc, r8 = ps(112, 128), ps(0, 256, 1, 8)
+            TM(ck + "Lst pA pD I In I16 K1 ONES", "nl", [(cc, cO, at("K1", 0, 16), 1, 0), (cc, cI, DX, 0, 0), (cc, cIn, dL, 0, 0), (cc, cIn, dO, 0, 0)] + [
+                (cc, at("I16"), s, 0, s is lL) for s in (AX, at("pA"), lL)])
+            cp("nl", "c16", at("c16"), cc)
+        vk = "X2_%d0 X2_%d1" % (t, t)
+        ts(vk, "v1", at("v1"), at("X2_%d" % t), 1.0, A.add, 1.0 / 64, A.mult)
+        tt("v1 Lst", "Lv", at("Lv"), at("v1"), lL, A.mult)
+        mm = [(ps(256, 384), cI, at("Forb"), 1, 0), (ps(384, 512), cI, at("Forb"), 0, 0)]
         for j in range(1, 16):
-            mm += [(ps(3, 256 + j, 384, 16), Rb(j - 1), tl("Lv"), 0, 0), (ps(3, 256 + j, 384, 16), cIn, tl("Lv"), 0, j == 15)]
-        TM(u("Lv I! In! Forb! R!"), u("dg"), mm)
-        scan(u("dg Lst"), u("pr"), tl("pr"), ps(3, 256, 384), tl("Lst", 0, 128), A.mult, A.add)
-        ts(u("pr"), u("w"), tl("w"), tl("pr", 15, 128, 16), 0.0, A.not_equal)
-        tt(u("w v16"), u("wv"), tl("wv"), tl("w"), tl("v16"), A.mult)
-        ts(u("wv KC!"), u("so"), tl("so", 0, 16, 2), tl("wv"), at("KC"), A.max)
-        TM(u("e Oe PN I!"), u("Y"), [(ps(3, 384, 512), cI, tl(n), n == "e", 0) for n in ("e", "Oe", "PN")])
+            mm += [(ps(256 + j, 512, 16), at("RI", 128 * j - 128, 128 * j), at("Lv"), 0, j == 15)]
+        TM("Lv I Forb RI", "dg", mm)
+        scan("dg Lst", "pr", at("pr"), ps(256, 512), at("Lst", 0, 256), A.mult, A.add)
+        ts("pr KL", "w", at("w"), at("pr", 15, 256, 16), 0.0, A.is_equal, at("KL"), A.mult)
+        tt("w v1", "wv", at("wv"), at("w"), at("v1"), A.max)
+        ts("wv", "so", at("so", 0, 32, 2), at("wv"), 64.0, A.mult, -1.0, A.add)
+        if t == HOPS - 1:
+            TM("c16 R", "yc", [(ps(b, 256, 16, 8), Rb(b, 16), at("c16"), b == 0, b == 15) for b in range(16)])
+            ac("yc", "YC", at("YC", rows=8), r8, F.Copy)
+            load("Y", "YC", "oc", lambda T: T.yc[:, :], lambda T: ap(T, at("YC", rows=8)))
 
     def tail(t, k):
         K, x1, x2, x3, y1, y2, y3, u, tl, ps = names(t, k)
         last = t == HOPS - 1
-        tL, tO = tl("LO", 0, 128), tl("LO", 128, 256)
+        o8, o = 8 * (1 - k), 128 * (1 - k)
+        tL, tO = at("LO", o, o + 128), at("LO", 256 + o, 384 + o)
         both = (FIRST[k], "h" if FIRST[k] == "e" else "e")
         per = 64 // PIECE
         for nm in both:
@@ -357,75 +399,116 @@ def build():
                     c0 = 64 * j + PIECE * i
                     op("S", u(nm + "u PX!"), gi, lambda g, T, q, nm=nm, c0=c0: q(g.scalar.activation(ap(T, tl("G" + nm, 16 * c0, 16 * (c0 + PIECE))),
                        T.PX[:, :].indirect(ap(T, tl(nm + "u", c0, c0 + PIECE))), F.Identity)), 0.08 + 16 * PIECE * 1.56 * CYC)
-                for kq in range(0, 16, 2):
-                    def f(g, T, q, nm=nm, j=j, kq=kq):
-                        for i in (kq, kq + 1):
-                            q(g.vector.tensor_tensor(ap(T, tl("M" + nm, i * 128 + 64 * j, i * 128 + 64 * (j + 1))), ap(T, tl("G" + nm, 1024 * j + i, 1024 * (j + 1), 16)),
-                                                     ap(T, ps(0, 128 + 64 * j, 192 + 64 * j)), A.max))
-                    op("V", gk + u(" q"), "M%s%d_%d_" % (nm, j, kq) + K, f, 2 * vc(64), ["p%d0" % k])
-        dk, lk = u("dist"), ps(2, 256, 264)
-        TM(y1 + "z " + u("L O KCT! KT! PEN! GL! ONES! Bk!"), dk, [
-            (ps(2, 0, 264), cO, at("KCT"), 1, 0), (ps(2, 0, 128), tL, at("PEN"), 0, 0), (lk, cO, at("KT", 8 * t, 8 * t + 8), 0, 0), (lk, at(y1, 0, 128), G8, 0, 0),
-            (lk, tL, at("GL", 0, 8), 0, 0), (lk, tO, at("GL", 0, 8), 0, 0), (lk, tO, at("GL", 8, 16), 0, 0)])
-        for nm in both:
+                for i in range(FAR if nm + K in FARS else 0, 16):
+                    tt(gk + u("q"), "M%s%d_%d_" % (nm, j, i) + K, tl("M" + nm, i * 128 + 64 * j, i * 128 + 64 * (j + 1)), tl("G" + nm, 1024 * j + i, 1024 * (j + 1), 16),
+                       ps(0, 128 + 64 * j, 192 + 64 * j), A.max)
+        pd, lk = {"h": ps(2, 0, 128), "e": ps(1, 256, 384)}, ps(2, 128, 136)
+
+        def distances(nm):
+            dk, far = u("d" + nm), FAR if nm + K in FARS else 0
+            if nm == "h":
+                TM("KCT ONES", dk, [(ps(2, 0, 136), cO, at("KCT"), 1, 0)])
+                TM(y1 + "z " + u("L O KT! GL! ONES! Bk!"), dk, [
+                    (lk, cO, at("KT", 8 * t, 8 * t + 8), 0, 0), (lk, at(y1, 0, 128), G8, 0, 0), (lk, tL, at("GL", 0, 8), 0, 0), (lk, tO, at("GL", 0, 8), 0, 0),
+                    (lk, tO, at("GL", 8, 16), 0, 0)])
+            else:
+                TM(u("L KN! PEN! ONES!"), dk, [(pd[nm], cO, at("KN"), 1, 0), (pd[nm], tL, at("PEN"), 0, 0)])
             gs = " ".join("G%s%d%d_" % (nm, j, i) + K for j in (0, 1) for i in range(per))
-            ou = [ps(2, i, 256 if nm == "h" else 128, 16) for i in range(16)]
-            r0, r1 = (at("RH", 48, 64), at("RH", 32, 48)) if nm == "h" else (at("RH", 16, 24), at("RH", 0, 8))
-            TM(gs + " " + dk + " RH2", dk, [(ou[i], tl("G" + nm, i, 2048, 16), r0, 0, 0) for i in range(16)])
-            for kq in range(0, 16, 4):
-                mx = " ".join("M%s%d_%d_" % (nm, j, kk) + K for j in (0, 1) for kk in (kq, kq + 2))
-                TM(mx + " " + dk + " RH2", dk, [(ou[i], tl("M" + nm, 128 * i, 128 * i + 128), r1, 0, nm == both[1] and i == 15) for i in range(kq, kq + 4)])
-        scan(dk + " RSTH", u("pm"), tl("pm"), at("RSTH"), ps(2, 128, 256), A.add, A.min)
-        ts(dk, u("T1"), tl("T1"), ps(2, 0, 128), 0.0, A.is_gt)
-        tt(dk + u(" pm"), u("KI"), tl("KI"), tl("pm", 15, 128, 16), lk, A.min)
-        tt(u("T1 H"), u("PA"), tl("PA"), tl("T1"), ps(1, 0, 128), A.mult)
-        ts(u("KI"), u("KA"), tl("KA"), tl("KI"), 15, A.bitwise_and)
-        tt(u("T1 H"), u("PB"), tl("PB"), tl("T1"), ps(1, 128, 256), A.mult)
-        cp(u("KA"), u("kk"), tl("kk"), tl("KA"))
-        k8 = ps(1, 256, 384, 1, 8)
-        TM(u("kk I!"), u("k8"), [(k8, tl("kk"), cI, 1, 1)])
-        cp(u("k8"), u("k8s"), tl("k8s", rows=8), k8)
-        TM(u("k8s E8!"), u("kF"), [(ps(1, 384, 512), at("E8", rows=8), tl("k8s", rows=8), 1, 1)])
-        ts(u("kF KC!"), u("oh"), tl("oh"), ps(1, 384, 512), at("KC"), A.is_equal)
-        TM(u("PA PB Y I! SW!"), u("Y"), [(ps(3, 384, 512), tl("PA"), cI, 0, 0), (ps(3, 384, 512), tl("PB"), at("SW"), 0, 1)])
-        en = ps(0, 0, 128)
-        TM(u("PA PB e Oe I! SW!"), u("en"), [(en, cI, tl("e"), 1, 0), (en, cI, tl("Oe"), 0, 0), (en, tl("PA"), cI, 0, 0), (en, tl("PB"), at("SW"), 0, 1)])
-        cp(u("en"), y3, at(y3), en)
-        tt(u("oh Y"), u("sel"), tl("sel"), tl("oh"), ps(3, 384, 512), A.mult)
-        if not last:
-            TM(u("sel C!"), u("vl"), [(ps(3, 0, 8), Lb(b), tl("sel", b, 128, 16), b == 0, b == 15) for b in range(16)])
-            cp(u("vl"), y2, at(y2), ps(3, 0, 8))
-            send(t, k, 3, y3, "X3_%d" % (t + 1) + K)
-            send(t, k, 2, y2, "X2_%d" % (t + 1) + K)
+            p, r, a, b, s = pd[nm]
+            ou = [(p, r, a + i, b, 16) for i in range(16)]
+            if far:
+                TM(x1 + "z QA" + u("Ld0"), dk, [(pd[nm], at(x1, 0, 128), at("QA"), 0, 0), (pd[nm], tl("Ld0"), at("QA"), 0, 0)])
+                mm = []
+                for i in range(far):
+                    df = at("p13", 128 * i, 128 * i + 128)
+                    mm += [(df, cIn, at(x1, 0, 128), 1, 0), (df, cIn, tl("Ld0"), 0, 0), (df, cI, tl("G" + nm, i, 2048, 16), 0, 1)]
+                TM(gs + " I In " + x1 + "z" + u("Ld0"), "df", mm, 6)
+                ac("df", u("Ab"), tl("Ab", 0, 128 * far), at("p13", 0, 128 * far), F.Abs)
+            TM(gs + dk + " RH", dk, [(ou[i], tl("G" + nm, i, 2048, 16), at("RH", 0, 8), 0, 0) for i in range(far, 16)])
+            for kq in range(far, 16, 4):
+                mx = " ".join("M%s%d_%d_" % (nm, j, kk) + K for j in (0, 1) for kk in range(kq, min(16, kq + 4)))
+                TM(mx + dk + " RH", dk, [(ou[i], tl("M" + nm, 128 * i, 128 * i + 128), at("RH", 8, 16), 0, i == 15 and not far) for i in range(kq, min(16, kq + 4))])
+            if far:
+                TM(u("Ab RH!") + dk, dk, [(ou[i], tl("Ab", 128 * i, 128 * i + 128), at("RH", 16, 24), 0, i == far - 1) for i in range(far)])
+            if nm == both[0]:
+                if "ks" in ON_SCALAR[k]:
+                    ac(dk, u("ks"), tl("ks"), pd[nm], F.Copy)
+                else:
+                    cp(dk, u("ks"), tl("ks"), pd[nm])
+
+        def place():
+            scan(u("dh RSTH!"), u("pm"), tl("pm"), at("RSTH"), pd["h"], A.add, A.min)
+            tt(u("dh pm"), u("KI"), tl("KI"), tl("pm", 15, 128, 16), lk, A.min)
+            if both[1] == "h":
+                nearer()
+            ts(u("KI"), u("KA"), tl("KA"), tl("KI"), 15, A.bitwise_and)
+            cp(u("KA"), u("kk"), tl("kk"), tl("KA"))
+            k8 = ps(2, 384, 512, 1, 8)
+            TM(u("kk I!"), u("k8"), [(k8, tl("kk"), cI, 1, 1)])
+            if "k8" in ON_SCALAR[k]:
+                ac(u("k8"), u("k8s"), tl("k8s", rows=8), k8, F.Copy)
+            else:
+                cp(u("k8"), u("k8s"), tl("k8s", rows=8), k8)
+            TM(u("k8s E8!"), u("kF"), [(ps(2, 256, 384), at("E8", rows=8), tl("k8s", rows=8), 1, 1)])
+            ts(u("kF KC!"), u("oh"), tl("oh"), ps(2, 256, 384), at("KC"), A.is_equal)
+
+        def nearer():
+            tt(u("ks d" + both[1]), u("T1"), tl("T1"), tl("ks"), pd[both[1]], A.is_lt if both[1] == "e" else A.is_gt)
+            tt(u("T1 H"), u("PA"), tl("PA"), tl("T1"), ps(1, 0, 128), A.mult)
+            TM(u("e I! In!"), u("eD"), [(ps(0, 384, 512), cIn, tl("e"), 1, 0)] + swap(ps(0, 384, 512), cI, tl("e")))
+            TM(u("PA eD SWI!"), u("eD"), [(ps(0, 384, 512), tl("PA"), at("SWI"), 0, 1)])
+            tt(u("O eD"), u("OD"), tl("OD"), tO, ps(0, 384, 512), A.mult)
+
+        def view(nm, ou, parts):
+            TM(u(" ".join(parts) + " I!"), u(nm), [(ou, cI, tl(n), n == "e", 0) for n in parts])
+            TM(u("PA I! " + nm), u(nm), [(ou, tl("PA"), cI, 0, 0)])
+            TM(u("OD I! " + nm), u(nm), [(ou, cI, tl("OD"), 0, 1)])
+        en, pY = ps(1, 128, 256), ps(2, 0, 128) if both[0] == "h" else at("p13", 0, 128)
+        distances(both[0])
+        if both[0] == "h":
+            place()
+        distances(both[1])
+        if both[0] == "h":
+            nearer()
         else:
-            c0 = 128 * (1 - k)
-            c1 = c0 + 128
+            place()
+        view("Y", pY, ("e", "PN"))
+        view("en", en, ("e",))
+        cp(u("en"), y3, at(y3), en)
+        tt(u("oh Y"), u("sel"), tl("sel"), tl("oh"), pY, A.mult)
+        if not last:
+            TM(u("sel C!"), u("vl"), [(ps(1, 256, 264), Lb(b), tl("sel", b, 128, 16), b == 0, b == 15) for b in range(16)], 16)
+            cp(u("vl"), y2 + K, at(y2, o8, o8 + 8), ps(1, 256, 264))
+            send(t, k, 3, y3, "X3_%d" % (t + 1) + K)
+            send(t, k, 2, y2 + K, "X2_%d" % (t + 1) + K, (o8, o8 + 8))
+        else:
+            c0, c1 = o, o + 128
             ac(y1 + "z", u("YZ"), at("YZ", c0, c1), at(y1, 0, 128), F.Copy)
             load("Y", u("YZ"), u("oz"), lambda T: T.yz[:, c0:c1], lambda T: ap(T, at("YZ", c0, c1)))
             ac(u("en"), u("YF"), at("YF", c0, c1), en, F.Copy)
             load("Y", u("YF"), u("of"), lambda T: T.yf[:, c0:c1], lambda T: ap(T, at("YF", c0, c1)))
-            TM(u("sel Bk!"), u("yv"), [(ps(1, 0, 128, 1, 8), G8, tl("sel"), 1, 1)])
-            ac(u("yv"), u("YV"), at("YV", c0, c1, 1, 8), ps(1, 0, 128, 1, 8), F.Copy)
+            TM(u("sel Bk!"), u("yv"), [(ps(1, 256, 384, 1, 8), G8, tl("sel"), 1, 1)])
+            ac(u("yv"), u("YV"), at("YV", c0, c1, 1, 8), ps(1, 256, 384, 1, 8), F.Copy)
             load("Y", u("YV"), u("ov"), lambda T: T.yv[:, c0:c1], lambda T: ap(T, at("YV", c0, c1, 1, 8)))
         for c in range(7, -1, -1):
-            op("V", y3 + u(" so VT0! VT1! VT2! VT!"), "VT", lambda g, T, q, c=c: q(g.vector.tensor_copy(
-                T.VT[:, 0:2064].indirect(ap(T, tl("so", 2 * c, 2 * c + 1))), ap(T, at(y3, 16 * c, 16 * c + 16)))), 0.05 + 16 * 3.8 * CYC)
+            op("V", y3 + " so VT0 VT1 VT", "VT", lambda g, T, q, c=c: q(g.vector.tensor_copy(
+                T.VT[:, 0:2064].indirect(ap(T, at("so", 2 * (o8 + c), 2 * (o8 + c) + 1))), ap(T, at(y3, 16 * c, 16 * c + 16)))), 0.05 + 16 * 3.8 * CYC)
 
     for t in range(HOPS):
-        for fn, k in ((head, 0), (head, 1), (tail, 0), (tail, 1)):
+        for fn, k in ((head, 0), (head, 1), (lambda t, k: joint(t), 1), (tail, 0), (tail, 1)):
             i0 = len(ops)
             fn(t, k)
             for o in ops[i0:]:
                 o["tk"] = 2 * t + k
-    for j in (0, 1):
-        pj, c0 = "p0%d" % (j + 1), 512 * j
-        ts("VT", "yh%d T%s" % (j, pj), at(pj), at("VT", 1040 + c0, 1552 + c0), 2048.0, A.mult)
-        tt("VT yh%d" % j, "YW%d" % j, at("YW", c0, c0 + 512), at("VT", 16 + c0, 528 + c0), at(pj), A.add)
-        load("Y", "YW%d" % j, "ow%d" % j, lambda T, c0=c0: T.yw[:, c0:c0 + 512], lambda T, c0=c0: ap(T, at("YW", c0, c0 + 512)))
+    for j in range(4):
+        pj, c0 = "p%d%d" % (j % 2, 1 + j // 2), 256 * j
+        ts("VT", "yh%d T%s" % (j, pj), at(pj, 0, 256), at("VT", 1024 + c0, 1280 + c0), 2048.0, A.mult)
+        tt("VT yh%d" % j, "YW%d" % j, at("YW", c0, c0 + 256), at("VT", c0, 256 + c0), at(pj, 0, 256), A.add)
+        load("YS"[j % 2], "YW%d" % j, "ow%d" % j, lambda T, c0=c0: T.yw[:, c0:c0 + 256], lambda T, c0=c0: ap(T, at("YW", c0, c0 + 256)))
     return ops
 
 
-PARTS = ("R", "TH", "Z1", "KS", "KV", "KT", "RH", "RH2", "KU", "KCT", "GL", "VDh", "X1_00c", "X1_01c")
+PARTS = ("R", "RI", "TH", "Z10", "Z11", "KS", "KV", "KT", "RH", "KU", "KCT", "GL", "VDh", "X1_0c", "VT1")
 
 
 def dag(ops):
@@ -461,45 +544,57 @@ def dag(ops):
 
 def plan():
     ops = dag(build())
+    n = len(ops)
+    eng = [o["e"] for o in ops]
+    cost = [o["c"] for o in ops]
+    hold = [0.0 if o["e"] == "N" else 0.1 if o["sem"] else o["c"] for o in ops]
     succ = [[] for _ in ops]
+    left0 = [len(o["p"]) for o in ops]
     for o in ops:
         for p in o["p"]:
-            succ[p].append(o["i"])
+            succ[p].append((o["i"], 0.0 if eng[p] == "T" and o["e"] == "T" else 0.08))
+    chain = [o["i"] for o in ops if o["e"] == "S" and o["w"][0][:2] in ("Ge", "Gh")]
+    for a, b in zip(chain, chain[1:]):
+        succ[a].append((b, 0.0))
+        left0[b] += 1
 
-    def lat(a, b):
-        return 0.0 if ops[a]["e"] == "T" and ops[b]["e"] == "T" else 0.08
-    prio = [0.0] * len(ops)
-    for o in reversed(ops):
-        prio[o["i"]] = o["c"] + max([prio[s] + lat(o["i"], s) for s in succ[o["i"]]] + [0.0])
+    def run(prio, soon):
+        left, ready, st, order = list(left0), [0.0] * n, [0.0] * n, []
+        free = dict((e, 0.0) for e in "VSTGYN")
+        avail = dict((e, [i for i in range(n) if eng[i] == e and not left[i]]) for e in free)
+        while len(order) < n:
+            t0, e = min((max(free[e], min(ready[i] for i in avail[e])), e) for e in avail if avail[e])
+            i = max((j for j in avail[e] if ready[j] <= t0 + soon + 1e-9), key=lambda j: (prio[j], -j))
+            avail[e].remove(i)
+            st[i] = max(t0, ready[i])
+            free[e] = st[i] + hold[i]
+            order.append(i)
+            for s, lat in succ[i]:
+                ready[s] = max(ready[s], st[i] + cost[i] + lat)
+                left[s] -= 1
+                if not left[s]:
+                    avail[eng[s]].append(s)
+        return max(st[i] + cost[i] for i in range(n)), st, order
+
+    def ways(order, queues):
+        way, own, after = [0.0] * n, [0.0] * n, {}
+        for i in reversed(order):
+            own[i] = way[i] = cost[i] + max([way[s] + lat for s, lat in succ[i]] + [0.0])
+            if queues and hold[i]:
+                way[i] = max(way[i], hold[i] + after.get(eng[i], 0.0))
+                after[eng[i]] = way[i]
+        return own
+    best = None
+    for soon in (0.0, 0.03, 0.06):
+        prio = ways(range(n), False)
+        for _ in range(PASSES):
+            got = run(prio, soon)
+            if best is None or got[0] < best[0]:
+                best = got
+            prio = [(a + b) / 2 for a, b in zip(prio, ways(got[2], True))]
     for o in ops:
-        if o["tk"] >= 0:
-            w = (o["w"] or [o["arg"][0] if o["arg"] else "?"])[0]
-            kind = o["e"] + "".join(ch for ch in w[:-1] if ch != "_")[:3]
-            o["kind"] = kind
-            prio[o["i"]] += LEAN.get(kind, 0.0) - (BONUS if o["tk"] % 2 else 0.0)
-    left = [len(o["p"]) for o in ops]
-    ready = [0.0] * len(ops)
-    free = dict((e, 0.0) for e in "VSTGYN")
-    avail = dict((e, []) for e in "VSTGYN")
-    for o in ops:
-        if not left[o["i"]]:
-            avail[o["e"]].append(o["i"])
-    order = []
-    while len(order) < len(ops):
-        t0, e = min((min(max(free[e], ready[i]) for i in avail[e]), e) for e in avail if avail[e])
-        i = max((j for j in avail[e] if max(free[e], ready[j]) <= t0 + 1e-9), key=lambda j: (prio[j], -j))
-        o = ops[i]
-        avail[e].remove(i)
-        if e != "N":
-            free[e] = t0 + (0.1 if o["sem"] else o["c"])
-        o["start"] = t0
-        order.append(i)
-        for s in succ[i]:
-            ready[s] = max(ready[s], t0 + o["c"] + lat(i, s))
-            left[s] -= 1
-            if not left[s]:
-                avail[ops[s]["e"]].append(s)
-    return ops, order
+        o["start"] = best[1][o["i"]]
+    return ops, best[2]
 
 
 PLAN = {}
@@ -517,7 +612,7 @@ def relay_program(g, core, T, topo, which, src, dst):
     for a, x, s, part in [ops[i]["arg"] for i in order if ops[i]["arg"]]:
         if RELAY[part] == which:
             g.wait_ge(T.sem[s], len(topo.engines(src, core)))
-            g.remote_dma(T[x][:, :], T[x][:, :], T.sem[s], T.sem.ls, pid, rid, topo.mask(core, dst))
+            g.remote_dma(ap(T, x), ap(T, x), T.sem[s], T.sem.ls, pid, rid, topo.mask(core, dst))
             sent += len(topo.engines(core, dst))
     g.wait_ge(T.sem.ls, sent)
 
@@ -565,7 +660,7 @@ def rank_program(g, core, T, topo):
             a, b, s, part = o["arg"]
             r = rl[RELAY[part]]
             rid, pid = topo.addr(r, core)
-            g.remote_dma(T[b][:, :], T[a][:, :], T.sem[s], T.sem.ls, pid, rid, topo.mask(core, r))
+            g.remote_dma(ap(T, b), ap(T, a), T.sem[s], T.sem.ls, pid, rid, topo.mask(core, r))
             sent += len(topo.engines(core, r))
         elif o["sem"]:
             o["f"](g, T, lambda x, s=o["sem"]: x.then_inc(T.sem[s], 16))

from concourse.mybir import AluOpType, ActivationFunctionType
A = AluOpType
F = ActivationFunctionType
N, HOPS, STEP = 4, 4, 3
FIRST = ("h", "e")
PIECE = 32
RELAY = {1: 0, 2: 1, 3: 0}
ON_SCALAR = (("like", "ks", "k8"), ("k8", "ks"))
SEND, WAY = 0.9, 3.9
FARS = ""
FAR = 4
MAGIC = 12582912.0
BIG = 2.0 ** 25
PASSES = 6

SCRATCH = {}
SEMAPHORES = ["sV", "sS", "sT", "sG", "ls"]
B16, H16, F32, I32, U16 = "bfloat16", "float16", "float32", "int32", "uint16"
POOL = {B16: "pB", H16: "pH", F32: "pF", I32: "pI", U16: "pU"}
PLACE = {}
used = {}


def buf(name, cols, dtype, where="sbuf"):
    SCRATCH[name] = (where, [128, cols], dtype)
    PLACE[name] = (name, 0, cols)


def tile(name, cols, dtype):
    o = used.get(dtype, 0)
    PLACE[name] = (POOL[dtype], o, cols)
    used[dtype] = o + -(-cols // 32) * 32


def at(name, a=0, b=None, s=1, rows=None):
    p, o, n = PLACE[name]
    r = (0, 128) if rows is None else rows if isinstance(rows, tuple) else (0, rows)
    return (p, r, o + a, o + (n if b is None else b), s)


def ap(T, x):
    if not isinstance(x, tuple):
        return x
    p, r, a, b, s = x
    return T[p][r[0]:r[1], a:b] if s == 1 else T[p][r[0]:r[1], a:b:s]


def width(x):
    return len(range(x[2], x[3], x[4]))


for _n, _c, _d in (("PX", 2048, B16), ("VT", 2064, I32), ("TH", 2048, F32), ("VW", 1024, I32), ("Z0", 256, B16), ("F0", 256, I32), ("VD0", 512, I32), ("WTi", 1, I32),
                   ("KPi", 1, I32), ("YZ", 256, F32), ("YF", 256, F32), ("YV", 256, F32), ("YC", 256, F32), ("YW", 1024, F32)):
    buf(_n, _c, _d)
for _n, _c, _d in (
        ("VDh", 512, H16), ("WTa", 1, F32), ("WTb", 1, F32), ("KP", 1, F32), ("PMAG", 1, F32), ("NMAG", 1, F32), ("P845", 1, F32), ("MHALF", 1, F32),
        ("ONES", 144, B16), ("ZERO", 256, B16), ("I", 128, B16), ("SWI", 128, B16), ("SWn", 128, B16), ("SW", 128, B16), ("Bt", 128, B16), ("Bk", 128, B16),
        ("QA", 128, B16), ("QB", 128, B16), ("KN", 128, B16), ("SWX", 128, B16), ("Wa", 128, B16), ("Wb", 128, B16), ("E8", 128, B16), ("CT", 144, B16), ("C", 144, B16), ("C16", 144, B16),
        ("R", 2048, B16), ("RI", 1920, B16), ("Qi", 16, I32), ("Q", 16, F32), ("Qa", 16, I32), ("KCi", 1, I32), ("KCa", 1, I32), ("KC", 1, F32), ("In", 128, B16),
        ("I2", 128, B16), ("I2n", 128, B16), ("I05", 128, B16), ("SW05", 128, B16), ("I32", 128, B16), ("I16", 128, B16), ("I2048n", 128, B16), ("Forb", 128, B16),
        ("BROW", 128, B16), ("KL", 1, F32), ("RSTH", 128, B16), ("KCT", 136, B16), ("PEN", 128, B16), ("RH", 24, B16), ("KQ", 128, B16), ("KU", 128, B16), ("K1", 128, B16),
        ("KS", 64, B16), ("KV", 80, B16), ("GL", 16, B16), ("KT", 32, B16), ("THi", 128, F32), ("THb", 16, F32),
        ("LO", 512, B16), ("Lst", 512, B16), ("pA", 16, B16), ("pD", 32, B16), ("pP", 32, B16), ("c16", 16, B16), ("v1", 16, F32), ("v16", 16, F32), ("Lv", 16, H16),
        ("pr", 256, F32), ("w", 16, F32), ("wv", 16, F32), ("so", 32, U16)):
    tile(_n, _c, _d)
for _k in "01":
    for _n, _c, _d in (
            ("Z1", 384, B16), ("BB", 128, B16), ("BX", 128, B16), ("ks", 128, F32), ("Ab", 512, B16), ("d0", 128, B16), ("ab", 256, B16), ("m", 128, H16), ("uk", 128, F32), ("t1", 128, I32), ("t2", 128, I32), ("hi", 128, I32), ("hu", 128, U16),
            ("Ld0", 128, B16), ("Oxz", 128, H16), ("zt", 128, F32), ("e", 128, H16), ("eu", 128, U16), ("hme", 128, H16), ("OD", 128, H16), ("PN", 128, H16),
            ("Ge", 2048, B16), ("Gh", 2048, B16), ("Me", 2048, B16), ("Mh", 2048, B16), ("T1", 128, B16), ("PA", 128, H16), ("PB", 128, H16),
            ("pm", 128, F32), ("KI", 8, I32), ("KA", 8, I32), ("kk", 8, B16), ("k8s", 128, B16), ("oh", 128, B16), ("sel", 128, H16)):
        tile(_n + _k, _c, _d)
    for _t in range(HOPS + 1):
        for _x in ("X", "Y"):
            if (_t < HOPS) if _x == "X" else (_t > 0):
                buf("%s1_%d" % (_x, _t) + _k, 128 + 64 * int(_k), B16)
                buf("%s3_%d" % (_x, _t) + _k, 128, H16)
                if _k == "0":
                    buf("%s2_%d" % (_x, _t), 16, U16)
    for _j in range(4):
        buf("p" + _k + str(_j), 512, F32, "psum")
for _dt in used:
    SCRATCH[POOL[_dt]] = ("sbuf", [128, used[_dt]], _dt)
for _t in range(1, HOPS):
    for _k in "01":
        SEMAPHORES += ["x1_%d" % _t + _k, "x2_%d" % _t + _k, "x3_%d" % _t + _k]
SEMAPHORES += ["d%d" % _i for _i in range(20)]
CYC = 0.00083 * 1.2


def vc(n, f=1.0):
    return max(64, n * f) * CYC


def build():
    ops = []
    nd = [0]

    def op(e, r, w, f, cost, banks=(), dma=False, arg=None):
        o = dict(e=e, r=r.split(), w=w.split(), f=f, c=cost, b=list(banks), sem=None, arg=arg, i=len(ops), tk=-1)
        if dma:
            o["sem"] = "d%d" % nd[0]
            nd[0] += 1
        ops.append(o)
        return o

    def banks(*xs):
        return sorted(set(x[0] for x in xs if isinstance(x, tuple) and SCRATCH[x[0]][0] == "psum"))

    def short(*xs):
        return 0.5 if all(SCRATCH[x[0]][2] in (B16, H16, U16) for x in xs) else 1.0

    def load(e, r, w, fo, fi, cost=2.5):
        op(e, r, w, lambda g, T, q: q((g.sync if e == "Y" else g.scalar).dma_start(fo(T), fi(T))), cost, dma=True)

    def G(r, w, f, cost):
        op("G", r, w, lambda g, T, q: q(f(g, T)), cost)

    def ms(w, o, v, r=""):
        op("V", r, w, lambda g, T, q: q(g.vector.memset(ap(T, o), v)), vc(width(o), short(o)))

    def cp(r, w, o, i):
        op("V", r, w, lambda g, T, q: q(g.vector.tensor_copy(ap(T, o), ap(T, i))), vc(width(o), short(o, i)), banks(o, i))

    def ts(r, w, o, i, s1, o1, s2=None, o2=None):
        def f(g, T, q):
            if o2 is None:
                q(g.vector.tensor_scalar(ap(T, o), ap(T, i), ap(T, s1), None, o1))
            else:
                q(g.vector.tensor_scalar(ap(T, o), ap(T, i), ap(T, s1), ap(T, s2), o1, o2))
        op("V", r, w, f, vc(width(o), short(o, i)), banks(o, i))

    def tt(r, w, o, i0, i1, al):
        op("V", r, w, lambda g, T, q: q(g.vector.tensor_tensor(ap(T, o), ap(T, i0), ap(T, i1), al)), vc(width(o), 1 if banks(i0, i1) else 2), banks(o, i0, i1))

    def scan(r, w, o, d0, d1, o0, o1):
        op("V", r, w, lambda g, T, q: q(g.vector.tensor_tensor_scan(ap(T, o), ap(T, d0), ap(T, d1), 0.0, o0, o1)), vc(width(o)), banks(o, d0, d1))

    def pick(r, w, o, win, off, i1=None, al=None):
        def f(g, T, q):
            x = ap(T, win).indirect(ap(T, off))
            q(g.vector.tensor_copy(ap(T, o), x) if al is None else g.vector.tensor_tensor(ap(T, o), x, ap(T, i1), al))
        op("V", r, w, f, 0.05 + width(o) * 1.56 * CYC)

    def ac(r, w, o, i, fn, **kw):
        op("S", r, w, lambda g, T, q: q(g.scalar.activation(ap(T, o), ap(T, i), fn, **dict((k, ap(T, x)) for k, x in kw.items()))), vc(width(o)) + 0.03, banks(o, i))

    def TM(r, w, lst, piece=8):
        bk = banks(*[x[0] for x in lst])
        for a in range(0, len(lst), piece):
            def f(g, T, q, part=lst[a:a + piece]):
                for (o, l, m, s, p) in part:
                    q(g.tensor.matmul(ap(T, o), ap(T, l), ap(T, m), bool(s), bool(p)))
            op("T", r, w + "".join(" T" + b for b in bk), f, 0.02 + sum(max(min(64, width(l)), width(m)) for (o, l, m, s, p) in lst[a:a + piece]) * 0.00042 * 1.25, bk)

    def Lb(b, name="C", rows=None):
        return at(name, 15 - b, 143 - b, 1, rows)

    def Rb(b, s=1):
        return at("R", 128 * b, 128 * b + 128, s)

    def swap(o, lhs, src, stop=0):
        p, r, a, b, s = o
        p2, r2, a2, b2, s2 = src
        return [((p, r, a + j, b, 2), lhs, (p2, r2, a2 + 1 - j, b2, 2), 0, stop and j) for j in (0, 1)]

    cI, cIn, cO, G8 = at("I"), at("In"), at("ONES", 0, 128), at("Bk", 0, 128, 16)
    users = at("VT", 0, 2048)
    lanes = [(0.5, -1.5) if "like" in on else (1.0, -25.5) for on in ON_SCALAR]
    load("Y", "", "VDv", lambda T: ap(T, at("VD0", 0, 256, 1, 8)), lambda T: T.v0[:, :], 2.0)
    load("S", "", "VDd", lambda T: ap(T, at("VD0", 256, 512, 1, 8)), lambda T: T.d0[:, :], 2.0)
    load("Y", "", "PX", lambda T: T.PX[:, :], lambda T: T.px[:, :], 4.5)
    load("S", "", "WTi", lambda T: T.WTi[:, :], lambda T: T.wt[:, :], 2.2)
    for k in (0, 1):
        load("S", "", "X1_0%dz" % k, lambda T, k=k: ap(T, at("X1_0%d" % k, 0, 128)), lambda T, k=k: T.z0[:, 128 - 128 * k:256 - 128 * k], 2.3)
    load("S", "", "KPi", lambda T: T.KPi[:, :], lambda T: T.kap[:, :], 2.4)
    load("S", "", "F0", lambda T: T.F0[:, :], lambda T: T.f0[:, :], 2.8)
    load("Y", "", "VW", lambda T: T.VW[:, :], lambda T: T.vw[:, :], 6.0)
    for nm, v in (("ONES", 1.0), ("C", 0.0), ("PMAG", MAGIC), ("NMAG", -MAGIC), ("KQ", -1.0 / 512), ("K1", 1.0 / 128), ("P845", 84.5)):
        ms(nm, at(nm), v)
    for rows, v in (((0, 32), -1.0 / 64), ((32, 64), 2.0 ** -17), ((64, 128), 0.0)):
        ms("KU", at("KU", rows=rows), v)

    def aff(src, dst, pat, cmp, base, cm, rows=None, fill=0.0):
        n = PLACE[dst][2]
        G(src, dst, lambda g, T: g.affine_select(ap(T, at(dst, rows=rows)), ap(T, at(src, 0, n, 1, rows)), pat, cmp, fill, base, cm), 0.17 + 2 * n * CYC)

    def fill(dst, a, b, v):
        G("ONES", dst, lambda g, T: g.affine_select(ap(T, at(dst, a, b)), ap(T, at("ONES", 0, b - a)), [[0, b - a]], A.is_ge, v, -1, 0), 0.17 + 2 * (b - a) * CYC)
    odd = [(8, (2 * lanes[k][1] - 1) * BIG / 128) for k in (1, 0)]
    for nm, parts in (("KS", ((16, 0.0), (16, 1.0 / 128), (32, 0.0))), ("KV", [(48, 1.0 / 128)] + odd + odd), ("KT", [(8, t / 128.0) for t in range(HOPS)]),
                      ("KN", ((128, -2048.0),)), ("ZERO", ((128, 0.0),))):
        c0 = 0
        for n, v in parts:
            fill(nm, c0, c0 + n, v)
            c0 += n
    fill("KCT", 128, 136, 2048.0)

    def iota(dst, pat, base, cm, small=False):
        cost = 0.13 + 2 * PLACE[dst][2] * CYC
        if small:
            G("", dst, lambda g, T: g.iota(ap(T, at(dst)), pat, base, cm, allow_small_or_imprecise_dtypes=True), cost)
        else:
            G("", dst, lambda g, T: g.iota(ap(T, at(dst)), pat, base, cm), cost)
    iota("THb", [[19616, 16]], 0, 0, True)
    iota("THi", [[-13824, 128]], 2097152, 0, True)
    aff("ONES", "CT", [[1, 144]], A.is_equal, -15, -16, 8)
    aff("ONES", "Bt", [[-16, 8], [0, 16]], A.is_ge, 0, 1)
    aff("Bt", "Bk", [[16, 8], [0, 16]], A.is_ge, 15, -1)
    aff("ONES", "I", [[-1, 128]], A.is_equal, 0, 1)
    iota("Qi", [[-1, 16]], 16, 1)
    iota("KCi", [[1, 1]], 0, 1)
    aff("ONES", "SW", [[-2, 64], [1, 2]], A.is_equal, -1, 1)
    iota("BROW", [[0, 8], [1, 16]], 0, 0, True)
    iota("Lst", [[0, 512]], 0, 0, True)
    G("", "VT0", lambda g, T: g.iota(ap(T, at("VT", 2048, 2064)), [[0, 16]], 0, 0), 0.17)
    aff("SW", "SWI", [[-1, 128]], A.not_equal, 0, 1, None, -1.0)
    aff("ZERO", "RSTH", [[0, 8], [1, 16]], A.not_equal, 0, 0, None, 2.0 ** 20)
    aff("ONES", "E8", [[-1, 8], [0, 16]], A.is_equal, 0, 1, 8)
    for j in range(16):
        ac("THi THb", "TH", at("TH", j, 2048, 16), at("THi"), F.Identity, bias=at("THb", j, j + 1))
    cp("Bk C", "C", at("C", 15, 143, 16), G8)
    ac("C", "C16", at("C16"), at("C"), F.Copy, scale=1.0 / 16)
    ts("Qi", "Qa", at("Qa"), at("Qi"), 15, A.bitwise_and)
    ts("Qa", "Q", at("Q"), at("Qa"), 0, A.is_equal)
    ts("KCi", "KCa", at("KCa"), at("KCi"), 15, A.bitwise_and)
    cp("KCa", "KC", at("KC"), at("KCa"))
    ts("KCa", "KL", at("KL"), at("KCa"), 2049.0, A.add, 1.0 / 64, A.mult)
    for b in range(16):
        ts("Bk Q", "R", Rb(b), at("Bk"), at("Q", b, b + 1), A.mult)
    for b in range(15):
        G("R", "RI", lambda g, T, b=b: g.affine_select(ap(T, at("RI", 128 * b, 128 * b + 128)), ap(T, Rb(b)), [[-1, 128]], A.not_equal, -1.0, 0, 1), 0.17 + 256 * CYC)
    for nm, src, s in (("In", "I", -1.0), ("I2", "I", 2.0), ("I2n", "I", -2.0), ("I05", "I", 0.5), ("I32", "I", 32.0), ("I2048n", "I", -2048.0),
                       ("BB0", "Bk", lanes[0][0] * BIG), ("BX0", "Bk", lanes[0][0] / 32), ("BB1", "Bk", lanes[1][0] * BIG), ("BX1", "Bk", lanes[1][0] / 32)):
        ts(src, nm, at(nm), at(src), s, A.mult)
    for nm, src, s in (("I16", "I", 16.0), ("SWX", "SW", 1.0 / 32 / BIG), ("PEN", "Bk", 16384.0)):
        ac(src, nm, at(nm), at(src), F.Copy, scale=s)
    aff("In", "SWn", [[-2, 64], [1, 2]], A.not_equal, -1, 1, None, -1.0)
    ts("BROW KC", "Forb", at("Forb"), at("BROW"), at("KC"), A.is_gt, 64.0, A.mult)
    ac("BROW", "KCT", at("KCT", 0, 128), at("BROW"), F.Copy, scale=1.0 / 128)
    for c0, s in ((0, -16.0), (8, 32.0), (16, 16.0)):
        ac("Bk", "RH", at("RH", c0, c0 + 8), G8, F.Copy, scale=s)
    if FARS:
        ts("BROW", "QB", at("QB"), at("BROW", 0, 128), FAR - 0.5, A.is_lt, 16.0, A.mult)
        tt("QB Bk", "QA", at("QA"), at("QB"), at("Bk"), A.mult)
    for c0, s in ((0, -32768.0), (8, 0.5)):
        ac("Bk", "GL", at("GL", c0, c0 + 8), G8, F.Copy, scale=s)
    cp("WTi", "WTa", at("WTa"), at("WTi"))
    ts("WTi", "WTb", at("WTb"), at("WTi"), 1.0 / 2048, A.mult)
    cp("KPi", "KP", at("KP"), at("KPi"))
    ts("Bk WTa", "Wa", at("Wa"), at("Bk"), at("WTa"), A.mult)
    ts("Bk WTb", "Wb", at("Wb"), at("Bk"), at("WTb"), A.mult)
    cp("VDv", "VDh", at("VDh", 0, 256, 1, 8), at("VD0", 0, 256, 1, 8))
    cp("VDd", "VDh", at("VDh", 256, 512, 1, 8), at("VD0", 256, 512, 1, 8))
    TM("VDh CT", "vdL", [(at("p03", 0, 32), Lb(b, "CT", 8), at("VDh", b, 512, 16, 8), b == 0, b == 15) for b in range(16)], 16)
    cp("vdL", "X2_00 X2_01", at("X2_0"), at("p03", 0, 16))
    cp("vdL", "X1_0c", at("X1_01", 144, 160), at("p03", 16, 32))
    ms("X1_0c", at("X1_01", 128, 144), 0.0)
    for k in (0, 1):
        o8, o = 8 * (1 - k), 128 * (1 - k)
        ms("X1_0c", at("X1_01", 160 + o8, 168 + o8), lanes[k][1] * BIG)
        ts("vdL", "X1_0c", at("X1_01", 176 + o8, 184 + o8), at("p03", 16 + o8, 24 + o8), 1.0, A.is_ge, lanes[k][1] / 32 - 1, A.add)
        cp("F0", "X3_0%d" % k, at("X3_0%d" % k), at("F0", o, o + 128))
    for c0 in range(0, 1024, 128):
        ts("VW", "VT1", at("VT", c0, 128 + c0), at("VW", c0, c0 + 128), 2047, A.bitwise_and)
        ts("VW", "VT1", at("VT", 1024 + c0, 1152 + c0), at("VW", c0, c0 + 128), 11, A.logical_shift_right)

    def send(t, k, part, rd, wr, cols=None):
        x = "%d_%d" % (part, t + 1) + ("" if cols else str(k))
        cols = cols or (0, None)
        o = op("G", rd, "", None, SEND, arg=(at("Y" + x, *cols), at("X" + x, *cols), "x%d_%d%d" % (part, t + 1, k), part))
        r = op("N", "", wr, None, WAY - (0.5 if part == 2 else 0.0))
        r["from"] = o["i"]

    def names(t, k):
        K = str(k)
        return (K, "X1_%d" % t + K, "X2_%d" % t, "X3_%d" % t + K, "Y1_%d" % (t + 1) + K, "Y2_%d" % (t + 1), "Y3_%d" % (t + 1) + K,
                lambda s: "".join(" " + (n + K if n[-1] != "!" else n[:-1]) for n in s.split()), lambda n, a=0, b=None, s=1, rows=None: at(n + K, a, b, s, rows),
                lambda j, a, b, s=1, rows=None: at("p%d%d" % (k, j), a, b, s, rows))

    def head(t, k):
        K, x1, x2, x3, y1, y2, y3, u, tl, ps = names(t, k)
        o8, o = 8 * (1 - k), 128 * (1 - k)
        zX, fX, vX = at(x1, 0, 128), at(x3), at(x2, o8, o8 + 8)
        zk, vk = x1 + "z ", x2 + K + " "
        tL, tO, ta, tb = at("LO", o, o + 128), at("LO", 256 + o, 384 + o), tl("ab", 0, 128), tl("ab", 128, 256)
        TM(zk + "Wb KU ONES", u("U"), [(ps(2, 0, 128), at("Wb"), zX, 1, 0), (ps(2, 0, 128), cO, at("KU"), 0, 1)])
        ts(u("U"), u("m"), tl("m"), ps(2, 0, 128), MAGIC, A.add, MAGIC, A.subtract)
        TM(zk + u("m Wa! I2048n!"), u("u"), [(ps(2, 128, 256), at("Wa"), zX, 1, 0), (ps(2, 128, 256), at("I2048n"), tl("m"), 0, 1)])
        ac(u("u KP!"), u("uk"), tl("uk"), ps(2, 128, 256), F.Identity, scale=at("KP"))
        pB, pX = ps(1, 0, 128), ps(1, 256, 384)
        TM("X1_%dc R" % t, u("B"), [(ps(1, b, 384, 16), Rb(b), at("X1_%d1" % t, 160 + o8, 184 + o8), b == 0, 0) for b in range(16)])
        signs, plain = "like" in ON_SCALAR[k], "x" in ON_SCALAR[k]
        if plain:
            op("S", vk + "PX", u("d0"), lambda g, T, q: q(g.scalar.activation(ap(T, tl("d0")), T.PX[:, :].indirect(ap(T, vX)), F.Identity)), 0.08 + 128 * 1.56 * CYC)
            TM(zk + u("d0 I! In!"), u("D0"), [(ps(0, 0, 128), cIn, zX, 1, 0), (ps(0, 0, 128), cI, tl("d0"), 0, 1)])
        else:
            pick(vk + "PX " + zk, u("d0"), tl("d0"), at("PX"), vX, zX, A.subtract)
        if signs:
            ac(u("D0" if plain else "d0"), u("a"), ta, ps(0, 0, 128) if plain else tl("d0"), F.Abs)
            ac(u("a P845!"), u("b"), tb, ta, F.Sign, scale=-1.0, bias=at("P845"))
        else:
            ts(u("d0"), u("a"), ta, tl("d0"), 84.0, A.is_le)
            ts(u("d0"), u("b"), tb, tl("d0"), -84.0, A.is_ge)
        pick(vk + "TH " + u("uk"), u("t1"), tl("t1"), at("TH"), vX, tl("uk"), A.add)
        for n, x in ((("b", tb),) if signs else (("a", ta), ("b", tb))):
            TM(u(n + " B BB BX"), u("B"), [(pB, tl("BB"), x, 0, 0)] + swap(pX, tl("BX"), x))
        TM(x3 + u("B I32!"), u("B"), [(pB, at("I32"), fX, 0, 1)])

        def liked():
            ts(u("B"), u("L"), tL, pB, 0.0, A.is_ge)
            tt(u("B L"), u("O"), tO, tL, pX, A.is_lt)

        def second():
            tt(u("t1 B"), u("t2"), tl("t2"), tl("t1"), pB, A.max)
            ts(u("t2"), u("hi"), tl("hi"), tl("t2"), 5, A.logical_shift_right, 2047, A.bitwise_and)
            cp(u("hi"), u("hu"), tl("hu"), tl("hi"))
        for step in ((second, liked) if FIRST[k] == "h" else (liked, second)):
            step()
        if not plain:
            TM(u("d0 I!"), u("D0"), [(ps(0, 0, 128), cI, tl("d0"), 1, 1)])
        TM(zk + u("d0 I! I2! I2n!"), u("xz"), [(ps(0, 384, 512), at("I2n"), zX, 1, 0)] + swap(ps(0, 384, 512), cI, tl("d0")) + swap(
            ps(0, 384, 512), cI if plain else at("I2"), zX, 1))
        tt(u("L D0"), u("Ld0"), tl("Ld0"), tL, ps(0, 0, 128), A.mult)
        tt(u("O xz"), u("Oxz"), tl("Oxz"), tO, ps(0, 384, 512), A.mult)
        TM(zk + u("Ld0 I!"), u("q"), [(ps(0, 128, 256), cI, zX, 1, 0), (ps(0, 128, 256), cI, tl("Ld0"), 0, 1)])
        zr, hf = ps(2, 256, 384), at("I05")
        TM(zk + u("Ld0 Oxz I! I05! KQ! ONES!"), u("zn"), [(zr, cI, zX, 1, 0), (zr, hf, tl("Ld0"), 0, 0), (zr, hf, tl("Oxz"), 0, 0), (zr, cO, at("KQ"), 0, 1)])
        if "z" in ON_SCALAR[k]:
            ac(u("zn PMAG!"), u("zt"), tl("zt"), zr, F.Identity, bias=at("PMAG"))
            ac(u("zt NMAG!"), y1 + "z", at(y1, 0, 128), tl("zt"), F.Identity, bias=at("NMAG"))
        else:
            ts(u("zn"), y1 + "z", at(y1, 0, 128), zr, MAGIC, A.add, MAGIC, A.subtract)
        if t < HOPS - 1 and k == 0:
            send(t, k, 1, y1 + "z", "X1_%d0z" % (t + 1))
        pick(vk + "VT1 VT", u("e"), tl("e"), users, vX)
        cp(u("e"), u("eu"), tl("eu"), tl("e"))
        TM(u("e I!"), u("eP"), [(ps(1, 0, 128), cI, tl("e"), 1, 1)])
        TM(u("L O In! ONES! K1!"), u("oP"), [(ps(1, 384, 512), cO, at("K1"), 1, 0), (ps(1, 384, 512), cIn, tL, 0, 0), (ps(1, 384, 512), cIn, tO, 0, 1)])
        tt(u("hi eP"), u("hme"), tl("hme"), tl("hi"), ps(1, 0, 128), A.subtract)
        tt(u("hme oP"), u("PN"), tl("PN"), tl("hme"), ps(1, 384, 512), A.mult)
        TM(u("hme I!"), u("H"), [(ps(1, 0, 128), tl("hme"), cI, 1, 1)])

    def joint(t):
        x1, y1, ck = "X1_%d1" % t, "Y1_%d1" % (t + 1), "X1_%dc " % t
        AX, DX, PX_ = at(x1, 128, 144), at(x1, 144, 160), at(x1, 160, 176)
        lL, lO, lst = at("Lst", 0, 256, 16), at("Lst", 256, 512, 16), at("Lst", 0, 512, 16)

        def ps(a, b, s=1, rows=None):
            return at("p03", a, b, s, rows)
        TM("L0 O0 L1 O1 C16", "ll", [(ps(0, 32), Lb(b, "C16"), at("LO", b, 512, 16), b == 0, b == 15) for b in range(16)])
        TM(ck + "KV SWI SWn I I2n ONES", "val", [
            (ps(32, 112), cO, at("KV"), 1, 0), (ps(32, 48), at("SWI"), AX, 0, 0), (ps(48, 64), cI, DX, 0, 0), (ps(64, 80), cI, DX, 0, 0),
            (ps(80, 96), at("I2n"), PX_, 0, 0), (ps(96, 112), at("SWn"), PX_, 0, 1)])
        cp("ll", "Lst", lst, ps(0, 32))
        tt("Lst val", "pA", at("pA"), lO, ps(32, 48), A.mult)
        tt("Lst val", "pD", at("pD"), lst, ps(48, 80), A.mult)
        dL, dO, pL, pO = at("pD", 0, 16), at("pD", 16, 32), at("pP", 0, 16), at("pP", 16, 32)
        if t < HOPS - 1:
            tt("Lst val", "pP", at("pP"), lst, ps(80, 112), A.mult)
            mm = [(ps(112, 176), cO, at("KS"), 1, 0), (ps(112, 160), cI, at(x1, 128, 176), 0, 0)]
            for c0, lhs, srcs in ((112, cI, (lL, at("pA"))), (128, cIn, (dL, dO)), (144, cI, (pL, pO)), (160, at("SWX"), (PX_, pL, pO)), (160, cIn, (lL, lO))):
                mm += [(ps(c0, c0 + 16), lhs, s, 0, s is lO) for s in srcs]
            TM(ck + "Lst pA pD pP I In SWX KS ONES", "nl", mm)
            cp("nl", y1 + "c", at(y1, 128, 192), ps(112, 176))
            send(t, 1, 1, y1 + "z " + y1 + "c", "X1_%d1z X1_%dc" % (t + 1, t + 1))
        else:
            cc, r8 = ps(112, 128), ps(0, 256, 1, 8)
            TM(ck + "Lst pA pD I In I16 K1 ONES", "nl", [(cc, cO, at("K1", 0, 16), 1, 0), (cc, cI, DX, 0, 0), (cc, cIn, dL, 0, 0), (cc, cIn, dO, 0, 0)] + [
                (cc, at("I16"), s, 0, s is lL) for s in (AX, at("pA"), lL)])
            cp("nl", "c16", at("c16"), cc)
        vk = "X2_%d0 X2_%d1" % (t, t)
        ts(vk, "v1", at("v1"), at("X2_%d" % t), 1.0, A.add, 1.0 / 64, A.mult)
        tt("v1 Lst", "Lv", at("Lv"), at("v1"), lL, A.mult)
        mm = [(ps(256, 384), cI, at("Forb"), 1, 0), (ps(384, 512), cI, at("Forb"), 0, 0)]
        for j in range(1, 16):
            mm += [(ps(256 + j, 512, 16), at("RI", 128 * j - 128, 128 * j), at("Lv"), 0, j == 15)]
        TM("Lv I Forb RI", "dg", mm)
        scan("dg Lst", "pr", at("pr"), ps(256, 512), at("Lst", 0, 256), A.mult, A.add)
        ts("pr KL", "w", at("w"), at("pr", 15, 256, 16), 0.0, A.is_equal, at("KL"), A.mult)
        tt("w v1", "wv", at("wv"), at("w"), at("v1"), A.max)
        ts("wv", "so", at("so", 0, 32, 2), at("wv"), 64.0, A.mult, -1.0, A.add)
        if t == HOPS - 1:
            TM("c16 R", "yc", [(ps(b, 256, 16, 8), Rb(b, 16), at("c16"), b == 0, b == 15) for b in range(16)])
            ac("yc", "YC", at("YC", rows=8), r8, F.Copy)
            load("Y", "YC", "oc", lambda T: T.yc[:, :], lambda T: ap(T, at("YC", rows=8)))

    def tail(t, k):
        K, x1, x2, x3, y1, y2, y3, u, tl, ps = names(t, k)
        last = t == HOPS - 1
        o8, o = 8 * (1 - k), 128 * (1 - k)
        tL, tO = at("LO", o, o + 128), at("LO", 256 + o, 384 + o)
        both = (FIRST[k], "h" if FIRST[k] == "e" else "e")
        per = 64 // PIECE
        for nm in both:
            for j in (0, 1):
                gk = " ".join("G%s%d%d_" % (nm, j, i) + K for i in range(per))
                for i, gi in enumerate(gk.split()):
                    c0 = 64 * j + PIECE * i
                    op("S", u(nm + "u PX!"), gi, lambda g, T, q, nm=nm, c0=c0: q(g.scalar.activation(ap(T, tl("G" + nm, 16 * c0, 16 * (c0 + PIECE))),
                       T.PX[:, :].indirect(ap(T, tl(nm + "u", c0, c0 + PIECE))), F.Identity)), 0.08 + 16 * PIECE * 1.56 * CYC)
                for i in range(FAR if nm + K in FARS else 0, 16):
                    tt(gk + u("q"), "M%s%d_%d_" % (nm, j, i) + K, tl("M" + nm, i * 128 + 64 * j, i * 128 + 64 * (j + 1)), tl("G" + nm, 1024 * j + i, 1024 * (j + 1), 16),
                       ps(0, 128 + 64 * j, 192 + 64 * j), A.max)
        pd, lk = {"h": ps(2, 0, 128), "e": ps(1, 256, 384)}, ps(2, 128, 136)

        def distances(nm):
            dk, far = u("d" + nm), FAR if nm + K in FARS else 0
            if nm == "h":
                TM("KCT ONES", dk, [(ps(2, 0, 136), cO, at("KCT"), 1, 0)])
                TM(y1 + "z " + u("L O KT! GL! ONES! Bk!"), dk, [
                    (lk, cO, at("KT", 8 * t, 8 * t + 8), 0, 0), (lk, at(y1, 0, 128), G8, 0, 0), (lk, tL, at("GL", 0, 8), 0, 0), (lk, tO, at("GL", 0, 8), 0, 0),
                    (lk, tO, at("GL", 8, 16), 0, 0)])
            else:
                TM(u("L KN! PEN! ONES!"), dk, [(pd[nm], cO, at("KN"), 1, 0), (pd[nm], tL, at("PEN"), 0, 0)])
            gs = " ".join("G%s%d%d_" % (nm, j, i) + K for j in (0, 1) for i in range(per))
            p, r, a, b, s = pd[nm]
            ou = [(p, r, a + i, b, 16) for i in range(16)]
            if far:
                TM(x1 + "z QA" + u("Ld0"), dk, [(pd[nm], at(x1, 0, 128), at("QA"), 0, 0), (pd[nm], tl("Ld0"), at("QA"), 0, 0)])
                mm = []
                for i in range(far):
                    df = at("p13", 128 * i, 128 * i + 128)
                    mm += [(df, cIn, at(x1, 0, 128), 1, 0), (df, cIn, tl("Ld0"), 0, 0), (df, cI, tl("G" + nm, i, 2048, 16), 0, 1)]
                TM(gs + " I In " + x1 + "z" + u("Ld0"), "df", mm, 6)
                ac("df", u("Ab"), tl("Ab", 0, 128 * far), at("p13", 0, 128 * far), F.Abs)
            TM(gs + dk + " RH", dk, [(ou[i], tl("G" + nm, i, 2048, 16), at("RH", 0, 8), 0, 0) for i in range(far, 16)])
            for kq in range(far, 16, 4):
                mx = " ".join("M%s%d_%d_" % (nm, j, kk) + K for j in (0, 1) for kk in range(kq, min(16, kq + 4)))
                TM(mx + dk + " RH", dk, [(ou[i], tl("M" + nm, 128 * i, 128 * i + 128), at("RH", 8, 16), 0, i == 15 and not far) for i in range(kq, min(16, kq + 4))])
            if far:
                TM(u("Ab RH!") + dk, dk, [(ou[i], tl("Ab", 128 * i, 128 * i + 128), at("RH", 16, 24), 0, i == far - 1) for i in range(far)])
            if nm == both[0]:
                if "ks" in ON_SCALAR[k]:
                    ac(dk, u("ks"), tl("ks"), pd[nm], F.Copy)
                else:
                    cp(dk, u("ks"), tl("ks"), pd[nm])

        def place():
            scan(u("dh RSTH!"), u("pm"), tl("pm"), at("RSTH"), pd["h"], A.add, A.min)
            tt(u("dh pm"), u("KI"), tl("KI"), tl("pm", 15, 128, 16), lk, A.min)
            if both[1] == "h":
                nearer()
            ts(u("KI"), u("KA"), tl("KA"), tl("KI"), 15, A.bitwise_and)
            cp(u("KA"), u("kk"), tl("kk"), tl("KA"))
            k8 = ps(2, 384, 512, 1, 8)
            TM(u("kk I!"), u("k8"), [(k8, tl("kk"), cI, 1, 1)])
            if "k8" in ON_SCALAR[k]:
                ac(u("k8"), u("k8s"), tl("k8s", rows=8), k8, F.Copy)
            else:
                cp(u("k8"), u("k8s"), tl("k8s", rows=8), k8)
            TM(u("k8s E8!"), u("kF"), [(ps(2, 256, 384), at("E8", rows=8), tl("k8s", rows=8), 1, 1)])
            ts(u("kF KC!"), u("oh"), tl("oh"), ps(2, 256, 384), at("KC"), A.is_equal)

        def nearer():
            tt(u("ks d" + both[1]), u("T1"), tl("T1"), tl("ks"), pd[both[1]], A.is_lt if both[1] == "e" else A.is_gt)
            tt(u("T1 H"), u("PA"), tl("PA"), tl("T1"), ps(1, 0, 128), A.mult)
            TM(u("e I! In!"), u("eD"), [(ps(0, 384, 512), cIn, tl("e"), 1, 0)] + swap(ps(0, 384, 512), cI, tl("e")))
            TM(u("PA eD SWI!"), u("eD"), [(ps(0, 384, 512), tl("PA"), at("SWI"), 0, 1)])
            tt(u("O eD"), u("OD"), tl("OD"), tO, ps(0, 384, 512), A.mult)

        def view(nm, ou, parts):
            TM(u(" ".join(parts) + " I!"), u(nm), [(ou, cI, tl(n), n == "e", 0) for n in parts])
            TM(u("PA I! " + nm), u(nm), [(ou, tl("PA"), cI, 0, 0)])
            TM(u("OD I! " + nm), u(nm), [(ou, cI, tl("OD"), 0, 1)])
        en, pY = ps(1, 128, 256), ps(2, 0, 128) if both[0] == "h" else at("p13", 0, 128)
        distances(both[0])
        if both[0] == "h":
            place()
        distances(both[1])
        if both[0] == "h":
            nearer()
        else:
            place()
        view("Y", pY, ("e", "PN"))
        view("en", en, ("e",))
        cp(u("en"), y3, at(y3), en)
        tt(u("oh Y"), u("sel"), tl("sel"), tl("oh"), pY, A.mult)
        if not last:
            TM(u("sel C!"), u("vl"), [(ps(1, 256, 264), Lb(b), tl("sel", b, 128, 16), b == 0, b == 15) for b in range(16)], 16)
            cp(u("vl"), y2 + K, at(y2, o8, o8 + 8), ps(1, 256, 264))
            send(t, k, 3, y3, "X3_%d" % (t + 1) + K)
            send(t, k, 2, y2 + K, "X2_%d" % (t + 1) + K, (o8, o8 + 8))
        else:
            c0, c1 = o, o + 128
            ac(y1 + "z", u("YZ"), at("YZ", c0, c1), at(y1, 0, 128), F.Copy)
            load("Y", u("YZ"), u("oz"), lambda T: T.yz[:, c0:c1], lambda T: ap(T, at("YZ", c0, c1)))
            ac(u("en"), u("YF"), at("YF", c0, c1), en, F.Copy)
            load("Y", u("YF"), u("of"), lambda T: T.yf[:, c0:c1], lambda T: ap(T, at("YF", c0, c1)))
            TM(u("sel Bk!"), u("yv"), [(ps(1, 256, 384, 1, 8), G8, tl("sel"), 1, 1)])
            ac(u("yv"), u("YV"), at("YV", c0, c1, 1, 8), ps(1, 256, 384, 1, 8), F.Copy)
            load("Y", u("YV"), u("ov"), lambda T: T.yv[:, c0:c1], lambda T: ap(T, at("YV", c0, c1, 1, 8)))
        for c in range(7, -1, -1):
            op("V", y3 + " so VT0 VT1 VT", "VT", lambda g, T, q, c=c: q(g.vector.tensor_copy(
                T.VT[:, 0:2064].indirect(ap(T, at("so", 2 * (o8 + c), 2 * (o8 + c) + 1))), ap(T, at(y3, 16 * c, 16 * c + 16)))), 0.05 + 16 * 3.8 * CYC)

    for t in range(HOPS):
        for fn, k in ((head, 0), (head, 1), (lambda t, k: joint(t), 1), (tail, 0), (tail, 1)):
            i0 = len(ops)
            fn(t, k)
            for o in ops[i0:]:
                o["tk"] = 2 * t + k
    for j in range(4):
        pj, c0 = "p%d%d" % (j % 2, 1 + j // 2), 256 * j
        ts("VT", "yh%d T%s" % (j, pj), at(pj, 0, 256), at("VT", 1024 + c0, 1280 + c0), 2048.0, A.mult)
        tt("VT yh%d" % j, "YW%d" % j, at("YW", c0, c0 + 256), at("VT", c0, 256 + c0), at(pj, 0, 256), A.add)
        load("YS"[j % 2], "YW%d" % j, "ow%d" % j, lambda T, c0=c0: T.yw[:, c0:c0 + 256], lambda T, c0=c0: ap(T, at("YW", c0, c0 + 256)))
    return ops


PARTS = ("R", "RI", "TH", "Z10", "Z11", "KS", "KV", "KT", "RH", "KU", "KCT", "GL", "VDh", "X1_0c", "VT1")


def dag(ops):
    writer, readers, bank = {}, {}, {}
    for o in ops:
        i, p = o["i"], set()
        if "from" in o:
            p.add(o["from"])
        for k in o["r"]:
            p.update(writer.get(k, []))
            readers.setdefault(k, []).append(i)
        for k in o["w"]:
            if k in PARTS and not readers.get(k):
                writer.setdefault(k, []).append(i)
                continue
            p.update(writer.get(k, []))
            p.update(readers.get(k, []))
            writer[k], readers[k] = [i], []
        for k in o["b"]:
            cur = bank.get(k)
            if cur is None:
                bank[k] = (o["e"], [i], [])
            elif cur[0] == o["e"]:
                cur[1].append(i)
                p.update(cur[2])
            else:
                p.update(cur[1])
                bank[k] = (o["e"], [i], list(cur[1]))
        p.discard(i)
        o["p"] = p
    return ops


def plan():
    ops = dag(build())
    n = len(ops)
    eng = [o["e"] for o in ops]
    cost = [o["c"] for o in ops]
    hold = [0.0 if o["e"] == "N" else 0.1 if o["sem"] else o["c"] for o in ops]
    succ = [[] for _ in ops]
    left0 = [len(o["p"]) for o in ops]
    for o in ops:
        for p in o["p"]:
            succ[p].append((o["i"], 0.0 if eng[p] == "T" and o["e"] == "T" else 0.08))
    chain = [o["i"] for o in ops if o["e"] == "S" and o["w"][0][:2] in ("Ge", "Gh")]
    for a, b in zip(chain, chain[1:]):
        succ[a].append((b, 0.0))
        left0[b] += 1

    def run(prio, soon):
        left, ready, st, order = list(left0), [0.0] * n, [0.0] * n, []
        free = dict((e, 0.0) for e in "VSTGYN")
        avail = dict((e, [i for i in range(n) if eng[i] == e and not left[i]]) for e in free)
        while len(order) < n:
            t0, e = min((max(free[e], min(ready[i] for i in avail[e])), e) for e in avail if avail[e])
            i = max((j for j in avail[e] if ready[j] <= t0 + soon + 1e-9), key=lambda j: (prio[j], -j))
            avail[e].remove(i)
            st[i] = max(t0, ready[i])
            free[e] = st[i] + hold[i]
            order.append(i)
            for s, lat in succ[i]:
                ready[s] = max(ready[s], st[i] + cost[i] + lat)
                left[s] -= 1
                if not left[s]:
                    avail[eng[s]].append(s)
        return max(st[i] + cost[i] for i in range(n)), st, order

    def ways(order, queues):
        way, own, after = [0.0] * n, [0.0] * n, {}
        for i in reversed(order):
            own[i] = way[i] = cost[i] + max([way[s] + lat for s, lat in succ[i]] + [0.0])
            if queues and hold[i]:
                way[i] = max(way[i], hold[i] + after.get(eng[i], 0.0))
                after[eng[i]] = way[i]
        return own
    best = None
    for soon in (0.0, 0.03, 0.06):
        prio = ways(range(n), False)
        for _ in range(PASSES):
            got = run(prio, soon)
            if best is None or got[0] < best[0]:
                best = got
            prio = [(a + b) / 2 for a, b in zip(prio, ways(got[2], True))]
    for o in ops:
        o["start"] = best[1][o["i"]]
    return ops, best[2]


PLAN = {}


def relays(core, T, topo):
    dst = T.cores[(T.rank_of(core) + STEP) % N]
    return [c for c in topo.cores_of(core) if c != core and topo.die(c) == topo.die(core) and topo.may_write(c, dst)][:2], dst


def relay_program(g, core, T, topo, which, src, dst):
    rid, pid = topo.addr(dst, core)
    sent = 0
    ops, order = PLAN["p"]
    for a, x, s, part in [ops[i]["arg"] for i in order if ops[i]["arg"]]:
        if RELAY[part] == which:
            g.wait_ge(T.sem[s], len(topo.engines(src, core)))
            g.remote_dma(ap(T, x), ap(T, x), T.sem[s], T.sem.ls, pid, rid, topo.mask(core, dst))
            sent += len(topo.engines(core, dst))
    g.wait_ge(T.sem.ls, sent)


def rank_program(g, core, T, topo):
    rank = T.rank_of(core)
    if "p" not in PLAN:
        PLAN["p"] = plan()
    if rank is None:
        for c in T.cores:
            rl, dst = relays(c, T, topo)
            if core in rl:
                relay_program(g, core, T, topo, rl.index(core), c, dst)
        return
    ops, order = PLAN["p"]
    rl, dst = relays(core, T, topo)
    rsrc, _d = relays(T.cores[(rank - STEP) % N], T, topo)
    queue = {"V": g.vector, "S": g.scalar, "T": g.tensor, "G": g, "Y": g.sync}
    count = {"sV": 0, "sS": 0, "sT": 0, "sG": 0}
    known = dict((e, {}) for e in queue)
    done = {}
    sent = 0
    for i in order:
        o = ops[i]
        e = o["e"]
        if e == "N":
            arg = ops[o["from"]]["arg"]
            done[i] = (arg[2], len(topo.engines(rsrc[RELAY[arg[3]]], core)), {})
            continue
        need = {}
        for p in o["p"]:
            if p in done and not (e == "T" and ops[p]["e"] == "T"):
                s, v, kn = done[p]
                if v > known[e].get(s, 0) and v > need.get(s, (0, 0))[0]:
                    need[s] = (v, kn)
        for s in sorted(need):
            v, kn = need[s]
            if v <= known[e].get(s, 0):
                continue
            queue[e].wait_ge(T.sem[s], v)
            known[e][s] = v
            for a in kn:
                known[e][a] = max(known[e].get(a, 0), kn[a])
        if o["arg"]:
            a, b, s, part = o["arg"]
            r = rl[RELAY[part]]
            rid, pid = topo.addr(r, core)
            g.remote_dma(ap(T, b), ap(T, a), T.sem[s], T.sem.ls, pid, rid, topo.mask(core, r))
            sent += len(topo.engines(core, r))
        elif o["sem"]:
            o["f"](g, T, lambda x, s=o["sem"]: x.then_inc(T.sem[s], 16))
            done[i] = (o["sem"], 16, dict(known[e]))
        else:
            def q(x, s="s" + e):
                x.then_inc(T.sem[s], 1)
                count[s] += 1
            o["f"](g, T, q)
            done[i] = ("s" + e, count["s" + e], dict(known[e]))
    for s in sorted(count):
        g.wait_ge(T.sem[s], count[s])
    for o in ops:
        if o["sem"]:
            g.wait_ge(T.sem[o["sem"]], 16)
    g.wait_ge(T.sem.ls, sent)
